import numpy as np, ml_dtypes
CORES = [6,15,38,47]
N = 4
BF = ml_dtypes.bfloat16
def gentries(a):
    return np.ascontiguousarray(a.reshape(8, 16, -1).transpose(0, 2, 1)).reshape(8, -1)
def gtable(e):
    e = np.asarray(e); return np.ascontiguousarray(e.reshape(8, -1, 16).transpose(0, 2, 1)).reshape(128, -1).astype(np.int32)
ND, NR, L, CAP, HB, LV, RO = 2048, 4096, 256, 64, 2, 4, 3
def parts(rng):
    cold = rng.random((N, 8, 1, NR)) < 0.4; cold[..., 5] = True
    regs = rng.integers(-15, 16, (N, 8, 16, NR)); warm = rng.random(regs.shape) < rng.random((N, 8, 1, NR))
    regs = np.where(cold | ~warm, -np.abs(regs), regs)
    acts = rng.integers(0, NR, (N, 8, 16, ND)); dead = rng.random((N, 8, 1, ND)) < 0.125
    order = np.argsort(~cold[:, :, 0], axis=-1, kind="stable"); cnt = np.add.reduce(cold[:, :, 0].astype(np.int64), axis=-1)
    pick = (rng.random(acts.shape) * cnt[:, :, None, None]).astype(np.int64).reshape(N, 8, -1)
    acts = np.where(dead, np.take_along_axis(order, pick, 2).reshape(acts.shape), acts)
    return acts, regs, rng.integers(0, 16, (N, 8, 16, ND)), rng.integers(0, ND, (N, 8, L)), rng.integers(1, 16, (N, 8, 16, L)), rng.integers(0, 64, (N, 8, RO, LV, L))
def pack(acts, regs, pay, n0, rch, dr):
    b = lambda a: np.ascontiguousarray(a.reshape(N, 128, -1)).astype(np.float32).astype(BF)
    return {"acts": np.ascontiguousarray(acts.reshape(N, 128, ND)).astype(np.int32), "regs": b(regs), "pay": b(pay), "n0": np.stack([gtable(a) for a in n0]), "rch": b(rch),
            "dr": np.ascontiguousarray(dr.reshape(N, 8, RO * LV * L)).astype(np.int32)}
def setup_inputs(rng):
    return pack(*parts(rng))
def setup_inputs_room(rng):
    acts, regs, pay, n0, rch, dr = parts(rng)
    regs[:, ::2] = -rng.integers(2 * RO, 16, (N, 4, 16, NR)); pay = pay * rng.integers(0, 2, pay.shape)
    for q in range(N):
        for g in range(0, 8, 2):
            for t in range(RO):
                p = int(rng.integers(0, 4))
                if q == 0: p = (g // 2 + (t if g else 0)) % 4
                c = np.zeros(N, np.int64)
                if p == 0: c[:] = CAP
                elif p == 1: c[::2] = CAP + 1; c[1::2] = CAP - 1
                elif p == 2: c[0] = L
                else: c[1] = 1; c[2] = CAP; c[3] = L - 1 - CAP
                to = rng.permutation(np.repeat(np.arange(N), np.roll(c, int(rng.integers(0, N)))))
                dr[q, g, t, HB - 1] = to + N * rng.integers(0, 64 // N, L)
    return pack(acts, regs, pay, n0, rch, dr)
def setup_inputs_ties(rng):
    acts, regs, pay, n0, rch, dr = parts(rng)
    for g in (0, 3, 6):
        regs[:, g] = 15; rch[:, g] = rng.integers(1, 16 - 2 * RO, (N, 16, L))
        dr[:, g] = rng.choice(np.concatenate([4 * np.arange(16), 4 * np.arange(1, 16) - 1, np.array([63])]), (N, RO, LV, L))
    for g in (1, 4):
        i = rng.integers(0, 16, (N, 1, NR)); one = (np.arange(16)[None, :, None] == i) & (rng.random((N, 1, NR)) < 0.25)
        regs[:, g] = np.where(one, 1, -rng.integers(0, 16, (N, 16, NR)))
        dr[:, g] = 8 * rng.integers(0, 8, (N, RO, LV, L))
    for g in (2, 5, 7):
        dr[:, g] = rng.choice(np.array([0, 1, 31, 32, 62, 63]), (N, RO, LV, L))
    return pack(acts, regs, pay, n0, rch, dr)
def setup_inputs_alike(rng):
    acts, regs, pay, n0, rch, dr = parts(rng)
    n0[:, ::2] = rng.choice(np.array([0, ND - 1, ND // 2, 3]), (N, 4, L))
    acts[:, 1] = rng.choice(np.array([0, NR - 1, 7, NR // 2]), (N, 16, ND))
    acts[:, 5] = rng.integers(NR - 64, NR, (N, 16, ND)); acts[:, 7] = rng.integers(0, 100, (N, 16, ND))
    acts[:, 2] = acts[:, 2, :1]
    dr[:, 4:] = dr[:, 4:, :, :, :1]
    return pack(acts, regs, pay, n0, rch, dr)
def setup_inputs_clip(rng):
    acts, regs, pay, n0, rch, dr = parts(rng)
    regs = rng.choice(np.array([-15, -14, -1, 0, 1, 14, 15]), (N, 8, 16, NR)); pay = 15 * rng.integers(0, 2, pay.shape)
    rch = np.where(rng.random(rch.shape) < 0.7, 15, rng.integers(1, 3, rch.shape))
    a, b = rng.permutation(8)[:2]
    regs[:, a] = 15; rch[:, a] = 15; regs[:, b] = -15
    return pack(acts, regs, pay, n0, rch, dr)
def setup_inputs_spread(rng):
    acts, regs, pay, n0, rch, dr = parts(rng)
    u = lambda shape: np.minimum((np.exp2(4 * rng.random((N, 8, 1, shape[-1]))) * rng.random(shape)).astype(np.int64), 15)
    regs = u(regs.shape) * np.where(rng.random(regs.shape) < rng.random((N, 8, 1, NR)), 1, -1)
    pay = u(pay.shape); rch = np.maximum(u(rch.shape), 1)
    dr = np.minimum((64 * rng.random(dr.shape) ** np.exp2(4 * rng.random((N, 8, 1, 1, L)) - 2)).astype(np.int64), 63)
    return pack(acts, regs, pay, n0, rch, dr)
def check_inputs(d):
    bad = []
    for k, lo, hi in (("acts", 0, NR - 1), ("regs", -15, 15), ("pay", 0, 15), ("n0", 0, ND - 1), ("rch", 1, 15), ("dr", 0, 63)):
        a = np.asarray(d[k]).astype(np.float64)
        if not (np.min(a) >= lo and np.max(a) <= hi): bad.append("range of " + k)
        elif not np.all(a == np.rint(a)): bad.append("whole numbers in " + k)
    return bad
def level(rg, ac, n, x, v, e):
    S = n.shape[1]
    a = np.take_along_axis(ac, n[:, None, :], 2)
    p = np.maximum(np.take_along_axis(rg, a.reshape(8, 1, 16 * S), 2), 0).reshape(8, 16, 16, S)
    c = np.add.accumulate(np.add.reduce(np.minimum(x[:, :, None, :], p), axis=1), axis=1)
    tot = c[:, 15]
    k = np.where(tot > 0, np.argmax(64 * c > (v * tot)[:, None, :], axis=1), v & 15)
    rec = np.take_along_axis(a, k[:, None, :], 1)[:, 0]
    x = np.minimum(x, np.take_along_axis(p, k[:, None, None, :], 2)[:, :, 0] + 1)
    return k, rec, x, (5 * rec + 13 * n + e) & (ND - 1)
def rewrite(rg, rec, live, w):
    for g in range(8):
        s = np.nonzero(live[g])[0]
        u, j = np.unique(rec[g, s], return_index=True)
        rg[g][:, u] = np.clip(rg[g][:, u] + w[g][:, s[j]], -15, 15)
def reference(acts, regs, pay, n0, rch, dr):
    ac = acts.astype(np.int64).reshape(N, 8, 16, ND); rg = regs.astype(np.float32).astype(np.int64).reshape(N, 8, 16, NR)
    py = pay.astype(np.float32).astype(np.int64).reshape(N, 8, 16, ND); x0 = rch.astype(np.float32).astype(np.int64).reshape(N, 8, 16, L)
    st = np.stack([gentries(a) for a in n0]).astype(np.int64); v = dr.astype(np.int64).reshape(N, 8, RO, LV, L)
    for t in range(RO):
        fn = np.zeros((N, 8, N * CAP), np.int64); fx = np.ones((N, 8, 16, N * CAP), np.int64); fv = np.zeros((N, 8, LV, N * CAP), np.int64); live = np.zeros((N, 8, N * CAP), bool)
        home = []
        for r in range(N):
            n, x, vt = st[r], x0[r], v[r, :, t]
            for e in range(1, HB + 1): k, rec, x, n = level(rg[r], ac[r], n, x, vt[:, e - 1], e)
            to = k & (N - 1); oh = (to[:, None, :] == np.arange(N)[None, :, None]).astype(np.int64)
            place = np.take_along_axis(np.add.accumulate(oh, axis=2), to[:, None, :], 1)[:, 0] - 1
            g, l = np.nonzero(place < CAP); d = to[g, l]; s = r * CAP + place[g, l]
            fn[d, g, s] = n[g, l]; fx[d, g, :, s] = x[g, :, l]; fv[d, g, :, s] = vt[g, :, l]; live[d, g, s] = True
            home.append((rec, g, l, d, s))
        recs, sg = [], []
        for q in range(N):
            n, x = fn[q], fx[q]
            for e in range(HB + 1, LV + 1): k, rec, x, n = level(rg[q], ac[q], n, x, fv[q, :, e - 1], e)
            val = np.minimum(np.take_along_axis(py[q], n[:, None, :], 2), x)
            recs.append(rec); sg.append(np.sign(16 * val - np.add.reduce(val, axis=1, keepdims=True)))
        for q in range(N): rewrite(rg[q], recs[q], live[q], sg[q])
        sg = np.stack(sg)
        for r in range(N):
            rec, g, l, d, s = home[r]
            w = np.zeros((8, 16, L), np.int64); went = np.zeros((8, L), bool)
            w[g, :, l] = -sg[d, g, :, s]; went[g, l] = True
            rewrite(rg[r], rec, went, w)
    return {"yr": rg.reshape(N, 128, NR).astype(np.float32).astype(BF)}

@@ -1,0 +1,655 @@
+from concourse.bass import DstId, RemoteDMATransfer
+from concourse.mybir import dt, AluOpType, AxisListType, ActivationFunctionType
+
+N = 4
+RO = 3
+REG = 320
+EPS = 2.0 ** -30
+BETA = 2.0 ** -12
+HU = (128, 128)
+FU = ((0,), (1, 2), (3,))
+CG, CW, CS = 64, 64, 64
+
+F, B, H, I, U = "float32", "bfloat16", "float16", "int32", "uint16"
+
+
+def _scratch():
+    s, at = {}, {}
+    def sb(name, cols, d):
+        if cols > 1024 or name in ("rch_s", "n0_i", "dr_i") or name[:4] == "land":
+            s[name] = ("sbuf", [128, cols], d)
+        else:
+            big = "p" + d
+            lo = s[big][1][1] if big in s else 0
+            s[big] = ("sbuf", [128, lo + cols + -cols % 32], d)
+            at[name] = (big, lo, cols)
+    sb("acts_i", 2048, I); sb("regs_s", 4128, B); sb("P", 4096, B); sb("pay_s", 2048, B); sb("paym", 2048, B)
+    sb("rch_s", 256, B); sb("n0_i", 16, I); sb("dr_i", 256, I); sb("w_i", 256, I)
+    sb("drb", 256, B); sb("wb", 256, B)
+    sb("xr1", 4096, B); sb("xr", 4096, B); sb("W", 4096, B)
+    for e in (1, 2, 3, 4):
+        sb("A%d" % e, 256, U); sb("Ah%d" % e, 256, H); sb("q%d" % e, 256, H); sb("rec%d" % e, 16, U); sb("pre%d" % e, 16, F)
+    for e in (1, 2, 3, 4, 5):
+        sb("nU%d" % e, 16, U)
+    for n in ("y1", "y2", "y3", "yF3", "yF4", "yF5", "lv", "zF", "NV", "zl", "HV", "ms", "ind", "auxB", "auxF", "ng"):
+        sb(n, 256, B)
+    sb("t1", 256, F); sb("s_i", 16, I); sb("n_i", 16, I); sb("nlf", 64, B); sb("nx", 1024, B)
+    for t in range(RO):
+        sb("vb%d" % t, 512, F); sb("wt%d" % t, 512, B); sb("auxS%d" % t, 256, B); sb("land%d" % t, 512, B); sb("zr%d" % t, 1280, B)
+    sb("vbF", 512, F); sb("wtF", 512, B)
+    sb("cum", 256, F); sb("Q", 256, H); sb("slot", 16, U); sb("send", 1280, B)
+    for n in ("h", "f"):
+        sb("rf8" + n, 16, F); sb("Y" + n, 256, F); sb("eq" + n, 256, B); sb("lc" + n, 256, B); sb("u" + n, 16, F)
+        sb("off" + n, 16, U); sb("Z2" + n, 256, F); sb("er" + n, 256, B); sb("ld" + n, 256, B)
+    for u in range(4):
+        sb("mk%d" % u, 128, H); sb("mq%d" % u, 128, H)
+    sb("Dm", 128, I); sb("Bm", 128, I); sb("pi", 2, I); sb("pk", 2, I); sb("rp", 256, I); sb("li", 256, I)
+    sb("crep", 256, U); sb("crep1", 16, U); sb("KH", 256, B); sb("KF", 256, B); sb("kf", 1, F); sb("pg", 1, F)
+    sb("BO", 128, B); sb("BO16", 128, H); sb("BO5", 128, H); sb("BOn", 128, B)
+    sb("ID", 128, B); sb("E1", 128, B); sb("E2", 128, B); sb("E3", 128, B); sb("OHM", 128, B); sb("DST", 128, B)
+    sb("TRI", 128, B); sb("Z", 144, B); sb("ZM", 128, B)
+    sb("cols", 16, F); sb("SR", 640, B); sb("SEL", 768, B); sb("ZT", 864, B)
+    sb("rd", 256, F); sb("ta", 256, F); sb("tb", 256, F); sb("CMh", 256, B); sb("CMf", 256, B); sb("MX", 256, B)
+    sb("RST", 256, B); sb("ONE", 256, B); sb("SIX", 256, B)
+    for b in range(8):
+        s["b%d" % b] = ("psum", [128, 512], F)
+    return s, at
+
+
+SCRATCH, AT = _scratch()
+SEMAPHORES = (["eV", "eP", "eS", "eG"] + ["ld%d" % i for i in range(8)] + ["yo"]
+              + ["%s%d_%d" % (k, t, r) for k in ("a", "z", "la", "lz") for t in range(RO) for r in range(N)])
+
+
+def rank_program(g, core, T, topo):
+    me = T.rank_of(core)
+    if me is None:
+        return
+    OP, ACT = AluOpType, ActivationFunctionType
+    queue = {"V": g.vector, "P": g.tensor, "S": g.scalar, "G": g, "Y": g.sync}
+    count = {"eV": 0, "eP": 0, "eS": 0, "eG": 0}
+    known = {e: {} for e in queue}
+    free = {e: 0.0 for e in queue}
+    snap, acc, when = {}, {}, {}
+    CY, WAKE, GA, SC = 0.83, 140.0, 1.5, 3.0
+    LAND = {"ld2": 8000.0, "ld4": 9000.0, "ld5": 10000.0, "ld6": 13000.0}
+
+    def a(name, lo=None, hi=None, step=1, rows=128):
+        name, base, cols = AT.get(name, (name, 0, 0))
+        t = T[name]
+        if lo is None:
+            lo, hi = 0, cols or SCRATCH[name][1][1]
+        lo, hi = base + lo, base + hi
+        ap = t[0:rows, lo:hi] if step == 1 else t[0:rows, lo:hi:step]
+        return ap, [(name, lo, hi)], (hi - lo + step - 1) // step, 0
+
+    def via(win, off):
+        return win[0].indirect(off[0]), win[1] + off[1], 16 * off[2], 1
+
+    def narrow(x):
+        return SCRATCH[x[1][0][0]][2] in (B, U, H)
+
+    def merge(eng, tok):
+        k = known[eng]
+        for s, v in list(snap.get(tok, {}).items()) + [tok]:
+            if k.get(s, 0) < v:
+                k[s] = v
+
+    def needs(eng, reads, writes):
+        need = {}
+        for regs, w in ((reads, False), (writes, True)):
+            for name, lo, hi in regs:
+                bank = SCRATCH[name][0] == "psum"
+                for (e2, tok, l2, h2, w2) in acc.get(name, []):
+                    if bank and e2 != eng:
+                        hit = True
+                    elif l2 < hi and lo < h2:
+                        if w and w2:
+                            hit = not (eng == "P" and e2 == "P")
+                        elif w:
+                            hit = e2 != eng
+                        else:
+                            hit = w2
+                    else:
+                        hit = False
+                    if hit and known[eng].get(tok[0], 0) < tok[1] and need.get(tok[0], 0) < tok[1]:
+                        need[tok[0]] = tok[1]
+        return need
+
+    def order(eng, reads, writes):
+        need = needs(eng, reads, writes)
+        for s in sorted(need):
+            v = need[s]
+            if any(s2 != s and snap.get((s2, need[s2]), {}).get(s, 0) >= v for s2 in need):
+                need[s] = 0
+        for s in sorted(need):
+            if need[s]:
+                queue[eng].wait_ge(T.sem[s], need[s])
+                merge(eng, (s, need[s]))
+
+    def record(eng, tok, reads, writes):
+        for regs, w in ((reads, False), (writes, True)):
+            for name, lo, hi in regs:
+                old = acc.get(name, [])
+                keep = [x for x in old if not (lo <= x[2] and x[3] <= hi and (w or (x[0] == eng and not x[4])))]
+                keep.append((eng, tok, lo, hi, w))
+                acc[name] = keep
+
+    def start(op):
+        if isinstance(op, list):
+            return max(start(o) for o in op)
+        eng, call, reads, writes, dur = op[:5]
+        t = free[eng]
+        for s, v in needs(eng, reads, writes).items():
+            t = max(t, when.get((s, v), 0.0) + WAKE)
+        return t
+
+    def done(tok, eng, t):
+        sn = dict(known[eng]); sn[tok[0]] = tok[1]
+        snap[tok] = sn
+        when[tok] = t
+
+    def do(op):
+        if isinstance(op, list):
+            for o in op:
+                do(o)
+            return
+        eng, call, reads, writes, dur = op[:5]
+        t = start(op)
+        order(eng, reads, writes)
+        free[eng] = t + dur
+        if len(op) > 5:
+            call()
+            done(op[5], eng, t + 3000.0)
+            record("R" + op[5][0], op[5], reads, [])
+            return
+        s = "e" + eng
+        count[s] += 1
+        call().then_inc(T.sem[s], 1)
+        done((s, count[s]), eng, t + dur)
+        record(eng, (s, count[s]), reads, writes)
+
+    pool = []
+
+    def spawn(p, j):
+        pool.append([p, j, None])
+
+    def together(jobs):
+        live = pool
+        for p, j in jobs:
+            spawn(p, j)
+        while live:
+            best = None
+            for x in list(live):
+                while not isinstance(x[2], (tuple, list)) and x[2] != "end":
+                    if x[2] is None:
+                        x[2] = next(x[1], "end")
+                    elif x[2]():
+                        x[2] = None
+                    else:
+                        break
+                if x[2] == "end":
+                    live.remove(x)
+                elif isinstance(x[2], (tuple, list)):
+                    k = (start(x[2]), x[0])
+                    if best is None or k < best[0]:
+                        best = (k, x)
+            if best:
+                do(best[1][2])
+                best[1][2] = None
+
+    def regs_of(*xs):
+        return [r for x in xs if isinstance(x, tuple) for r in x[1]]
+
+    def val(x):
+        return x[0] if isinstance(x, tuple) else x
+
+    def vop(call, out, ins, n, wide=1.0):
+        x = [i for i in ins if i[3]]
+        d = x[0][2] * GA * CY if x else out[2] * SC * CY if out[3] else max(64.0, n * wide) * CY
+        return ("V", call, regs_of(*ins), out[1], 60.0 + d)
+
+    def ts(out, in0, s1, op0, s2=None, op1=None):
+        if op1 is None:
+            f = lambda: g.vector.tensor_scalar(out[0], in0[0], val(s1), None, op0)
+        else:
+            f = lambda: g.vector.tensor_scalar(out[0], in0[0], val(s1), val(s2), op0, op1)
+        return vop(f, out, [in0] + [x for x in (s1, s2) if isinstance(x, tuple)], in0[2], 0.5 if narrow(out) and narrow(in0) else 1.0)
+
+    def tt(out, in0, in1, op):
+        ps = any(SCRATCH[x[1][0][0]][0] == "psum" for x in (in0, in1))
+        return vop(lambda: g.vector.tensor_tensor(out[0], in0[0], in1[0], op), out, [in0, in1], in1[2], 1.0 if ps else 2.0)
+
+    def cp(out, in_):
+        return vop(lambda: g.vector.tensor_copy(out[0], in_[0]), out, [in_], in_[2])
+
+    def scatter(win, off, in_):
+        return vop(lambda: g.vector.tensor_copy(win[0].indirect(off[0]), in_[0]), (None, win[1], in_[2], 1), [in_, off], in_[2])
+
+    def fill(out, c):
+        return vop(lambda: g.vector.memset(out[0], c), out, [], out[2], 0.5)
+
+    def scan(out, d0, d1, init):
+        return vop(lambda: g.vector.tensor_tensor_scan(out[0], d0[0], d1[0], val(init), OP.mult, OP.add), out,
+                   [d0, d1] + [x for x in (init,) if isinstance(x, tuple)], d1[2], 0.5 if narrow(out) and narrow(d1) else 1.0)
+
+    def act(out, in_, func, bias=0.0, scale=1.0):
+        if func == ACT.Copy:
+            f = lambda: g.scalar.activation(out[0], in_[0], func, scale=scale)
+        else:
+            f = lambda: g.scalar.activation(out[0], in_[0], func, bias=val(bias), scale=scale)
+        return ("S", f, regs_of(in_, bias), out[1], 65.0 + in_[2] * GA * CY if in_[3] else 165.0 + in_[2] * CY)
+
+    def mm(out, lhsT, rhs, start=True, stop=True):
+        return ("P", lambda: g.tensor.matmul(out[0], lhsT[0], rhs[0], start, stop), regs_of(lhsT, rhs), out[1], 10.0 + max(64, rhs[2]) * CY)
+
+    def iota(out, pattern, base, ch):
+        return ("G", lambda: g.iota(out[0], pattern, base, ch), [], out[1], 130.0 + 2 * out[2] * CY)
+
+    def zeros(out):
+        return ("G", lambda: g.iota(out[0], [[0, out[2]]], 0, 0, allow_small_or_imprecise_dtypes=True), [], out[1], 130.0 + 2 * out[2] * CY)
+
+    def sel(out, in_, pattern, base, ch):
+        return ("G", lambda: g.affine_select(out[0], in_[0], pattern, OP.is_equal, 0.0, base, ch), regs_of(in_), out[1], 170.0 + 2 * out[2] * CY)
+
+    def load(eng, sem, out, src, reg):
+        order(eng, [], reg)
+        queue[eng].dma_start(out, src).then_inc(T.sem[sem], 16)
+        done((sem, 16), eng, LAND.get(sem, 3000.0))
+        record("D" + sem, (sem, 16), [], reg)
+
+    def send(r, src, dst, sem, lsem):
+        rid, pid, _ = topo.addr(T.cores[r])
+        m = sum(1 << x for x in topo.engines(core, T.cores[r])[:8])
+        return ("G", lambda: g.remote_dma(dst, src[0], T.sem[sem], T.sem[lsem], pid, rid, m), regs_of(src), [], 300.0, (lsem, 8))
+
+    def arrives(sem, regions, t):
+        snap[(sem, 8)] = {sem: 8}
+        when[(sem, 8)] = t
+        record("R" + sem, (sem, 8), [], regions)
+
+    def far_key(r):
+        c1, c2 = topo.chip(core), topo.chip(T.cores[r])
+        return 0 if topo.mates(c1, c2) else 1 if topo.same_plane(c1, c2) else 2
+    others = sorted([r for r in range(N) if r != me], key=far_key)
+    place = [me] + others
+    def units(sizes):
+        out, lo = [], 0
+        for n in sizes:
+            out.append((lo, lo + n))
+            lo += n
+        return out
+    HUN = units(HU)
+    FUN = units([64 * len(p) for p in FU])
+
+    load("Y", "ld0", T.n0_i[:], T.n0[:], [("n0_i", 0, 16)])
+    load("S", "ld1", T.rch_s[:], T.rch[:], [("rch_s", 0, 256)])
+    load("Y", "ld2", T.acts_i[:], T.acts[:], [("acts_i", 0, 2048)])
+    load("S", "ld3", T.dr_i[0:96, :], T.dr[:, :], [("dr_i", 0, 256)])
+    load("S", "ld4", T.regs_s[:, 0:2048], T.regs[:, 0:2048], [("regs_s", 0, 2048)])
+    load("Y", "ld5", T.regs_s[:, 2048:4096], T.regs[:, 2048:4096], [("regs_s", 2048, 4096)])
+    load("Y", "ld6", T.pay_s[:], T.pay[:], [("pay_s", 0, 2048)])
+
+    kf = a("kf")
+    def col(j):
+        return a("cols", j, j + 1)
+    home_te = [4 * t + e for t in range(RO) for e in (0, 1)]
+    far_te = [4 * t + e for t in range(RO) for e in (2, 3)]
+    marks = {}
+
+    def mark(k):
+        return lambda: k in marks
+
+    def constants():
+        yield iota(a("li"), [[1, 256]], 0, 0)
+        yield iota(a("pi"), [[0, 2]], 0, 1)
+        yield iota(a("Bm"), [[1, 8], [0, 16]], 0, 0)
+        yield iota(a("rp"), [[0, 16], [1, 16]], 0, 0)
+        yield iota(a("Dm"), [[1, 128]], 0, -1)
+        yield fill(a("ONE"), 1.0)
+        yield cp(a("crep"), a("li"))
+        yield cp(a("nU1"), a("n0_i"))
+        yield ts(a("pk", 0, 1), a("pi", 0, 1), 15, OP.bitwise_and)
+        yield ts(a("pk", 1, 2), a("pi", 1, 2), 4, OP.arith_shift_right)
+        yield cp(a("kf"), a("pk", 0, 1))
+        yield cp(a("pg"), a("pk", 1, 2))
+        yield fill(col(3), BETA)
+        yield fill(col(14), 1.0)
+        yield fill(col(15), -1.0)
+        yield ts(a("BO"), a("Bm"), a("pg"), OP.is_equal)
+        yield fill(a("Z"), 0.0)
+        yield cp(a("Z", 15, 143, 16), a("BO", 0, 128, 16))
+        for u in range(4):
+            yield act(a("xr1", 1024 * u, 1024 * u + 1024), via(a("rch_s", 64 * u, 64 * u + 64), a("crep", 0, 64)), ACT.Copy)
+        yield ts(a("BO16"), a("BO"), 1.0, OP.mult)
+        yield ts(a("BO5"), a("BO"), 5.0, OP.mult)
+        yield ts(a("rd"), a("rp"), kf, OP.subtract)
+        yield ts(a("MX"), a("rd"), 0.0, OP.is_equal)
+        yield ts(a("TRI"), a("Dm"), 0, OP.is_ge, 64.0, OP.mult)
+        yield tt(a("TRI"), a("TRI"), a("BO"), OP.mult)
+        yield fill(a("TRI", 15, 128, 16), 0.0)
+        yield ts(col(0), kf, 15.0, OP.is_lt)
+        yield fill(a("SIX"), 0.0625)
+        yield mark("o")
+        yield tt(a("E1"), a("E1"), a("E3"), OP.add)
+        yield ts(a("E2"), a("ID"), col(0), OP.mult)
+        yield tt(a("OHM"), a("E1"), a("E2"), OP.subtract)
+        yield ts(col(1), kf, -EPS, OP.mult)
+        yield ts(col(2), kf, 15.0, OP.is_equal, 16 * EPS, OP.mult)
+        yield tt(col(1), col(1), col(2), OP.add)
+        yield cp(a("drb", rows=96), a("dr_i", rows=96))
+        yield ts(a("w_i", rows=96), a("dr_i", rows=96), 15, OP.bitwise_and)
+        yield cp(a("wb", rows=96), a("w_i", rows=96))
+        yield ts(a("y1"), a("rch_s"), -1.0, OP.add)
+        yield ts(a("pre1"), a("n0_i"), 13.0, OP.mult, 1.0 + 10240.0, OP.add)
+        for x in draws(0):
+            yield x
+        yield tt(a("DST", 0, 116), a("OHM", 0, 116), a("OHM", 4, 120), OP.add)
+        yield tt(a("E1", 0, 116), a("OHM", 8, 124), a("OHM", 12, 128), OP.add)
+        yield ts(a("E2"), a("rp", 0, 128), 4, OP.is_lt)
+        yield tt(a("DST", 0, 116), a("DST", 0, 116), a("E1", 0, 116), OP.add)
+        yield tt(a("DST", 0, 116), a("DST", 0, 116), a("E2", 0, 116), OP.mult)
+        yield ts(col(4), kf, 320.0, OP.mult, -1.0, OP.add)
+        yield ts(col(5), kf, 320.0, OP.mult, 64.0, OP.add)
+        yield ts(col(6), kf, 4096.0, OP.add)
+        yield mark("z")
+        for x in aux_static(0):
+            yield x
+        marks["c"] = 1
+        yield ts(col(7), kf, 2.0, OP.is_equal)
+        yield ts(col(8), kf, 3.0, OP.is_equal)
+        yield tt(col(7), col(7), col(8), OP.add)
+        yield ts(a("BOn"), a("BO"), col(7), OP.mult)
+        for j, (row, w) in enumerate(((0, 1.0), (1, 1.0), (5, 1.0), (6, 1.0), (4, -8192.0))):
+            yield ts(col(9 + j), kf, float(row), OP.is_equal, w, OP.mult)
+            yield ts(a("SR", 128 * j, 128 * j + 128), a("BO"), col(9 + j), OP.mult)
+        yield ts(a("ZM"), a("ID"), 16.0, OP.mult)
+        yield tt(a("ZM"), a("ZM"), a("BO"), OP.subtract)
+        yield ts(a("ta"), a("rd"), 0.0, OP.is_gt, 16384.0, OP.mult)
+        yield ts(a("tb"), a("rd"), 0.0, OP.is_equal, -8192.0, OP.mult)
+        yield tt(a("ta"), a("ta"), a("tb"), OP.add)
+        yield ts(a("CMh"), a("ta"), 2048.0, OP.add)
+        yield ts(a("CMf"), a("ta"), 10240.0, OP.add)
+        yield ts(a("RST"), a("rp"), 0, OP.is_gt)
+        yield ts(a("crep1"), a("li", 0, 16), 1.0, OP.add)
+        yield ts(col(8), kf, 4112.0, OP.add)
+        yield fill(a("KH"), 2048.0)
+        yield fill(a("KF"), 10240.0)
+        yield act(a("paym"), a("pay_s"), ACT.Identity, bias=col(15))
+        marks["e"] = 1
+
+    def patterns():
+        for j in (0, 1):
+            yield sel(a("SEL", 128 * j, 128 * j + 128, rows=96), a("ONE", 0, 128, rows=96), [[-12, 8], [0, 16]], -home_te[j], 1)
+        yield sel(a("ID"), a("ONE", 0, 128), [[-1, 128]], 0, 1)
+        yield sel(a("E1"), a("BO"), [[1, 128]], -1, -1)
+        yield sel(a("E3"), a("BO"), [[1, 128]], 15, -1)
+        yield zeros(a("DST"))
+        marks["o"] = 1
+        yield zeros(a("ZT"))
+        for j in range(6):
+            yield sel(a("ZT", 144 * j + 15, 144 * j + 143, 16, rows=96), a("ONE", 0, 8, rows=96), [[-12, 8]], -far_te[j], 1)
+        marks["z"] = 1
+        yield zeros(a("send"))
+        for t in range(RO):
+            yield zeros(a("zr%d" % t))
+        for j in range(2, 6):
+            yield sel(a("SEL", 128 * j, 128 * j + 128, rows=96), a("ONE", 0, 128, rows=96), [[-12, 8], [0, 16]], -home_te[j], 1)
+
+    def draws(t):
+        for src, b in (("drb", "b6"), ("wb", "b7")):
+            for j in (0, 1):
+                s = 128 * (2 * t + j)
+                yield mm(a(b, 256 * j, 256 * j + 256), a("SEL", s, s + 128, rows=96), a(src, rows=96))
+            if src == "drb":
+                yield act(a("vb%d" % t), a(b), ACT.Identity, bias=col(3))
+            else:
+                yield act(a("wt%d" % t), a(b), ACT.Relu, bias=col(1), scale=EPS)
+        marks["v%d" % t] = 1
+
+    def aux_static(t):
+        grp = []
+        for k, (src, j, row) in enumerate((("drb", 0, 0), ("drb", 1, 1), ("wb", 0, 5), ("wb", 1, 6))):
+            s = 144 * (2 * t + j) + 15 - row
+            grp.append(mm(a("b7", 0, 256), a("ZT", s, s + 128, rows=96), a(src, rows=96), k == 0, False))
+        yield grp + [mm(a("b7", 0, 256), a("Z", 11, 139), a("SIX"), False, True)]
+        yield act(a("auxS%d" % t), a("b7", 0, 256), ACT.Copy)
+        marks["x%d" % t] = 1
+
+    def relu_records():
+        yield ts(a("P", 0, 2736), a("regs_s", 0, 2736), 0.0, OP.max)
+        yield act(a("P", 2736, 4096), a("regs_s", 2736, 4096), ACT.Relu)
+        marks["P"] = 1
+
+    def acts_at(e, lo, hi):
+        return cp(a("A%d" % e, lo, hi), via(a("acts_i"), a("nU%d" % e, lo // 16, hi // 16)))
+
+    def acts_half(e, lo, hi):
+        return ts(a("Ah%d" % e, lo, hi), a("A%d" % e, lo, hi), -2048.0, OP.add)
+
+    YN = {1: "y1", 2: "y2", 3: "yF3", 4: "yF4"}
+    YO = {1: "y2", 2: "y3", 3: "yF4", 4: "yF5"}
+
+    def spread(e, lo, hi):
+        for l in range(lo, hi, CS):
+            n = min(CS, hi - l)
+            yield act(a("xr", 16 * l, 16 * l + 16 * n), via(a(YN[e], l, l + n), a("crep", 0, n)), ACT.Identity, bias=col(14))
+
+    def diag(b1, c1, src, ones, mk, b2, c2, last, n, lo, hi):
+        yield mm(a(b1, c1, c1 + 128, rows=n), a(src, lo, hi), a(ones))
+        yield tt(a(mk, rows=n), a(b1, c1, c1 + 128, rows=n), a("MX", 0, 128, rows=n), OP.mult)
+        yield mm(a(b2, c2, c2 + n // 16), a(mk, rows=n), a(last, 0, n, 16, rows=n))
+
+    def level(e, t, u, lo, hi):
+        n = hi - lo
+        bank = "b%d" % u
+        tl, th = lo // 16, hi // 16
+        x = "xr1" if e == 1 else "xr"
+        vb, wt = ("vb%d" % t, "wt%d" % t) if e < 3 else ("vbF", "wtF")
+        at = 256 * ((e - 1) % 2)
+        for l in range(lo, hi, CW):
+            m = min(CW, hi - l)
+            for j in range(l, l + m, CG):
+                c = min(CG, l + m - j)
+                yield tt(a("W", 16 * j, 16 * j + 16 * c), via(a("P"), a("A%d" % e, j, j + c)), a(x, 16 * j, 16 * j + 16 * c), OP.min)
+            if e == 1:
+                yield mark("v%d" % t)
+            for k in range(16):
+                yield mm(a(bank, l - lo, l - lo + m), a("Z", 15 - k, 143 - k), a("W", 16 * l + k, 16 * l + 16 * m, 16), k == 0, k == 15)
+        yield act(a("ms", lo, hi), a(bank, 0, n), ACT.Copy)
+        yield mm(a(bank, n, 2 * n), a("ID"), a(wt, at + lo, at + hi), True, False)
+        yield mm(a(bank, n, 2 * n), a("BO"), a("ms", lo, hi), False, True)
+        yield mm(a(bank, 2 * n, 3 * n), a("TRI"), a("ms", lo, hi))
+        yield tt(a("t1", lo, hi), a(bank, n, 2 * n), a(vb, at + lo, at + hi), OP.mult)
+        yield tt(a("ind", lo, hi), a(bank, 2 * n, 3 * n), a("t1", lo, hi), OP.is_lt)
+        yield mm(a(bank, 3 * n, 4 * n), a("OHM"), a("ind", lo, hi))
+
+        def slots():
+            yield mm(a("b4", lo, hi), a("DST"), a("ind", lo, hi))
+            yield lambda: lo == 0 or "s%d_%d" % (t, lo) in marks
+            yield scan(a("cum", lo, hi), a("ONE", lo, hi), a("b4", lo, hi), col(4) if lo == 0 else a("cum", lo - 1, lo))
+            marks["s%d_%d" % (t, hi)] = 1
+            yield tt(a("Q", lo, hi), a("b4", lo, hi), a("cum", lo, hi), OP.mult)
+            for o in diag("b5", 128 * u, "Q", "BO16", "mq%d" % u, "b4", 256 + tl, "BO16", n, lo, hi):
+                yield o
+            yield cp(a("slot", tl, th), a("b4", 256 + tl, 256 + th))
+            marks["S%d_%d" % (t, u)] = 1
+        if e == 2:
+            yield mark("c")
+            spawn(u + 0.2, slots())
+        if e in (2, 4):
+            yield mark("R%d_%d_%d" % (t, e, u))
+        yield tt(a("q%d" % e, lo, hi), a(bank, 3 * n, 4 * n), a("Ah%d" % e, lo, hi), OP.mult)
+        for o in diag(bank, 0, "q%d" % e, "BO16", "mk%d" % u, bank, n, "BO5", n, lo, hi):
+            yield o
+        p = a(bank, n, n + n // 16)
+        yield ts(a("rec%d" % e, tl, th), p, 0.2, OP.mult, 2048.25, OP.add)
+
+        def reaches():
+            yield tt(a(YO[e], lo, hi), via(a("P"), a("rec%d" % e, tl, th)), a(YN[e], lo, hi), OP.min)
+            if e in (1, 3):
+                for o in spread(e + 1, lo, hi):
+                    yield o
+            marks["Y%d_%d_%d" % (t, e, u)] = 1
+        spawn(u - 0.5, reaches())
+        yield tt(a("s_i", tl, th), p, a("pre%d" % e, tl, th), OP.add)
+        yield ts(a("n_i", tl, th), a("s_i", tl, th), 2047, OP.bitwise_and)
+        if e != 2:
+            yield cp(a("nU%d" % (e + 1), tl, th), a("n_i", tl, th))
+        if e in (1, 3):
+            yield acts_at(e + 1, lo, hi)
+
+            def rest():
+                yield ts(a("pre%d" % (e + 1), tl, th), a("n_i", tl, th), 13.0, OP.mult, e + 1.0 + 10240.0, OP.add)
+                yield acts_half(e + 1, lo, hi)
+                marks["R%d_%d_%d" % (t, e + 1, u)] = 1
+            spawn(u + 5, rest())
+        yield mark("Y%d_%d_%d" % (t, e, u))
+
+    def home(t, u, lo, hi):
+        tl, th = lo // 16, hi // 16
+        if t == 0:
+            yield acts_at(1, lo, hi)
+            yield acts_half(1, lo, hi)
+        yield mark("P")
+        for e in (1, 2):
+            for o in level(e, t, u, lo, hi):
+                yield o
+        n = hi - lo
+        w = n // 16
+        f0, x0 = 16 * u, 256 * u
+        yield cp(a("nlf", f0, f0 + w), a("n_i", tl, th))
+        yield tt(a("nlf", f0 + w, f0 + 2 * w), a("n_i", tl, th), a("nlf", f0, f0 + w), OP.subtract)
+        yield tt(a("nx", x0, x0 + 2 * n), via(a("nlf", f0, f0 + 2 * w), a("crep", 0, 2 * w)), a("MX", 0, 2 * n), OP.mult)
+        yield mark("x%d" % t)
+        yield [mm(a("b6", lo, hi), a("ID"), a("auxS%d" % t, lo, hi), True, False),
+               mm(a("b6", lo, hi), a("Z", 13, 141), a("nx", x0, x0 + n), False, False),
+               mm(a("b6", lo, hi), a("Z", 12, 140), a("nx", x0 + n, x0 + 2 * n), False, True)]
+        yield act(a("auxB", lo, hi), a("b6", lo, hi), ACT.Copy)
+        yield mark("S%d_%d" % (t, u))
+        yield scatter(a("send", 0, 1216), a("slot", tl, th), a("y3", lo, hi))
+        marks["y%d_%d" % (t, lo)] = 1
+        yield lambda: all("y%d_%d" % (t, l) in marks for l, h in HUN)
+        yield scatter(a("send", 64, 1280), a("slot", tl, th), a("auxB", lo, hi))
+
+    def depart(t):
+        order("G", [("zr%d" % t, 0, 1280)], [])
+        for r in others:
+            do(send(r, a("send", REG * r, REG * r + 128), T["land%d" % t][:, 128 * me:128 * me + 128], "a%d_%d" % (t, me), "la%d_%d" % (t, r)))
+        for i, r in enumerate(others):
+            arrives("a%d_%d" % (t, r), [("land%d" % t, 128 * r, 128 * r + 128)], free["G"] + 2700.0 + 500.0 * i)
+            arrives("z%d_%d" % (t, r), [("zr%d" % t, REG * r, REG * r + 64)], free["G"] + 30000.0)
+
+    def far(t, u, ps, lo, hi):
+        tl, th = lo // 16, hi // 16
+        n = hi - lo
+        bank = "b%d" % u
+        for p in ps:
+            name, s = ("send", REG * me) if p == 0 else ("land%d" % t, 128 * place[p])
+            yield act(a("auxF", 64 * p, 64 * p + 64), a(name, s + 64, s + 128), ACT.Copy)
+            yield act(a("yF3", 64 * p, 64 * p + 64), a(name, s, s + 64), ACT.Copy)
+        for o in spread(3, lo, hi):
+            yield o
+        for o in diag("b5", 128 * u, "auxF", "BOn", "mq%d" % u, "b4", tl, "BO16", n, lo, hi):
+            yield o
+        for j in (0, 2, 1, 3):
+            yield mm(a(bank, n * j, n * j + n), a("SR", 128 * j, 128 * j + 128), a("auxF", lo, hi))
+        yield cp(a("nU3", tl, th), a("b4", tl, th))
+        yield acts_at(3, lo, hi)
+        for j in (0, 1):
+            yield act(a("vbF", 256 * j + lo, 256 * j + hi), a(bank, n * j, n * j + n), ACT.Identity, bias=col(3))
+            yield act(a("wtF", 256 * j + lo, 256 * j + hi), a(bank, n * (2 + j), n * (3 + j)), ACT.Relu, bias=col(1), scale=EPS)
+        yield ts(a("pre3", tl, th), a("b4", tl, th), 13.0, OP.mult, 3.0 + 10240.0, OP.add)
+        yield acts_half(3, lo, hi)
+        for e in (3, 4):
+            for o in level(e, t, u, lo, hi):
+                yield o
+        marks["g%d_%d" % (t, u)] = 1
+        yield tt(a("lv", lo, hi), via(a("paym"), a("nU5", tl, th)), a("yF5", lo, hi), OP.min)
+        yield mm(a(bank, 0, n), a("ZM"), a("lv", lo, hi))
+        yield act(a("zF", lo, hi), a(bank, 0, n), ACT.Sign)
+        for p in ps:
+            r = place[p]
+            if p:
+                yield send(r, a("zF", 64 * p, 64 * p + 64), T["zr%d" % t][:, REG * me:REG * me + 64], "z%d_%d" % (t, me), "lz%d_%d" % (t, r))
+            else:
+                yield act(a("zr%d" % t, REG * me, REG * me + 64), a("zF", 0, 64), ACT.Copy)
+        yield tt(a("NV", lo, hi), via(a("regs_s", 0, 4096), a("rec4", tl, th)), a("zF", lo, hi), OP.add)
+        yield ts(a("NV", lo, hi), a("NV", lo, hi), 15.0, OP.min, -15.0, OP.max)
+        marks["f%d_%d" % (t, u)] = 1
+
+    def first_of(n, q, cm, kc, extra, rec):
+        b = "b7" if n == "h" else "b6"
+        yield ts(a("rf8" + n), a(rec), 2.0 ** -13, OP.mult)
+        yield [mm(a(b, 0, 256), a("BO16"), a(q), True, False), mm(a(b, 0, 256), a("ID"), a(cm), False, False),
+               mm(a(b, 0, 256), extra[0], extra[1], False, True)]
+        yield [mm(a(b, 256, 512), a("BO16"), a(q), True, False), mm(a(b, 256, 512), a("ID"), a(kc), False, False),
+               mm(a(b, 256, 512), extra[0], extra[1], False, True)]
+        yield act(a("Y" + n), via(a("rf8" + n), a("crep", 0, 16)), ACT.Copy, scale=8192.0)
+        yield act(a("Z2" + n, 0, 240), via(a("rf8" + n), a("crep1", 0, 15)), ACT.Copy, scale=8192.0)
+        yield tt(a("eq" + n), a(b, 0, 256), a("Y" + n), OP.is_equal)
+        yield scan(a("lc" + n), a("RST"), a("eq" + n), 0.0)
+        yield tt(a("er" + n, 0, 240), a(b, 256, 496), a("Z2" + n, 0, 240), OP.is_equal)
+        yield tt(a("u" + n), a("lc" + n, 15, 256, 16), a("rf8" + n), OP.add)
+        yield scan(a("ld" + n, 0, 240), a("RST", 0, 240), a("er" + n, 0, 240), 0.0)
+        yield ts(a("off" + n, 0, 16, 2), a("u" + n, 0, 16, 2), 8192.0, OP.mult, col(6), OP.min)
+        yield tt(a("u" + n, 1, 16, 2), a("u" + n, 1, 16, 2), a("ld" + n, 15, 240, 32), OP.add)
+        yield ts(a("off" + n, 1, 16, 2), a("u" + n, 1, 16, 2), 8192.0, OP.mult, col(8), OP.min)
+
+    def change(n, blocks, values):
+        for c in blocks:
+            yield scatter(a("regs_s"), a("off" + n, 2 * c, 2 * c + 2), a(values, 32 * c, 32 * c + 32))
+
+    def waiting(t):
+        yield mark("e")
+        yield ts(a("ng"), a("Q"), col(5), OP.is_ge, 8192.0, OP.mult)
+        for o in first_of("h", "q2", "CMh", "KH", (a("BO"), a("ng")), "rec2"):
+            yield o
+        if t + 1 < RO:
+            yield zeros(a("send"))
+            for o in draws(t + 1):
+                yield o
+            for o in aux_static(t + 1):
+                yield o
+
+    def leaves(t):
+        yield lambda: all("g%d_%d" % (t, u) in marks for u in range(len(FUN)))
+        for o in first_of("f", "q4", "CMf", "KF", (a("SR", 512, 640), a("auxF")), "rec4"):
+            yield o
+        yield lambda: all("f%d_%d" % (t, u) in marks for u in range(len(FUN)))
+        for o in change("f", [2 * place.index(r) + c for r in (3, 2, 1, 0) for c in (1, 0)], "NV"):
+            yield o
+        for lo in (128, 0):
+            yield act(a("zl", lo, lo + 128), via(a("zr%d" % t), a("slot", lo // 16, lo // 16 + 8)), ACT.Copy, scale=-1.0)
+        for lo in (128, 0):
+            yield tt(a("HV", lo, lo + 128), via(a("regs_s", 0, 4096), a("rec2", lo // 16, lo // 16 + 8)), a("zl", lo, lo + 128), OP.add)
+        for lo in (128, 0):
+            yield ts(a("HV", lo, lo + 128), a("HV", lo, lo + 128), 15.0, OP.min, -15.0, OP.max)
+        for o in change("h", list(range(7, -1, -1)), "HV"):
+            yield o
+
+    for t in range(RO):
+        jobs = [(u, home(t, u, lo, hi)) for u, (lo, hi) in enumerate(HUN)]
+        if t == 0:
+            c = constants()
+            for i in range(17):
+                do(next(c))
+            together([(9, c), (8, relu_records()), (9, patterns())] + jobs)
+        else:
+            for o in relu_records():
+                do(o)
+            together(jobs)
+        depart(t)
+        together([(u, far(t, u, FU[u], lo, hi)) for u, (lo, hi) in enumerate(FUN)] + [(8, waiting(t)), (7, leaves(t))])
+
+    order("Y", [("regs_s", 0, 4128)], [])
+    g.sync.dma_start(T.yr[:], T.regs_s[:, 0:4096]).then_inc(T.sem.yo, 16)
+    g.sync.wait_ge(T.sem.yo, 16)
+    for s in ("eV", "eP", "eS", "eG"):
+        g.sync.wait_ge(T.sem[s], count[s])
+    for i in range(7):
+        g.sync.wait_ge(T.sem["ld%d" % i], 16)
+    for t in range(RO):
+        for r in others:
+            for k in ("a", "z", "la", "lz"):
+                g.sync.wait_ge(T.sem["%s%d_%d" % (k, t, r)], 8)

@@ -6,9 +6,12 @@ RO = 3
 REG = 320
 EPS = 2.0 ** -30
 BETA = 2.0 ** -12
-HU = (128, 128)
-FU = ((0,), (1, 2), (3,))
-CG, CW, CS = 64, 64, 64
+CG, CS = 32, 32
+LOOK = 100.0
+MG = 4
+FILL = {"V": 3000.0, "P": 1000.0, "S": 1000.0}
+BANKS = ["b%d" % b for b in range(8)]
+PV = 2736
 
 F, B, H, I, U = "float32", "bfloat16", "float16", "int32", "uint16"
 
@@ -25,32 +28,30 @@ def _scratch():
             at[name] = (big, lo, cols)
     sb("acts_i", 2048, I); sb("regs_s", 4128, B); sb("P", 4096, B); sb("pay_s", 2048, B); sb("paym", 2048, B)
     sb("rch_s", 256, B); sb("n0_i", 16, I); sb("dr_i", 256, I); sb("w_i", 256, I)
-    sb("drb", 256, B); sb("wb", 256, B)
+    sb("drb", 256, B); sb("wb", 256, B); sb("n0f", 16, F); sb("n0u", 16, U); sb("q0", 256, H); sb("TD1", 256, H)
     sb("xr1", 4096, B); sb("xr", 4096, B); sb("W", 4096, B)
     for e in (1, 2, 3, 4):
-        sb("A%d" % e, 256, U); sb("Ah%d" % e, 256, H); sb("q%d" % e, 256, H); sb("rec%d" % e, 16, U); sb("pre%d" % e, 16, F)
-    for e in (1, 2, 3, 4, 5):
-        sb("nU%d" % e, 16, U)
-    for n in ("y1", "y2", "y3", "yF3", "yF4", "yF5", "lv", "zF", "NV", "zl", "HV", "ms", "ind", "auxB", "auxF", "ng"):
+        sb("A%d" % e, 256, U); sb("Ah%d" % e, 256, H)
+        for u in (0, 1):
+            sb("q%d_%d" % (e, u), 384, H); sb("L%d_%d" % (e, u), 16, U)
+    for u in (0, 1):
+        sb("TA%d" % u, 256, F); sb("nF%d" % u, 16, U); sb("vbF%d" % u, 256, F); sb("wtF%d" % u, 256, B)
+    for n in ("y1", "y2", "y3", "y4", "y5", "yF", "lv", "zN", "NV", "old", "HV", "ms", "fl", "aux1", "auxB", "ng"):
         sb(n, 256, B)
-    sb("t1", 256, F); sb("s_i", 16, I); sb("n_i", 16, I); sb("nlf", 64, B); sb("nx", 1024, B)
+    sb("t1", 256, F); sb("ind", 256, H); sb("cum", 256, F)
     for t in range(RO):
         sb("vb%d" % t, 512, F); sb("wt%d" % t, 512, B); sb("auxS%d" % t, 256, B); sb("land%d" % t, 512, B); sb("zr%d" % t, 1280, B)
-    sb("vbF", 512, F); sb("wtF", 512, B)
-    sb("cum", 256, F); sb("Q", 256, H); sb("slot", 16, U); sb("send", 1280, B)
+    sb("send", 1280, B)
     for n in ("h", "f"):
-        sb("rf8" + n, 16, F); sb("Y" + n, 256, F); sb("eq" + n, 256, B); sb("lc" + n, 256, B); sb("u" + n, 16, F)
-        sb("off" + n, 16, U); sb("Z2" + n, 256, F); sb("er" + n, 256, B); sb("ld" + n, 256, B)
-    for u in range(4):
-        sb("mk%d" % u, 128, H); sb("mq%d" % u, 128, H)
+        sb("rf8" + n, 16, F); sb("Y" + n, 512, F); sb("eq" + n, 512, B); sb("lc" + n, 512, B); sb("u" + n, 16, F); sb("off" + n, 16, U)
     sb("Dm", 128, I); sb("Bm", 128, I); sb("pi", 2, I); sb("pk", 2, I); sb("rp", 256, I); sb("li", 256, I)
-    sb("crep", 256, U); sb("crep1", 16, U); sb("KH", 256, B); sb("KF", 256, B); sb("kf", 1, F); sb("pg", 1, F)
-    sb("BO", 128, B); sb("BO16", 128, H); sb("BO5", 128, H); sb("BOn", 128, B)
-    sb("ID", 128, B); sb("E1", 128, B); sb("E2", 128, B); sb("E3", 128, B); sb("OHM", 128, B); sb("DST", 128, B)
-    sb("TRI", 128, B); sb("Z", 144, B); sb("ZM", 128, B)
-    sb("cols", 16, F); sb("SR", 640, B); sb("SEL", 768, B); sb("ZT", 864, B)
-    sb("rd", 256, F); sb("ta", 256, F); sb("tb", 256, F); sb("CMh", 256, B); sb("CMf", 256, B); sb("MX", 256, B)
-    sb("RST", 256, B); sb("ONE", 256, B); sb("SIX", 256, B)
+    sb("crep", 256, U); sb("crep2", 32, U); sb("kf", 1, F); sb("pg", 1, F)
+    for n in ("BO", "ID", "E1", "E2", "E3", "OHM", "DST", "TRI", "ZM", "I5", "In", "BO13", "N13", "D5", "Dn", "R13", "RN13", "M23", "DIF"):
+        sb(n, 128, B)
+    sb("Z", 144, B); sb("ZN", 144, B); sb("CST", 512, B); sb("LC", 32, H)
+    sb("cols", 24, F); sb("SR", 640, B); sb("SEL", 768, B); sb("ZT", 864, B)
+    sb("rd", 256, F); sb("ta", 256, F); sb("tb", 256, F); sb("CMh", 512, B); sb("CMf", 512, B); sb("MX", 256, B)
+    sb("RST", 512, B); sb("ONE", 256, B); sb("SIX", 256, B)
     for b in range(8):
         s["b%d" % b] = ("psum", [128, 512], F)
     return s, at
@@ -67,12 +68,8 @@ def rank_program(g, core, T, topo):
         return
     OP, ACT = AluOpType, ActivationFunctionType
     queue = {"V": g.vector, "P": g.tensor, "S": g.scalar, "G": g, "Y": g.sync}
-    count = {"eV": 0, "eP": 0, "eS": 0, "eG": 0}
-    known = {e: {} for e in queue}
-    free = {e: 0.0 for e in queue}
-    snap, acc, when = {}, {}, {}
-    CY, WAKE, GA, SC = 0.83, 140.0, 1.5, 3.0
-    LAND = {"ld2": 8000.0, "ld4": 9000.0, "ld5": 10000.0, "ld6": 13000.0}
+    CY, WAKE, GA, SC = 0.83, 110.0, 1.56, 3.8
+    ops = []
 
     def a(name, lo=None, hi=None, step=1, rows=128):
         name, base, cols = AT.get(name, (name, 0, 0))
@@ -89,19 +86,449 @@ def rank_program(g, core, T, topo):
     def narrow(x):
         return SCRATCH[x[1][0][0]][2] in (B, U, H)
 
-    def merge(eng, tok):
-        k = known[eng]
-        for s, v in list(snap.get(tok, {}).items()) + [tok]:
-            if k.get(s, 0) < v:
-                k[s] = v
+    def regs_of(*xs):
+        return [r for x in xs if isinstance(x, tuple) for r in x[1]]
+
+    def val(x):
+        return x[0] if isinstance(x, tuple) else x
+
+    def put(eng, call, reads, writes, dur, tok=None, late=0.0, after=()):
+        ops.append({"e": eng, "calls": [call], "r": reads, "w": writes, "d": dur, "tok": tok, "late": late, "after": list(after), "fill": 0})
+        return len(ops) - 1
+
+    def vop(call, out, ins, n, wide=1.0):
+        x = [i for i in ins if i[3]]
+        d = x[0][2] * GA * CY if x else out[2] * SC * CY if out[3] else max(64.0, n * wide) * CY
+        put("V", call, regs_of(*ins), out[1], 50.0 + d)
+
+    def ts(out, in0, s1, op0, s2=None, op1=None):
+        if op1 is None:
+            f = lambda: g.vector.tensor_scalar(out[0], in0[0], val(s1), None, op0)
+        else:
+            f = lambda: g.vector.tensor_scalar(out[0], in0[0], val(s1), val(s2), op0, op1)
+        vop(f, out, [in0] + [x for x in (s1, s2) if isinstance(x, tuple)], in0[2], 0.5 if narrow(out) and narrow(in0) else 1.0)
+
+    def tt(out, in0, in1, op):
+        ps = any(SCRATCH[x[1][0][0]][0] == "psum" for x in (in0, in1))
+        vop(lambda: g.vector.tensor_tensor(out[0], in0[0], in1[0], op), out, [in0, in1], in1[2], 1.0 if ps else 2.0)
+
+    def cp(out, in_):
+        vop(lambda: g.vector.tensor_copy(out[0], in_[0]), out, [in_], in_[2], 0.5 if narrow(out) and narrow(in_) else 1.0)
+
+    def scatter(win, off, in_):
+        vop(lambda: g.vector.tensor_copy(win[0].indirect(off[0]), in_[0]), (None, win[1], in_[2], 1), [in_, off], in_[2])
+
+    def fill(out, c):
+        vop(lambda: g.vector.memset(out[0], c), out, [], out[2], 0.5)
+
+    def scan(out, d0, d1, init):
+        vop(lambda: g.vector.tensor_tensor_scan(out[0], d0[0], d1[0], val(init), OP.mult, OP.add), out,
+            [d0, d1] + [x for x in (init,) if isinstance(x, tuple)], d1[2], 0.5 if narrow(out) and narrow(d1) else 1.0)
+
+    def act(out, in_, func=None, bias=0.0, scale=1.0):
+        if func is None:
+            f = lambda: g.scalar.activation(out[0], in_[0], ACT.Copy, scale=scale)
+        else:
+            f = lambda: g.scalar.activation(out[0], in_[0], func, bias=val(bias), scale=scale)
+        put("S", f, regs_of(in_, bias), out[1], 65.0 + in_[2] * GA * CY if in_[3] else 120.0 + in_[2] * CY)
+
+    def mm(*terms, fill=0):
+        calls, reads, writes, d = [], [], [], 0.0
+        for k, (out, lhsT, rhs) in enumerate(terms):
+            calls.append(lambda out=out, lhsT=lhsT, rhs=rhs, k=k: g.tensor.matmul(out[0], lhsT[0], rhs[0], k == 0, k == len(terms) - 1))
+            reads += [r for r in regs_of(lhsT, rhs) if r not in reads]
+            writes += [r for r in out[1] if r not in writes]
+            d += 10.0 + max(64, rhs[2]) * CY
+            if k % MG == MG - 1 or k == len(terms) - 1:
+                put("P", None, reads, writes + [("lock" + out[1][0][0], 0, 1)], d)
+                ops[-1]["calls"], ops[-1]["fill"] = calls, fill
+                calls, reads, writes, d = [], [], [], 0.0
+
+    def iota(out, pattern, base, ch):
+        put("G", lambda: g.iota(out[0], pattern, base, ch), [], out[1], 130.0 + 2 * out[2] * CY)
+
+    def zeros(out):
+        put("G", lambda: g.iota(out[0], [[0, out[2]]], 0, 0, allow_small_or_imprecise_dtypes=True), [], out[1], 130.0 + 2 * out[2] * CY)
+
+    def sel(out, in_, pattern, base, ch):
+        put("G", lambda: g.affine_select(out[0], in_[0], pattern, OP.is_equal, 0.0, base, ch), regs_of(in_), out[1], 170.0 + 2 * out[2] * CY)
+
+    def load(eng, sem, out, src, reg, late):
+        put(eng, lambda: queue[eng].dma_start(out, src).then_inc(T.sem[sem], 16), [], reg + [("turn" + eng, 0, 1)], 100.0, (sem, 16), late)
+
+    def send(r, src, dst, sem, lsem, also=()):
+        rid, pid, _ = topo.addr(T.cores[r])
+        m = sum(1 << x for x in topo.engines(core, T.cores[r])[:8])
+        return put("G", lambda: g.remote_dma(dst, src[0], T.sem[sem], T.sem[lsem], pid, rid, m), regs_of(src) + list(also), [], 500.0, (lsem, 8), 2800.0)
+
+    def arrives(sem, region, like):
+        put("R", None, [], region[1], 0.0, (sem, 8), 0.0, [like])
+
+    def places(q):
+        def far_key(r):
+            c1, c2 = topo.chip(T.cores[q]), topo.chip(T.cores[r])
+            return 0 if topo.mates(c1, c2) else 1 if topo.same_plane(c1, c2) else 2
+        return [q] + sorted([r for r in range(N) if r != q], key=far_key)
+    place = places(me)
+    others = place[1:]
+
+    load("Y", "ld0", T.n0_i[:], T.n0[:], [("n0_i", 0, 16)], 2000.0)
+    load("S", "ld1", T.rch_s[:], T.rch[:], [("rch_s", 0, 256)], 2400.0)
+    load("Y", "ld2", T.acts_i[:], T.acts[:], [("acts_i", 0, 2048)], 8000.0)
+    load("S", "ld3", T.dr_i[0:96, :], T.dr[:, :], [("dr_i", 0, 256)], 3000.0)
+    load("S", "ld4", T.regs_s[:, 0:2048], T.regs[:, 0:2048], [("regs_s", 0, 2048)], 11000.0)
+    load("Y", "ld5", T.regs_s[:, 2048:4096], T.regs[:, 2048:4096], [("regs_s", 2048, 4096)], 13500.0)
+    load("Y", "ld6", T.pay_s[:], T.pay[:], [("pay_s", 0, 2048)], 16500.0)
+
+    kf = a("kf")
+    def col(j):
+        return a("cols", j, j + 1)
+    home_te = [4 * t + e for t in range(RO) for e in (0, 1)]
+    far_te = [4 * t + e for t in range(RO) for e in (2, 3)]
+
+    iota(a("li"), [[1, 256]], 0, 0)
+    iota(a("pi"), [[0, 2]], 0, 1)
+    iota(a("Bm"), [[1, 8], [0, 16]], 0, 0)
+    iota(a("rp"), [[0, 16], [1, 16]], 0, 0)
+    iota(a("Dm"), [[1, 128]], 0, -1)
+    fill(a("ONE"), 1.0)
+    cp(a("crep"), a("li"))
+    ts(a("pk", 0, 1), a("pi", 0, 1), 15, OP.bitwise_and)
+    ts(a("pk", 1, 2), a("pi", 1, 2), 4, OP.arith_shift_right)
+    cp(a("kf"), a("pk", 0, 1))
+    cp(a("pg"), a("pk", 1, 2))
+    fill(col(3), BETA)
+    fill(col(14), 1.0)
+    fill(col(15), -1.0)
+    for e in (1, 2, 3, 4):
+        fill(col(15 + e), 129.0 + (10240.0 + e - 1023.5) / 2048.0)
+    ts(a("BO"), a("Bm"), a("pg"), OP.is_equal)
+    fill(a("Z"), 0.0)
+    cp(a("Z", 15, 143, 16), a("BO", 0, 128, 16))
+    ts(a("rd"), a("rp"), kf, OP.subtract)
+    ts(a("MX"), a("rd"), 0.0, OP.is_equal)
+    ts(a("TRI"), a("Dm"), 0, OP.is_ge, 64.0, OP.mult)
+    tt(a("TRI"), a("TRI"), a("BO"), OP.mult)
+    fill(a("TRI", 15, 128, 16), 0.0)
+    ts(col(0), kf, 15.0, OP.is_lt)
+    fill(a("SIX"), 0.0625)
+    for j in (0, 1):
+        sel(a("SEL", 128 * j, 128 * j + 128, rows=96), a("ONE", 0, 128, rows=96), [[-12, 8], [0, 16]], -home_te[j], 1)
+    sel(a("ID"), a("ONE", 0, 128), [[-1, 128]], 0, 1)
+    sel(a("E1"), a("BO"), [[1, 128]], -1, -1)
+    sel(a("E3"), a("BO"), [[1, 128]], 15, -1)
+    sel(a("DIF"), a("BO"), [[1, 128]], 1, -1)
+    sel(a("D5"), a("BO"), [[1, 128]], -15, -1)
+    zeros(a("DST"))
+    tt(a("E1"), a("E1"), a("E3"), OP.add)
+    ts(a("E2"), a("ID"), col(0), OP.mult)
+    tt(a("OHM"), a("E1"), a("E2"), OP.subtract)
+    tt(a("DIF"), a("DIF"), a("D5"), OP.add)
+    tt(a("DIF"), a("DIF"), a("E2"), OP.subtract)
+    ts(a("D5"), a("DIF"), 5.0, OP.mult)
+    ts(a("Dn"), a("DIF"), -2048.0, OP.mult)
+    ts(a("I5"), a("ID"), 5.0, OP.mult)
+    ts(a("In"), a("ID"), -2048.0, OP.mult)
+    ts(a("BO13"), a("BO"), 13.0, OP.mult)
+    ts(a("R13"), a("Z", 0, 128), 13.0, OP.mult)
+    fill(a("CST", rows=64), 0.0)
+    for e, step, c in ((1, 16, 274432.0), (2, 1, 274432.0), (3, 16, 274432.0), (4, 1, 272384.0)):
+        lo = 128 * (e - 1) + step - 1
+        fill(a("CST", lo, 128 * e, step, rows=1), c)
+        vop(lambda lo=lo, e=e, step=step: g.vector.memset(T[AT["CST"][0]][32:33, AT["CST"][1] + lo:AT["CST"][1] + 128 * e:step], float(e)), a("CST", lo, 128 * e), [], 64)
+    fill(a("LC"), 0.0)
+    fill(a("LC", 24, 32), -2048.0)
+    fill(col(22), 0.25)
+    ts(col(20), kf, 16.0, OP.mult, -1.0, OP.add)
+    ts(a("LC", 8, 16), a("li", 0, 8), 256.0, OP.mult, col(20), OP.add)
+    ts(col(1), kf, -EPS, OP.mult)
+    ts(col(2), kf, 15.0, OP.is_equal, 16 * EPS, OP.mult)
+    tt(col(1), col(1), col(2), OP.add)
+    cp(a("n0u"), a("n0_i"))
+    cp(a("n0f"), a("n0_i"))
+    tt(a("q0"), via(a("n0f"), a("crep", 0, 16)), a("MX"), OP.mult)
+    for u in range(4):
+        act(a("xr1", 1024 * u, 1024 * u + 1024), via(a("rch_s", 64 * u, 64 * u + 64), a("crep", 0, 64)))
+    cp(a("drb", rows=96), a("dr_i", rows=96))
+    ts(a("w_i", rows=96), a("dr_i", rows=96), 15, OP.bitwise_and)
+    cp(a("wb", rows=96), a("w_i", rows=96))
+    ts(a("y1"), a("rch_s"), -1.0, OP.add)
+    tt(a("DST", 0, 116), a("OHM", 0, 116), a("OHM", 4, 120), OP.add)
+    tt(a("E1", 0, 116), a("OHM", 8, 124), a("OHM", 12, 128), OP.add)
+    ts(a("E3"), a("rp", 0, 128), 4, OP.is_lt)
+    tt(a("DST", 0, 116), a("DST", 0, 116), a("E1", 0, 116), OP.add)
+    tt(a("DST", 0, 116), a("DST", 0, 116), a("E3", 0, 116), OP.mult)
+    ts(col(4), kf, float(REG), OP.mult, -1.0, OP.add)
+    ts(col(5), kf, float(REG), OP.mult, 64.0, OP.add)
+    ts(col(6), kf, 4096.0, OP.add)
+    ts(col(21), kf, 4112.0, OP.add)
+    zeros(a("ZT"))
+    for j in range(6):
+        sel(a("ZT", 144 * j + 15, 144 * j + 143, 16, rows=96), a("ONE", 0, 8, rows=96), [[-12, 8]], -far_te[j], 1)
+    ts(col(7), kf, 2.0, OP.is_equal)
+    ts(col(8), kf, 3.0, OP.is_equal)
+    tt(col(8), col(7), col(8), OP.add)
+    ts(a("ZN"), a("Z"), col(8), OP.mult)
+    ts(a("N13"), a("BO13"), col(8), OP.mult)
+    ts(a("RN13"), a("R13"), col(8), OP.mult)
+    ts(a("M23"), a("Z", 12, 140), col(7), OP.mult)
+    tt(a("M23"), a("ID"), a("M23"), OP.subtract)
+    for j, (row, w) in enumerate(((0, 1.0), (1, 1.0), (5, 1.0), (6, 1.0), (4, -8192.0))):
+        ts(col(9 + j), kf, float(row), OP.is_equal, w, OP.mult)
+        ts(a("SR", 128 * j, 128 * j + 128), a("BO"), col(9 + j), OP.mult)
+    ts(a("ZM"), a("ID"), 16.0, OP.mult)
+    tt(a("ZM"), a("ZM"), a("BO"), OP.subtract)
+    ts(a("ta"), a("rd"), 0.0, OP.is_gt, 16384.0, OP.mult)
+    ts(a("tb"), a("rd"), 0.0, OP.is_equal, -8192.0, OP.mult)
+    tt(a("ta"), a("ta"), a("tb"), OP.add)
+    ts(a("CMh", 0, 256), a("ta"), 2048.0, OP.add)
+    fill(a("CMh", 256, 512), 2048.0)
+    ts(a("CMf"), a("CMh"), 8192.0, OP.add)
+    for h in (0, 1):
+        ts(a("RST", 256 * h, 256 * h + 256), a("rp"), 0, OP.is_gt)
+    cp(a("crep2", 0, 16), a("li", 0, 16))
+    ts(a("crep2", 16, 32), a("li", 0, 16), 1.0, OP.add, 15.0, OP.min)
+    act(a("paym"), a("pay_s"), ACT.Identity, bias=col(15))
+    zeros(a("send"))
+    for t in range(RO):
+        zeros(a("zr%d" % t))
+    for j in range(2, 6):
+        sel(a("SEL", 128 * j, 128 * j + 128, rows=96), a("ONE", 0, 128, rows=96), [[-12, 8], [0, 16]], -home_te[j], 1)
+
+    def draws(t):
+        for src, b in (("drb", "b6"), ("wb", "b7")):
+            for j in (0, 1):
+                s = 128 * (2 * t + j)
+                mm((a(b, 256 * j, 256 * j + 256), a("SEL", s, s + 128, rows=96), a(src, rows=96)))
+            if src == "drb":
+                act(a("vb%d" % t), a(b), ACT.Identity, bias=col(3))
+            else:
+                act(a("wt%d" % t), a(b), ACT.Relu, bias=col(1), scale=EPS)
+        grp = []
+        for src, j, row in (("drb", 0, 0), ("drb", 1, 1), ("wb", 0, 5), ("wb", 1, 6)):
+            s = 144 * (2 * t + j) + 15 - row
+            grp.append((a("b7", 0, 256), a("ZT", s, s + 128, rows=96), a(src, rows=96)))
+        mm(*(grp + [(a("b7", 0, 256), a("Z", 11, 139), a("SIX"))]))
+        act(a("auxS%d" % t), a("b7", 0, 256))
+
+    def lists(out, src, n, first=(), z="Z"):
+        name, lo = src
+        mm(*(list(first) + [(out, a(z, 15 - r, 143 - r), a(name, lo + r, lo + n, 16)) for r in range(16)]))
+
+    def acts_at(e, lo, hi, nodes):
+        cp(a("A%d" % e, lo, hi), via(a("acts_i"), nodes))
+
+    def next_nodes(e, u, node_terms):
+        lo, hi, y = 128 * u, 128 * u + 128, "b%d" % (2 + u)
+        ah = a("Ah%d" % e, lo, hi)
+        ts(ah, a("A%d" % e, lo, hi), -2048.0, OP.add)
+        odd = e % 2
+        mm((a(y, 0, 128), a("I5"), ah), *[(a(y, c0, c1), a(m), x) for c0, c1, m, _, x in node_terms])
+        act(a("fl", lo, hi), a(y, 0, 128), ACT.Identity, bias=col(15 + e), scale=2.0 ** -11)
+        mm((a(y, 128, 256), a("D5" if odd else "I5"), ah), *([(a(y, 128 + c0, 128 + c1), a(m2 if odd else m), x) for c0, c1, m, m2, x in node_terms]
+           + [(a(y, 128, 256), a("CST", 128 * e - 128, 128 * e, rows=64), a("ONE", 0, 128, rows=64)),
+              (a(y, 128, 256), a("Dn" if odd else "In"), a("fl", lo, hi))]))
+        if not odd:
+            mm((a(y, 256, 384), a("ID"), ah))
+            act(a("TA%d" % u), a(y, 128, 384))
+
+    def spread(win, lo, n):
+        for l in range(0, n, CS):
+            name, w0, _ = win[1][0]
+            act(a("xr", 16 * (lo + l), 16 * (lo + l + CS)), via(a(name, w0 + l, w0 + l + CS), a("crep", 0, CS)), ACT.Identity, bias=col(14))
+            ops[-1]["fill"] = 1 + lo // 128
+
+    def weights(e, u, l0):
+        for j in range(l0, l0 + 64, CG):
+            tt(a("W", 16 * j, 16 * (j + CG)), via(a("P"), a("A%d" % e, j, j + CG)), a("xr1" if e == 1 else "xr", 16 * j, 16 * (j + CG)), OP.min)
+            ops[-1]["fill"] = 1 + u
+        c = l0 - 128 * u
+        mm(*[(a("b%d" % u, c, c + 64), a("Z", 15 - k, 143 - k), a("W", 16 * l0 + k, 16 * l0 + 1024, 16)) for k in range(16)], fill=1 + u)
+
+    def choose(e, t, u):
+        lo, hi = 128 * u, 128 * u + 128
+        x, y, z, q, L = "b%d" % u, "b%d" % (2 + u), "b%d" % (4 + u), "q%d_%d" % (e, u), "L%d_%d" % (e, u)
+        if e < 3:
+            vb, wt = [a(n % t, 256 * (e - 1) + lo, 256 * (e - 1) + hi) for n in ("vb%d", "wt%d")]
+        else:
+            vb, wt = [a(n % u, 128 * (e - 3), 128 * (e - 2)) for n in ("vbF%d", "wtF%d")]
+        odd = e % 2
+        ind = a(q, 128, 256) if odd else a("ind", lo, hi)
+        act(a("ms", lo, hi), a(x, 0, 128))
+        mm((a(x, 128, 256), a("ID"), wt), (a(x, 128, 256), a("BO"), a("ms", lo, hi)))
+        mm((a(x, 256, 384), a("TRI"), a("ms", lo, hi)))
+        tt(a("t1", lo, hi), a(x, 128, 256), vb, OP.mult)
+        tt(ind, a(x, 256, 384), a("t1", lo, hi), OP.is_lt)
+        yin = a("yF" if e == 3 else "y%d" % e, lo, hi)
+        yout = a("y%d" % (e + 1), lo, hi)
+        if odd:
+            tt(a(q, 0, 128), a(y, 128, 256), ind, OP.mult)
+            lists(a(z, 0, 16), (q, 0), 256, [(a(z, 0, 16), a("ID"), a("LC", 0, 16))])
+            cp(a(L), a(z, 0, 16))
+            tt(yout, via(a("W", 16 * lo, 16 * hi), a(L, 8, 16)), yin, OP.min)
+            acts_at(e + 1, lo, hi, a(L, 0, 8))
+            spread(yout, lo, 128)
+            next_nodes(e + 1, u, [(0, 128, "BO13", "R13", a(q, 0, 128))])
+            return
+        if e == 2:
+            mm((a(z, 128, 256), a("DST"), ind))
+        mm((a(x, 128, 256), a("OHM"), ind))
+        mm((a(x, 256, 384), a("OHM"), ind))
+        if e == 2:
+            scan(a("cum", lo, hi), a("ONE", lo, hi), a(z, 128, 256), col(4) if u == 0 else a("cum", lo - 1, lo))
+            tt(a(q, 256, 384), a(z, 128, 256), a("cum", lo, hi), OP.mult)
+        tt(a(q, 0, 256), a(x, 128, 384), a("TA%d" % u), OP.mult)
+        if e == 2:
+            mm((a(y, 0, 128), a("ID"), a("auxS%d" % t, lo, hi)), (a(y, 0, 128), a("Z", 13, 141), a(q, 0, 128)))
+            act(a("aux1", lo, hi), a(y, 0, 128))
+        lists(a(z, 0, 16), (q, 128 if e == 2 else 0), 256, [(a(z, 0, 16), a("ID"), a("LC", 16, 32))] if e == 2 else [])
+        ts(a(L), a(z, 0, 16), 2048.0, OP.add)
+        c = 0 if e == 2 else 8
+        act(a("rf8" + "hf"[e // 4], 8 * u, 8 * u + 8), a(z, c, c + 8), ACT.Identity, bias=col(22), scale=2.0 ** -13)
+        tt(yout, via(a("P"), a(L, c, c + 8)), yin, OP.min)
+        if e == 2:
+            mm((a(y, 128, 256), a("M23"), a("aux1", lo, hi)), (a(y, 128, 256), a("Z", 12, 140), a(q, 0, 128)))
+            act(a("auxB", lo, hi), a(y, 128, 256))
+
+    def first_of(n, e, cm, extra):
+        b = "b7" if n == "h" else "b6"
+        for h in (0, 256):
+            mm((a(b, h, h + 256), a("ID"), a(cm, h, h + 256)),
+               *([(a(b, h + 128 * u, h + 128 * u + 128), a("BO"), a("q%d_%d" % (e, u), 128, 256)) for u in (0, 1)]
+                 + [(a(b, h + c0, h + c1), m, x) for c0, c1, m, x in extra]))
+        act(a("Y" + n), via(a("rf8" + n), a("crep2")), scale=8192.0)
+        tt(a("eq" + n), a(b), a("Y" + n), OP.is_equal)
+        scan(a("lc" + n), a("RST"), a("eq" + n), 0.0)
+        tt(a("u" + n), a("lc" + n, 15, 256, 16), a("rf8" + n), OP.add)
+        tt(a("u" + n, 1, 16, 2), a("u" + n, 1, 16, 2), a("lc" + n, 271, 512, 32), OP.add)
+        ts(a("off" + n, 0, 16, 2), a("u" + n, 0, 16, 2), 8192.0, OP.mult, col(6), OP.min)
+        ts(a("off" + n, 1, 16, 2), a("u" + n, 1, 16, 2), 8192.0, OP.mult, col(21), OP.min)
+
+    def change(n, blocks, values):
+        for c in blocks:
+            scatter(a("regs_s"), a("off" + n, 2 * c, 2 * c + 2), a(values, 32 * c, 32 * c + 32))
+
+    draws(0)
+    for u in (0, 1):
+        acts_at(1, 128 * u, 128 * u + 128, a("n0u", 8 * u, 8 * u + 8))
+        next_nodes(1, u, [(0, 128, "BO13", "R13", a("q0", 128 * u, 128 * u + 128))])
+        cp(a("TD1", 128 * u, 128 * u + 128), a("b%d" % (2 + u), 128, 256))
+    for t in range(RO):
+        if t == 0:
+            ts(a("P", 0, 2048), a("regs_s", 0, 2048), 0.0, OP.max)
+            ts(a("P", 2048, 3424), a("regs_s", 2048, 3424), 0.0, OP.max)
+            act(a("P", 3424, 4096), a("regs_s", 3424, 4096), ACT.Relu)
+        else:
+            ts(a("P", 0, PV), a("regs_s", 0, PV), 0.0, OP.max)
+            act(a("P", PV, 4096), a("regs_s", PV, 4096), ACT.Relu)
+            for u in (0, 1):
+                mm((a("b%d" % (2 + u), 128, 256), a("ID"), a("TD1", 128 * u, 128 * u + 128)))
+        for e in (1, 2):
+            for u in (0, 1):
+                weights(e, u, 128 * u)
+                weights(e, u, 128 * u + 64)
+                choose(e, t, u)
+        for u in (0, 1):
+            scatter(a("send", 0, 1216), a("L2_%d" % u, 8, 16), a("auxB", 128 * u, 128 * u + 128))
+        for u in (0, 1):
+            scatter(a("send", 64, 1280), a("L2_%d" % u, 8, 16), a("y3", 128 * u, 128 * u + 128))
+        land, zr = "land%d" % t, "zr%d" % t
+        for p, r in enumerate(others):
+            s = 128 * places(r).index(me)
+            o = send(r, a("send", REG * r, REG * r + 128), T[land][:, s:s + 128], "a%d_%d" % (t, me), "la%d_%d" % (t, r), [(zr, 0, 1280)])
+            arrives("a%d_%d" % (t, r), a(land, 128 * p + 128, 128 * p + 256), o)
+        for u in (0, 1):
+            ts(a("ng", 128 * u, 128 * u + 128), a("q2_%d" % u, 256, 384), col(5), OP.is_ge, 8192.0, OP.mult)
+        first_of("h", 2, "CMh", [(0, 256, a("BO"), a("ng"))])
+
+        def aux(p, lo=0, hi=64):
+            name, s = ("send", REG * me) if p == 0 else (land, 128 * p)
+            return a(name, s + lo, s + hi)
+        for u in (0, 1):
+            z, m, nF = "b%d" % (4 + u), "b%d" % (6 + u), "nF%d" % u
+            if u == 1:
+                lists(a(z, 0, 12), (land, 256), 192, z="ZN")
+                cp(a(nF, 0, 12), a(z, 0, 12))
+            for h in (0, 1):
+                p = 2 * u + h
+                if u == 0:
+                    src = aux(p)[1][0]
+                    lists(a(z, 8 * h, 8 * h + 4), (src[0], src[1]), 64, z="ZN")
+                    cp(a(nF, 8 * h, 8 * h + 4), a(z, 8 * h, 8 * h + 4))
+                acts_at(3, 64 * p, 64 * p + 64, a(nF, 8 * h, 8 * h + 4))
+                spread(aux(p, 64, 128), 64 * p, 64)
+                for j in range(4):
+                    mm((a(m, 128 * j + 64 * h, 128 * j + 64 * h + 64), a("SR", 128 * j, 128 * j + 128), aux(p)))
+                act(a("yF", 64 * p, 64 * p + 64), aux(p, 64, 128))
+                weights(3, u, 64 * p)
+            act(a("vbF%d" % u), a(m, 0, 256), ACT.Identity, bias=col(3))
+            act(a("wtF%d" % u), a(m, 256, 512), ACT.Relu, bias=col(1), scale=EPS)
+            next_nodes(3, u, [(64 * h, 64 * h + 64, "N13", "RN13", aux(2 * u + h)) for h in (0, 1)])
+            choose(3, t, u)
+        if t + 1 < RO:
+            draws(t + 1)
+        for u in (0, 1):
+            lo, hi, x, L = 128 * u, 128 * u + 128, "b%d" % u, "L4_%d" % u
+            weights(4, u, lo)
+            weights(4, u, lo + 64)
+            choose(4, t, u)
+            tt(a("lv", lo, hi), via(a("paym"), a(L, 0, 8)), a("y5", lo, hi), OP.min)
+            mm((a(x, 0, 128), a("ZM"), a("lv", lo, hi)))
+            act(a("zN", lo, hi), a(x, 0, 128), ACT.Sign, scale=-1.0)
+            for p in (2 * u, 2 * u + 1):
+                r = place[p]
+                if p:
+                    o = send(r, a("zN", 64 * p, 64 * p + 64), T[zr][:, REG * me:REG * me + 64], "z%d_%d" % (t, me), "lz%d_%d" % (t, r))
+                    arrives("z%d_%d" % (t, r), a(zr, REG * r, REG * r + 64), o)
+                else:
+                    act(a(zr, REG * me, REG * me + 64), a("zN", 0, 64))
+            tt(a("NV", lo, hi), via(a("regs_s", 0, 4096), a(L, 8, 16)), a("zN", lo, hi), OP.subtract)
+            ts(a("NV", lo, hi), a("NV", lo, hi), 15.0, OP.min, -15.0, OP.max)
+        first_of("f", 4, "CMf", [(64 * p, 64 * p + 64, a("SR", 512, 640), aux(p)) for p in range(4)])
+        if t + 1 < RO:
+            zeros(a("send"))
+        change("f", [2 * place.index(r) + c for r in (3, 2, 1, 0) for c in (1, 0)], "NV")
+        for u in (1, 0):
+            lo, hi = 128 * u, 128 * u + 128
+            act(a("old", lo, hi), via(a("regs_s", 0, 4096), a("L2_%d" % u, 0, 8)))
+            tt(a("HV", lo, hi), via(a(zr), a("L2_%d" % u, 8, 16)), a("old", lo, hi), OP.add)
+            ts(a("HV", lo, hi), a("HV", lo, hi), 15.0, OP.min, -15.0, OP.max)
+        change("h", list(range(7, -1, -1)), "HV")
+    put("Y", lambda: g.sync.dma_start(T.yr[:], T.regs_s[:, 0:4096]).then_inc(T.sem.yo, 16), [("regs_s", 0, 4128)], [], 100.0, ("yo", 16), 8000.0)
+
+    seen = {}
+    for i, o in enumerate(ops):
+        pred = {j: WAKE for j in o["after"]}
+        for regs, w in ((o["r"], False), (o["w"], True)):
+            for name, lo, hi in regs:
+                for j, l2, h2, w2 in seen.get(name, []):
+                    if l2 < hi and lo < h2 and (w or w2) and j != i:
+                        same = ops[j]["e"] == o["e"] and (not w2 or (w and o["e"] == "P"))
+                        pred[j] = max(pred.get(j, -1e9), -ops[j]["late"] if name[:4] == "turn" else 0.0 if same else WAKE)
+        for regs, w in ((o["r"], False), (o["w"], True)):
+            for name, lo, hi in regs:
+                seen[name] = [x for x in seen.get(name, []) if not (w and lo <= x[1] and x[2] <= hi)] + [(i, lo, hi, w)]
+        o["pred"], o["succ"], o["left"] = pred, [], len(pred)
+        for j in pred:
+            ops[j]["succ"].append(i)
+    for i in range(len(ops) - 1, -1, -1):
+        o = ops[i]
+        o["way"] = o["d"] + o["late"] + max([ops[j]["way"] + ops[j]["pred"][i] for j in o["succ"]] + [0.0])
+
+    count = {"eV": 0, "eP": 0, "eS": 0, "eG": 0}
+    known = {e: {} for e in "VPSGYR"}
+    free = {e: 0.0 for e in "VPSGYR"}
+    snap, acc, when = {}, {}, {}
 
     def needs(eng, reads, writes):
         need = {}
         for regs, w in ((reads, False), (writes, True)):
             for name, lo, hi in regs:
-                bank = SCRATCH[name][0] == "psum"
+                bank = name in BANKS
                 for (e2, tok, l2, h2, w2) in acc.get(name, []):
-                    if bank and e2 != eng:
+                    if name not in SCRATCH:
+                        hit = False
+                    elif bank and e2 != eng:
                         hit = True
                     elif l2 < hi and lo < h2:
                         if w and w2:
@@ -116,534 +543,57 @@ def rank_program(g, core, T, topo):
                         need[tok[0]] = tok[1]
         return need
 
-    def order(eng, reads, writes):
-        need = needs(eng, reads, writes)
-        for s in sorted(need):
-            v = need[s]
-            if any(s2 != s and snap.get((s2, need[s2]), {}).get(s, 0) >= v for s2 in need):
-                need[s] = 0
-        for s in sorted(need):
-            if need[s]:
-                queue[eng].wait_ge(T.sem[s], need[s])
-                merge(eng, (s, need[s]))
-
-    def record(eng, tok, reads, writes):
-        for regs, w in ((reads, False), (writes, True)):
-            for name, lo, hi in regs:
-                old = acc.get(name, [])
-                keep = [x for x in old if not (lo <= x[2] and x[3] <= hi and (w or (x[0] == eng and not x[4])))]
-                keep.append((eng, tok, lo, hi, w))
-                acc[name] = keep
-
-    def start(op):
-        if isinstance(op, list):
-            return max(start(o) for o in op)
-        eng, call, reads, writes, dur = op[:5]
-        t = free[eng]
-        for s, v in needs(eng, reads, writes).items():
-            t = max(t, when.get((s, v), 0.0) + WAKE)
+    def start(o):
+        if o["e"] == "R":
+            return max(ops[j]["end"] for j in o["after"])
+        t = free[o["e"]]
+        for s, v in needs(o["e"], o["r"], o["w"]).items():
+            t = max(t, when[(s, v)] + WAKE)
         return t
 
-    def done(tok, eng, t):
-        sn = dict(known[eng]); sn[tok[0]] = tok[1]
-        snap[tok] = sn
-        when[tok] = t
+    def issue(o, t):
+        eng = o["e"]
+        tok = o["tok"]
+        if eng != "R":
+            need = needs(eng, o["r"], o["w"])
+            for s in sorted(need):
+                v = need[s]
+                if not any(s2 != s and need[s2] and snap[(s2, need[s2])].get(s, 0) >= v for s2 in need):
+                    queue[eng].wait_ge(T.sem[s], v)
+                    for s3, v3 in snap[(s, v)].items():
+                        known[eng][s3] = max(known[eng].get(s3, 0), v3)
+                else:
+                    need[s] = 0
+            free[eng] = t + o["d"]
+            for call in o["calls"]:
+                if tok:
+                    call()
+                else:
+                    count["e" + eng] += 1
+                    call().then_inc(T.sem["e" + eng], 1)
+        who = eng if not tok else "D" + tok[0]
+        tok = tok or ("e" + eng, count["e" + eng])
+        snap[tok] = dict(known[eng])
+        snap[tok][tok[0]] = tok[1]
+        o["end"] = when[tok] = t + o["d"] + o["late"]
+        for regs, w in ((o["r"], False), (o["w"], True)):
+            for name, lo, hi in regs:
+                keep = [x for x in acc.get(name, []) if not (lo <= x[2] and x[3] <= hi and (w or (x[0] == who and not x[4])))]
+                acc[name] = keep + [(who, tok, lo, hi, w)]
 
-    def do(op):
-        if isinstance(op, list):
-            for o in op:
-                do(o)
-            return
-        eng, call, reads, writes, dur = op[:5]
-        t = start(op)
-        order(eng, reads, writes)
-        free[eng] = t + dur
-        if len(op) > 5:
-            call()
-            done(op[5], eng, t + 3000.0)
-            record("R" + op[5][0], op[5], reads, [])
-            return
-        s = "e" + eng
-        count[s] += 1
-        call().then_inc(T.sem[s], 1)
-        done((s, count[s]), eng, t + dur)
-        record(eng, (s, count[s]), reads, writes)
+    ready = [i for i, o in enumerate(ops) if not o["left"]]
+    while ready:
+        at = {i: start(ops[i]) for i in ready}
+        i = min(ready, key=lambda j: (at[j] + min(LOOK, ops[j]["d"]), -ops[j]["way"]))
+        soon = [j for j in ready if ops[j]["e"] == ops[i]["e"] and at[j] <= at[i] + min(LOOK, ops[i]["d"])]
+        i = max(soon, key=lambda j: ops[j]["way"] - FILL.get(ops[j]["e"], 0.0) * ops[j]["fill"])
+        issue(ops[i], at[i])
+        ready.remove(i)
+        for j in ops[i]["succ"]:
+            ops[j]["left"] -= 1
+            if not ops[j]["left"]:
+                ready.append(j)
 
-    pool = []
-
-    def spawn(p, j):
-        pool.append([p, j, None])
-
-    def together(jobs):
-        live = pool
-        for p, j in jobs:
-            spawn(p, j)
-        while live:
-            best = None
-            for x in list(live):
-                while not isinstance(x[2], (tuple, list)) and x[2] != "end":
-                    if x[2] is None:
-                        x[2] = next(x[1], "end")
-                    elif x[2]():
-                        x[2] = None
-                    else:
-                        break
-                if x[2] == "end":
-                    live.remove(x)
-                elif isinstance(x[2], (tuple, list)):
-                    k = (start(x[2]), x[0])
-                    if best is None or k < best[0]:
-                        best = (k, x)
-            if best:
-                do(best[1][2])
-                best[1][2] = None
-
-    def regs_of(*xs):
-        return [r for x in xs if isinstance(x, tuple) for r in x[1]]
-
-    def val(x):
-        return x[0] if isinstance(x, tuple) else x
-
-    def vop(call, out, ins, n, wide=1.0):
-        x = [i for i in ins if i[3]]
-        d = x[0][2] * GA * CY if x else out[2] * SC * CY if out[3] else max(64.0, n * wide) * CY
-        return ("V", call, regs_of(*ins), out[1], 60.0 + d)
-
-    def ts(out, in0, s1, op0, s2=None, op1=None):
-        if op1 is None:
-            f = lambda: g.vector.tensor_scalar(out[0], in0[0], val(s1), None, op0)
-        else:
-            f = lambda: g.vector.tensor_scalar(out[0], in0[0], val(s1), val(s2), op0, op1)
-        return vop(f, out, [in0] + [x for x in (s1, s2) if isinstance(x, tuple)], in0[2], 0.5 if narrow(out) and narrow(in0) else 1.0)
-
-    def tt(out, in0, in1, op):
-        ps = any(SCRATCH[x[1][0][0]][0] == "psum" for x in (in0, in1))
-        return vop(lambda: g.vector.tensor_tensor(out[0], in0[0], in1[0], op), out, [in0, in1], in1[2], 1.0 if ps else 2.0)
-
-    def cp(out, in_):
-        return vop(lambda: g.vector.tensor_copy(out[0], in_[0]), out, [in_], in_[2])
-
-    def scatter(win, off, in_):
-        return vop(lambda: g.vector.tensor_copy(win[0].indirect(off[0]), in_[0]), (None, win[1], in_[2], 1), [in_, off], in_[2])
-
-    def fill(out, c):
-        return vop(lambda: g.vector.memset(out[0], c), out, [], out[2], 0.5)
-
-    def scan(out, d0, d1, init):
-        return vop(lambda: g.vector.tensor_tensor_scan(out[0], d0[0], d1[0], val(init), OP.mult, OP.add), out,
-                   [d0, d1] + [x for x in (init,) if isinstance(x, tuple)], d1[2], 0.5 if narrow(out) and narrow(d1) else 1.0)
-
-    def act(out, in_, func, bias=0.0, scale=1.0):
-        if func == ACT.Copy:
-            f = lambda: g.scalar.activation(out[0], in_[0], func, scale=scale)
-        else:
-            f = lambda: g.scalar.activation(out[0], in_[0], func, bias=val(bias), scale=scale)
-        return ("S", f, regs_of(in_, bias), out[1], 65.0 + in_[2] * GA * CY if in_[3] else 165.0 + in_[2] * CY)
-
-    def mm(out, lhsT, rhs, start=True, stop=True):
-        return ("P", lambda: g.tensor.matmul(out[0], lhsT[0], rhs[0], start, stop), regs_of(lhsT, rhs), out[1], 10.0 + max(64, rhs[2]) * CY)
-
-    def iota(out, pattern, base, ch):
-        return ("G", lambda: g.iota(out[0], pattern, base, ch), [], out[1], 130.0 + 2 * out[2] * CY)
-
-    def zeros(out):
-        return ("G", lambda: g.iota(out[0], [[0, out[2]]], 0, 0, allow_small_or_imprecise_dtypes=True), [], out[1], 130.0 + 2 * out[2] * CY)
-
-    def sel(out, in_, pattern, base, ch):
-        return ("G", lambda: g.affine_select(out[0], in_[0], pattern, OP.is_equal, 0.0, base, ch), regs_of(in_), out[1], 170.0 + 2 * out[2] * CY)
-
-    def load(eng, sem, out, src, reg):
-        order(eng, [], reg)
-        queue[eng].dma_start(out, src).then_inc(T.sem[sem], 16)
-        done((sem, 16), eng, LAND.get(sem, 3000.0))
-        record("D" + sem, (sem, 16), [], reg)
-
-    def send(r, src, dst, sem, lsem):
-        rid, pid, _ = topo.addr(T.cores[r])
-        m = sum(1 << x for x in topo.engines(core, T.cores[r])[:8])
-        return ("G", lambda: g.remote_dma(dst, src[0], T.sem[sem], T.sem[lsem], pid, rid, m), regs_of(src), [], 300.0, (lsem, 8))
-
-    def arrives(sem, regions, t):
-        snap[(sem, 8)] = {sem: 8}
-        when[(sem, 8)] = t
-        record("R" + sem, (sem, 8), [], regions)
-
-    def far_key(r):
-        c1, c2 = topo.chip(core), topo.chip(T.cores[r])
-        return 0 if topo.mates(c1, c2) else 1 if topo.same_plane(c1, c2) else 2
-    others = sorted([r for r in range(N) if r != me], key=far_key)
-    place = [me] + others
-    def units(sizes):
-        out, lo = [], 0
-        for n in sizes:
-            out.append((lo, lo + n))
-            lo += n
-        return out
-    HUN = units(HU)
-    FUN = units([64 * len(p) for p in FU])
-
-    load("Y", "ld0", T.n0_i[:], T.n0[:], [("n0_i", 0, 16)])
-    load("S", "ld1", T.rch_s[:], T.rch[:], [("rch_s", 0, 256)])
-    load("Y", "ld2", T.acts_i[:], T.acts[:], [("acts_i", 0, 2048)])
-    load("S", "ld3", T.dr_i[0:96, :], T.dr[:, :], [("dr_i", 0, 256)])
-    load("S", "ld4", T.regs_s[:, 0:2048], T.regs[:, 0:2048], [("regs_s", 0, 2048)])
-    load("Y", "ld5", T.regs_s[:, 2048:4096], T.regs[:, 2048:4096], [("regs_s", 2048, 4096)])
-    load("Y", "ld6", T.pay_s[:], T.pay[:], [("pay_s", 0, 2048)])
-
-    kf = a("kf")
-    def col(j):
-        return a("cols", j, j + 1)
-    home_te = [4 * t + e for t in range(RO) for e in (0, 1)]
-    far_te = [4 * t + e for t in range(RO) for e in (2, 3)]
-    marks = {}
-
-    def mark(k):
-        return lambda: k in marks
-
-    def constants():
-        yield iota(a("li"), [[1, 256]], 0, 0)
-        yield iota(a("pi"), [[0, 2]], 0, 1)
-        yield iota(a("Bm"), [[1, 8], [0, 16]], 0, 0)
-        yield iota(a("rp"), [[0, 16], [1, 16]], 0, 0)
-        yield iota(a("Dm"), [[1, 128]], 0, -1)
-        yield fill(a("ONE"), 1.0)
-        yield cp(a("crep"), a("li"))
-        yield cp(a("nU1"), a("n0_i"))
-        yield ts(a("pk", 0, 1), a("pi", 0, 1), 15, OP.bitwise_and)
-        yield ts(a("pk", 1, 2), a("pi", 1, 2), 4, OP.arith_shift_right)
-        yield cp(a("kf"), a("pk", 0, 1))
-        yield cp(a("pg"), a("pk", 1, 2))
-        yield fill(col(3), BETA)
-        yield fill(col(14), 1.0)
-        yield fill(col(15), -1.0)
-        yield ts(a("BO"), a("Bm"), a("pg"), OP.is_equal)
-        yield fill(a("Z"), 0.0)
-        yield cp(a("Z", 15, 143, 16), a("BO", 0, 128, 16))
-        for u in range(4):
-            yield act(a("xr1", 1024 * u, 1024 * u + 1024), via(a("rch_s", 64 * u, 64 * u + 64), a("crep", 0, 64)), ACT.Copy)
-        yield ts(a("BO16"), a("BO"), 1.0, OP.mult)
-        yield ts(a("BO5"), a("BO"), 5.0, OP.mult)
-        yield ts(a("rd"), a("rp"), kf, OP.subtract)
-        yield ts(a("MX"), a("rd"), 0.0, OP.is_equal)
-        yield ts(a("TRI"), a("Dm"), 0, OP.is_ge, 64.0, OP.mult)
-        yield tt(a("TRI"), a("TRI"), a("BO"), OP.mult)
-        yield fill(a("TRI", 15, 128, 16), 0.0)
-        yield ts(col(0), kf, 15.0, OP.is_lt)
-        yield fill(a("SIX"), 0.0625)
-        yield mark("o")
-        yield tt(a("E1"), a("E1"), a("E3"), OP.add)
-        yield ts(a("E2"), a("ID"), col(0), OP.mult)
-        yield tt(a("OHM"), a("E1"), a("E2"), OP.subtract)
-        yield ts(col(1), kf, -EPS, OP.mult)
-        yield ts(col(2), kf, 15.0, OP.is_equal, 16 * EPS, OP.mult)
-        yield tt(col(1), col(1), col(2), OP.add)
-        yield cp(a("drb", rows=96), a("dr_i", rows=96))
-        yield ts(a("w_i", rows=96), a("dr_i", rows=96), 15, OP.bitwise_and)
-        yield cp(a("wb", rows=96), a("w_i", rows=96))
-        yield ts(a("y1"), a("rch_s"), -1.0, OP.add)
-        yield ts(a("pre1"), a("n0_i"), 13.0, OP.mult, 1.0 + 10240.0, OP.add)
-        for x in draws(0):
-            yield x
-        yield tt(a("DST", 0, 116), a("OHM", 0, 116), a("OHM", 4, 120), OP.add)
-        yield tt(a("E1", 0, 116), a("OHM", 8, 124), a("OHM", 12, 128), OP.add)
-        yield ts(a("E2"), a("rp", 0, 128), 4, OP.is_lt)
-        yield tt(a("DST", 0, 116), a("DST", 0, 116), a("E1", 0, 116), OP.add)
-        yield tt(a("DST", 0, 116), a("DST", 0, 116), a("E2", 0, 116), OP.mult)
-        yield ts(col(4), kf, 320.0, OP.mult, -1.0, OP.add)
-        yield ts(col(5), kf, 320.0, OP.mult, 64.0, OP.add)
-        yield ts(col(6), kf, 4096.0, OP.add)
-        yield mark("z")
-        for x in aux_static(0):
-            yield x
-        marks["c"] = 1
-        yield ts(col(7), kf, 2.0, OP.is_equal)
-        yield ts(col(8), kf, 3.0, OP.is_equal)
-        yield tt(col(7), col(7), col(8), OP.add)
-        yield ts(a("BOn"), a("BO"), col(7), OP.mult)
-        for j, (row, w) in enumerate(((0, 1.0), (1, 1.0), (5, 1.0), (6, 1.0), (4, -8192.0))):
-            yield ts(col(9 + j), kf, float(row), OP.is_equal, w, OP.mult)
-            yield ts(a("SR", 128 * j, 128 * j + 128), a("BO"), col(9 + j), OP.mult)
-        yield ts(a("ZM"), a("ID"), 16.0, OP.mult)
-        yield tt(a("ZM"), a("ZM"), a("BO"), OP.subtract)
-        yield ts(a("ta"), a("rd"), 0.0, OP.is_gt, 16384.0, OP.mult)
-        yield ts(a("tb"), a("rd"), 0.0, OP.is_equal, -8192.0, OP.mult)
-        yield tt(a("ta"), a("ta"), a("tb"), OP.add)
-        yield ts(a("CMh"), a("ta"), 2048.0, OP.add)
-        yield ts(a("CMf"), a("ta"), 10240.0, OP.add)
-        yield ts(a("RST"), a("rp"), 0, OP.is_gt)
-        yield ts(a("crep1"), a("li", 0, 16), 1.0, OP.add)
-        yield ts(col(8), kf, 4112.0, OP.add)
-        yield fill(a("KH"), 2048.0)
-        yield fill(a("KF"), 10240.0)
-        yield act(a("paym"), a("pay_s"), ACT.Identity, bias=col(15))
-        marks["e"] = 1
-
-    def patterns():
-        for j in (0, 1):
-            yield sel(a("SEL", 128 * j, 128 * j + 128, rows=96), a("ONE", 0, 128, rows=96), [[-12, 8], [0, 16]], -home_te[j], 1)
-        yield sel(a("ID"), a("ONE", 0, 128), [[-1, 128]], 0, 1)
-        yield sel(a("E1"), a("BO"), [[1, 128]], -1, -1)
-        yield sel(a("E3"), a("BO"), [[1, 128]], 15, -1)
-        yield zeros(a("DST"))
-        marks["o"] = 1
-        yield zeros(a("ZT"))
-        for j in range(6):
-            yield sel(a("ZT", 144 * j + 15, 144 * j + 143, 16, rows=96), a("ONE", 0, 8, rows=96), [[-12, 8]], -far_te[j], 1)
-        marks["z"] = 1
-        yield zeros(a("send"))
-        for t in range(RO):
-            yield zeros(a("zr%d" % t))
-        for j in range(2, 6):
-            yield sel(a("SEL", 128 * j, 128 * j + 128, rows=96), a("ONE", 0, 128, rows=96), [[-12, 8], [0, 16]], -home_te[j], 1)
-
-    def draws(t):
-        for src, b in (("drb", "b6"), ("wb", "b7")):
-            for j in (0, 1):
-                s = 128 * (2 * t + j)
-                yield mm(a(b, 256 * j, 256 * j + 256), a("SEL", s, s + 128, rows=96), a(src, rows=96))
-            if src == "drb":
-                yield act(a("vb%d" % t), a(b), ACT.Identity, bias=col(3))
-            else:
-                yield act(a("wt%d" % t), a(b), ACT.Relu, bias=col(1), scale=EPS)
-        marks["v%d" % t] = 1
-
-    def aux_static(t):
-        grp = []
-        for k, (src, j, row) in enumerate((("drb", 0, 0), ("drb", 1, 1), ("wb", 0, 5), ("wb", 1, 6))):
-            s = 144 * (2 * t + j) + 15 - row
-            grp.append(mm(a("b7", 0, 256), a("ZT", s, s + 128, rows=96), a(src, rows=96), k == 0, False))
-        yield grp + [mm(a("b7", 0, 256), a("Z", 11, 139), a("SIX"), False, True)]
-        yield act(a("auxS%d" % t), a("b7", 0, 256), ACT.Copy)
-        marks["x%d" % t] = 1
-
-    def relu_records():
-        yield ts(a("P", 0, 2736), a("regs_s", 0, 2736), 0.0, OP.max)
-        yield act(a("P", 2736, 4096), a("regs_s", 2736, 4096), ACT.Relu)
-        marks["P"] = 1
-
-    def acts_at(e, lo, hi):
-        return cp(a("A%d" % e, lo, hi), via(a("acts_i"), a("nU%d" % e, lo // 16, hi // 16)))
-
-    def acts_half(e, lo, hi):
-        return ts(a("Ah%d" % e, lo, hi), a("A%d" % e, lo, hi), -2048.0, OP.add)
-
-    YN = {1: "y1", 2: "y2", 3: "yF3", 4: "yF4"}
-    YO = {1: "y2", 2: "y3", 3: "yF4", 4: "yF5"}
-
-    def spread(e, lo, hi):
-        for l in range(lo, hi, CS):
-            n = min(CS, hi - l)
-            yield act(a("xr", 16 * l, 16 * l + 16 * n), via(a(YN[e], l, l + n), a("crep", 0, n)), ACT.Identity, bias=col(14))
-
-    def diag(b1, c1, src, ones, mk, b2, c2, last, n, lo, hi):
-        yield mm(a(b1, c1, c1 + 128, rows=n), a(src, lo, hi), a(ones))
-        yield tt(a(mk, rows=n), a(b1, c1, c1 + 128, rows=n), a("MX", 0, 128, rows=n), OP.mult)
-        yield mm(a(b2, c2, c2 + n // 16), a(mk, rows=n), a(last, 0, n, 16, rows=n))
-
-    def level(e, t, u, lo, hi):
-        n = hi - lo
-        bank = "b%d" % u
-        tl, th = lo // 16, hi // 16
-        x = "xr1" if e == 1 else "xr"
-        vb, wt = ("vb%d" % t, "wt%d" % t) if e < 3 else ("vbF", "wtF")
-        at = 256 * ((e - 1) % 2)
-        for l in range(lo, hi, CW):
-            m = min(CW, hi - l)
-            for j in range(l, l + m, CG):
-                c = min(CG, l + m - j)
-                yield tt(a("W", 16 * j, 16 * j + 16 * c), via(a("P"), a("A%d" % e, j, j + c)), a(x, 16 * j, 16 * j + 16 * c), OP.min)
-            if e == 1:
-                yield mark("v%d" % t)
-            for k in range(16):
-                yield mm(a(bank, l - lo, l - lo + m), a("Z", 15 - k, 143 - k), a("W", 16 * l + k, 16 * l + 16 * m, 16), k == 0, k == 15)
-        yield act(a("ms", lo, hi), a(bank, 0, n), ACT.Copy)
-        yield mm(a(bank, n, 2 * n), a("ID"), a(wt, at + lo, at + hi), True, False)
-        yield mm(a(bank, n, 2 * n), a("BO"), a("ms", lo, hi), False, True)
-        yield mm(a(bank, 2 * n, 3 * n), a("TRI"), a("ms", lo, hi))
-        yield tt(a("t1", lo, hi), a(bank, n, 2 * n), a(vb, at + lo, at + hi), OP.mult)
-        yield tt(a("ind", lo, hi), a(bank, 2 * n, 3 * n), a("t1", lo, hi), OP.is_lt)
-        yield mm(a(bank, 3 * n, 4 * n), a("OHM"), a("ind", lo, hi))
-
-        def slots():
-            yield mm(a("b4", lo, hi), a("DST"), a("ind", lo, hi))
-            yield lambda: lo == 0 or "s%d_%d" % (t, lo) in marks
-            yield scan(a("cum", lo, hi), a("ONE", lo, hi), a("b4", lo, hi), col(4) if lo == 0 else a("cum", lo - 1, lo))
-            marks["s%d_%d" % (t, hi)] = 1
-            yield tt(a("Q", lo, hi), a("b4", lo, hi), a("cum", lo, hi), OP.mult)
-            for o in diag("b5", 128 * u, "Q", "BO16", "mq%d" % u, "b4", 256 + tl, "BO16", n, lo, hi):
-                yield o
-            yield cp(a("slot", tl, th), a("b4", 256 + tl, 256 + th))
-            marks["S%d_%d" % (t, u)] = 1
-        if e == 2:
-            yield mark("c")
-            spawn(u + 0.2, slots())
-        if e in (2, 4):
-            yield mark("R%d_%d_%d" % (t, e, u))
-        yield tt(a("q%d" % e, lo, hi), a(bank, 3 * n, 4 * n), a("Ah%d" % e, lo, hi), OP.mult)
-        for o in diag(bank, 0, "q%d" % e, "BO16", "mk%d" % u, bank, n, "BO5", n, lo, hi):
-            yield o
-        p = a(bank, n, n + n // 16)
-        yield ts(a("rec%d" % e, tl, th), p, 0.2, OP.mult, 2048.25, OP.add)
-
-        def reaches():
-            yield tt(a(YO[e], lo, hi), via(a("P"), a("rec%d" % e, tl, th)), a(YN[e], lo, hi), OP.min)
-            if e in (1, 3):
-                for o in spread(e + 1, lo, hi):
-                    yield o
-            marks["Y%d_%d_%d" % (t, e, u)] = 1
-        spawn(u - 0.5, reaches())
-        yield tt(a("s_i", tl, th), p, a("pre%d" % e, tl, th), OP.add)
-        yield ts(a("n_i", tl, th), a("s_i", tl, th), 2047, OP.bitwise_and)
-        if e != 2:
-            yield cp(a("nU%d" % (e + 1), tl, th), a("n_i", tl, th))
-        if e in (1, 3):
-            yield acts_at(e + 1, lo, hi)
-
-            def rest():
-                yield ts(a("pre%d" % (e + 1), tl, th), a("n_i", tl, th), 13.0, OP.mult, e + 1.0 + 10240.0, OP.add)
-                yield acts_half(e + 1, lo, hi)
-                marks["R%d_%d_%d" % (t, e + 1, u)] = 1
-            spawn(u + 5, rest())
-        yield mark("Y%d_%d_%d" % (t, e, u))
-
-    def home(t, u, lo, hi):
-        tl, th = lo // 16, hi // 16
-        if t == 0:
-            yield acts_at(1, lo, hi)
-            yield acts_half(1, lo, hi)
-        yield mark("P")
-        for e in (1, 2):
-            for o in level(e, t, u, lo, hi):
-                yield o
-        n = hi - lo
-        w = n // 16
-        f0, x0 = 16 * u, 256 * u
-        yield cp(a("nlf", f0, f0 + w), a("n_i", tl, th))
-        yield tt(a("nlf", f0 + w, f0 + 2 * w), a("n_i", tl, th), a("nlf", f0, f0 + w), OP.subtract)
-        yield tt(a("nx", x0, x0 + 2 * n), via(a("nlf", f0, f0 + 2 * w), a("crep", 0, 2 * w)), a("MX", 0, 2 * n), OP.mult)
-        yield mark("x%d" % t)
-        yield [mm(a("b6", lo, hi), a("ID"), a("auxS%d" % t, lo, hi), True, False),
-               mm(a("b6", lo, hi), a("Z", 13, 141), a("nx", x0, x0 + n), False, False),
-               mm(a("b6", lo, hi), a("Z", 12, 140), a("nx", x0 + n, x0 + 2 * n), False, True)]
-        yield act(a("auxB", lo, hi), a("b6", lo, hi), ACT.Copy)
-        yield mark("S%d_%d" % (t, u))
-        yield scatter(a("send", 0, 1216), a("slot", tl, th), a("y3", lo, hi))
-        marks["y%d_%d" % (t, lo)] = 1
-        yield lambda: all("y%d_%d" % (t, l) in marks for l, h in HUN)
-        yield scatter(a("send", 64, 1280), a("slot", tl, th), a("auxB", lo, hi))
-
-    def depart(t):
-        order("G", [("zr%d" % t, 0, 1280)], [])
-        for r in others:
-            do(send(r, a("send", REG * r, REG * r + 128), T["land%d" % t][:, 128 * me:128 * me + 128], "a%d_%d" % (t, me), "la%d_%d" % (t, r)))
-        for i, r in enumerate(others):
-            arrives("a%d_%d" % (t, r), [("land%d" % t, 128 * r, 128 * r + 128)], free["G"] + 2700.0 + 500.0 * i)
-            arrives("z%d_%d" % (t, r), [("zr%d" % t, REG * r, REG * r + 64)], free["G"] + 30000.0)
-
-    def far(t, u, ps, lo, hi):
-        tl, th = lo // 16, hi // 16
-        n = hi - lo
-        bank = "b%d" % u
-        for p in ps:
-            name, s = ("send", REG * me) if p == 0 else ("land%d" % t, 128 * place[p])
-            yield act(a("auxF", 64 * p, 64 * p + 64), a(name, s + 64, s + 128), ACT.Copy)
-            yield act(a("yF3", 64 * p, 64 * p + 64), a(name, s, s + 64), ACT.Copy)
-        for o in spread(3, lo, hi):
-            yield o
-        for o in diag("b5", 128 * u, "auxF", "BOn", "mq%d" % u, "b4", tl, "BO16", n, lo, hi):
-            yield o
-        for j in (0, 2, 1, 3):
-            yield mm(a(bank, n * j, n * j + n), a("SR", 128 * j, 128 * j + 128), a("auxF", lo, hi))
-        yield cp(a("nU3", tl, th), a("b4", tl, th))
-        yield acts_at(3, lo, hi)
-        for j in (0, 1):
-            yield act(a("vbF", 256 * j + lo, 256 * j + hi), a(bank, n * j, n * j + n), ACT.Identity, bias=col(3))
-            yield act(a("wtF", 256 * j + lo, 256 * j + hi), a(bank, n * (2 + j), n * (3 + j)), ACT.Relu, bias=col(1), scale=EPS)
-        yield ts(a("pre3", tl, th), a("b4", tl, th), 13.0, OP.mult, 3.0 + 10240.0, OP.add)
-        yield acts_half(3, lo, hi)
-        for e in (3, 4):
-            for o in level(e, t, u, lo, hi):
-                yield o
-        marks["g%d_%d" % (t, u)] = 1
-        yield tt(a("lv", lo, hi), via(a("paym"), a("nU5", tl, th)), a("yF5", lo, hi), OP.min)
-        yield mm(a(bank, 0, n), a("ZM"), a("lv", lo, hi))
-        yield act(a("zF", lo, hi), a(bank, 0, n), ACT.Sign)
-        for p in ps:
-            r = place[p]
-            if p:
-                yield send(r, a("zF", 64 * p, 64 * p + 64), T["zr%d" % t][:, REG * me:REG * me + 64], "z%d_%d" % (t, me), "lz%d_%d" % (t, r))
-            else:
-                yield act(a("zr%d" % t, REG * me, REG * me + 64), a("zF", 0, 64), ACT.Copy)
-        yield tt(a("NV", lo, hi), via(a("regs_s", 0, 4096), a("rec4", tl, th)), a("zF", lo, hi), OP.add)
-        yield ts(a("NV", lo, hi), a("NV", lo, hi), 15.0, OP.min, -15.0, OP.max)
-        marks["f%d_%d" % (t, u)] = 1
-
-    def first_of(n, q, cm, kc, extra, rec):
-        b = "b7" if n == "h" else "b6"
-        yield ts(a("rf8" + n), a(rec), 2.0 ** -13, OP.mult)
-        yield [mm(a(b, 0, 256), a("BO16"), a(q), True, False), mm(a(b, 0, 256), a("ID"), a(cm), False, False),
-               mm(a(b, 0, 256), extra[0], extra[1], False, True)]
-        yield [mm(a(b, 256, 512), a("BO16"), a(q), True, False), mm(a(b, 256, 512), a("ID"), a(kc), False, False),
-               mm(a(b, 256, 512), extra[0], extra[1], False, True)]
-        yield act(a("Y" + n), via(a("rf8" + n), a("crep", 0, 16)), ACT.Copy, scale=8192.0)
-        yield act(a("Z2" + n, 0, 240), via(a("rf8" + n), a("crep1", 0, 15)), ACT.Copy, scale=8192.0)
-        yield tt(a("eq" + n), a(b, 0, 256), a("Y" + n), OP.is_equal)
-        yield scan(a("lc" + n), a("RST"), a("eq" + n), 0.0)
-        yield tt(a("er" + n, 0, 240), a(b, 256, 496), a("Z2" + n, 0, 240), OP.is_equal)
-        yield tt(a("u" + n), a("lc" + n, 15, 256, 16), a("rf8" + n), OP.add)
-        yield scan(a("ld" + n, 0, 240), a("RST", 0, 240), a("er" + n, 0, 240), 0.0)
-        yield ts(a("off" + n, 0, 16, 2), a("u" + n, 0, 16, 2), 8192.0, OP.mult, col(6), OP.min)
-        yield tt(a("u" + n, 1, 16, 2), a("u" + n, 1, 16, 2), a("ld" + n, 15, 240, 32), OP.add)
-        yield ts(a("off" + n, 1, 16, 2), a("u" + n, 1, 16, 2), 8192.0, OP.mult, col(8), OP.min)
-
-    def change(n, blocks, values):
-        for c in blocks:
-            yield scatter(a("regs_s"), a("off" + n, 2 * c, 2 * c + 2), a(values, 32 * c, 32 * c + 32))
-
-    def waiting(t):
-        yield mark("e")
-        yield ts(a("ng"), a("Q"), col(5), OP.is_ge, 8192.0, OP.mult)
-        for o in first_of("h", "q2", "CMh", "KH", (a("BO"), a("ng")), "rec2"):
-            yield o
-        if t + 1 < RO:
-            yield zeros(a("send"))
-            for o in draws(t + 1):
-                yield o
-            for o in aux_static(t + 1):
-                yield o
-
-    def leaves(t):
-        yield lambda: all("g%d_%d" % (t, u) in marks for u in range(len(FUN)))
-        for o in first_of("f", "q4", "CMf", "KF", (a("SR", 512, 640), a("auxF")), "rec4"):
-            yield o
-        yield lambda: all("f%d_%d" % (t, u) in marks for u in range(len(FUN)))
-        for o in change("f", [2 * place.index(r) + c for r in (3, 2, 1, 0) for c in (1, 0)], "NV"):
-            yield o
-        for lo in (128, 0):
-            yield act(a("zl", lo, lo + 128), via(a("zr%d" % t), a("slot", lo // 16, lo // 16 + 8)), ACT.Copy, scale=-1.0)
-        for lo in (128, 0):
-            yield tt(a("HV", lo, lo + 128), via(a("regs_s", 0, 4096), a("rec2", lo // 16, lo // 16 + 8)), a("zl", lo, lo + 128), OP.add)
-        for lo in (128, 0):
-            yield ts(a("HV", lo, lo + 128), a("HV", lo, lo + 128), 15.0, OP.min, -15.0, OP.max)
-        for o in change("h", list(range(7, -1, -1)), "HV"):
-            yield o
-
-    for t in range(RO):
-        jobs = [(u, home(t, u, lo, hi)) for u, (lo, hi) in enumerate(HUN)]
-        if t == 0:
-            c = constants()
-            for i in range(17):
-                do(next(c))
-            together([(9, c), (8, relu_records()), (9, patterns())] + jobs)
-        else:
-            for o in relu_records():
-                do(o)
-            together(jobs)
-        depart(t)
-        together([(u, far(t, u, FU[u], lo, hi)) for u, (lo, hi) in enumerate(FUN)] + [(8, waiting(t)), (7, leaves(t))])
-
-    order("Y", [("regs_s", 0, 4128)], [])
-    g.sync.dma_start(T.yr[:], T.regs_s[:, 0:4096]).then_inc(T.sem.yo, 16)
     g.sync.wait_ge(T.sem.yo, 16)
     for s in ("eV", "eP", "eS", "eG"):
         g.sync.wait_ge(T.sem[s], count[s])

@@ -7,9 +7,14 @@ REG = 320
 EPS = 2.0 ** -30
 BETA = 2.0 ** -12
 CG, CS = 32, 32
-LOOK = 100.0
 MG = 4
-FILL = {"V": 3000.0, "P": 1000.0, "S": 1000.0}
+SELF, FAR = 40.0, 6000.0
+FILL = {"V": 2000.0, "P": 500.0, "S": 2000.0}
+HOLD = {"V": 1.0, "S": 5.0, "P": 5.0, "G": 5.0}
+DEPTH = 3
+PCY = 0.45
+BYS = (1, 3, 4, 5, 6)
+LAND = (2000.0, 2200.0, 6000.0, 2400.0, 7800.0, 9600.0, 11500.0)
 BANKS = ["b%d" % b for b in range(8)]
 PV = 2736
 
@@ -26,7 +31,7 @@ def _scratch():
             lo = s[big][1][1] if big in s else 0
             s[big] = ("sbuf", [128, lo + cols + -cols % 32], d)
             at[name] = (big, lo, cols)
-    sb("acts_i", 2048, I); sb("regs_s", 4128, B); sb("P", 4096, B); sb("pay_s", 2048, B); sb("paym", 2048, B)
+    sb("acts_i", 2048, I); sb("regs_s", 4128, B); sb("P", 4128, B); sb("pay_s", 2048, B); sb("paym", 2048, B)
     sb("rch_s", 256, B); sb("n0_i", 16, I); sb("dr_i", 256, I); sb("w_i", 256, I)
     sb("drb", 256, B); sb("wb", 256, B); sb("n0f", 16, F); sb("n0u", 16, U); sb("q0", 256, H); sb("TD1", 256, H)
     sb("xr1", 4096, B); sb("xr", 4096, B); sb("W", 4096, B)
@@ -36,16 +41,16 @@ def _scratch():
             sb("q%d_%d" % (e, u), 384, H); sb("L%d_%d" % (e, u), 16, U)
     for u in (0, 1):
         sb("TA%d" % u, 256, F); sb("nF%d" % u, 16, U); sb("vbF%d" % u, 256, F); sb("wtF%d" % u, 256, B)
-    for n in ("y1", "y2", "y3", "y4", "y5", "yF", "lv", "zN", "NV", "old", "HV", "ms", "fl", "aux1", "auxB", "ng"):
+    for n in ("y1", "y2", "y3", "y4", "y5", "yF", "lv", "zN", "NV", "old", "HV", "HP", "ms", "fl", "aux1", "auxB", "ng"):
         sb(n, 256, B)
     sb("t1", 256, F); sb("ind", 256, H); sb("cum", 256, F)
     for t in range(RO):
         sb("vb%d" % t, 512, F); sb("wt%d" % t, 512, B); sb("auxS%d" % t, 256, B); sb("land%d" % t, 512, B); sb("zr%d" % t, 1280, B)
-    sb("send", 1280, B)
+        sb("send%d" % t, 1280, B)
     for n in ("h", "f"):
         sb("rf8" + n, 16, F); sb("Y" + n, 512, F); sb("eq" + n, 512, B); sb("lc" + n, 512, B); sb("u" + n, 16, F); sb("off" + n, 16, U)
-    sb("Dm", 128, I); sb("Bm", 128, I); sb("pi", 2, I); sb("pk", 2, I); sb("rp", 256, I); sb("li", 256, I)
-    sb("crep", 256, U); sb("crep2", 32, U); sb("kf", 1, F); sb("pg", 1, F)
+    sb("Dm", 128, I); sb("Bm", 128, I); sb("pi", 2, I); sb("pk", 2, I); sb("rp", 256, I); sb("li", 64, I)
+    sb("crep", 64, U); sb("crep2", 32, U); sb("kf", 1, F); sb("pg", 1, F)
     for n in ("BO", "ID", "E1", "E2", "E3", "OHM", "DST", "TRI", "ZM", "I5", "In", "BO13", "N13", "D5", "Dn", "R13", "RN13", "M23", "DIF"):
         sb(n, 128, B)
     sb("Z", 144, B); sb("ZN", 144, B); sb("CST", 512, B); sb("LC", 32, H)
@@ -96,6 +101,11 @@ def rank_program(g, core, T, topo):
         ops.append({"e": eng, "calls": [call], "r": reads, "w": writes, "d": dur, "tok": tok, "late": late, "after": list(after), "fill": 0})
         return len(ops) - 1
 
+    def stream():
+        if ops[-1]["e"] == "V":
+            ops[-1]["w"] = ops[-1]["w"] + [("turnV", 0, 1)]
+        ops[-1]["fill"] = 1
+
     def vop(call, out, ins, n, wide=1.0):
         x = [i for i in ins if i[3]]
         d = x[0][2] * GA * CY if x else out[2] * SC * CY if out[3] else max(64.0, n * wide) * CY
@@ -138,9 +148,9 @@ def rank_program(g, core, T, topo):
             calls.append(lambda out=out, lhsT=lhsT, rhs=rhs, k=k: g.tensor.matmul(out[0], lhsT[0], rhs[0], k == 0, k == len(terms) - 1))
             reads += [r for r in regs_of(lhsT, rhs) if r not in reads]
             writes += [r for r in out[1] if r not in writes]
-            d += 10.0 + max(64, rhs[2]) * CY
+            d += 15.0 + max(64, rhs[2]) * PCY
             if k % MG == MG - 1 or k == len(terms) - 1:
-                put("P", None, reads, writes + [("lock" + out[1][0][0], 0, 1)], d)
+                put("P", None, reads, writes + [("lock" + out[1][0][0], 0, 1)] + [("turnP", 0, 1)] * fill, d)
                 ops[-1]["calls"], ops[-1]["fill"] = calls, fill
                 calls, reads, writes, d = [], [], [], 0.0
 
@@ -172,13 +182,13 @@ def rank_program(g, core, T, topo):
     place = places(me)
     others = place[1:]
 
-    load("Y", "ld0", T.n0_i[:], T.n0[:], [("n0_i", 0, 16)], 2000.0)
-    load("S", "ld1", T.rch_s[:], T.rch[:], [("rch_s", 0, 256)], 2400.0)
-    load("Y", "ld2", T.acts_i[:], T.acts[:], [("acts_i", 0, 2048)], 8000.0)
-    load("S", "ld3", T.dr_i[0:96, :], T.dr[:, :], [("dr_i", 0, 256)], 3000.0)
-    load("S", "ld4", T.regs_s[:, 0:2048], T.regs[:, 0:2048], [("regs_s", 0, 2048)], 11000.0)
-    load("Y", "ld5", T.regs_s[:, 2048:4096], T.regs[:, 2048:4096], [("regs_s", 2048, 4096)], 13500.0)
-    load("Y", "ld6", T.pay_s[:], T.pay[:], [("pay_s", 0, 2048)], 16500.0)
+    load("Y", "ld0", T.n0_i[:], T.n0[:], [("n0_i", 0, 16)], LAND[0])
+    load("S", "ld1", T.rch_s[:], T.rch[:], [("rch_s", 0, 256)], LAND[1])
+    load("S", "ld3", T.dr_i[0:96, :], T.dr[:, :], [("dr_i", 0, 256)], LAND[3])
+    load("Y", "ld2", T.acts_i[:], T.acts[:], [("acts_i", 0, 2048)], LAND[2])
+    load("Y", "ld4", T.regs_s[:, 0:2048], T.regs[:, 0:2048], [("regs_s", 0, 2048)], LAND[4])
+    load("Y", "ld5", T.regs_s[:, 2048:4096], T.regs[:, 2048:4096], [("regs_s", 2048, 4096)], LAND[5])
+    load("Y", "ld6", T.pay_s[:], T.pay[:], [("pay_s", 0, 2048)], LAND[6])
 
     kf = a("kf")
     def col(j):
@@ -186,7 +196,7 @@ def rank_program(g, core, T, topo):
     home_te = [4 * t + e for t in range(RO) for e in (0, 1)]
     far_te = [4 * t + e for t in range(RO) for e in (2, 3)]
 
-    iota(a("li"), [[1, 256]], 0, 0)
+    iota(a("li"), [[1, 64]], 0, 0)
     iota(a("pi"), [[0, 2]], 0, 1)
     iota(a("Bm"), [[1, 8], [0, 16]], 0, 0)
     iota(a("rp"), [[0, 16], [1, 16]], 0, 0)
@@ -197,11 +207,6 @@ def rank_program(g, core, T, topo):
     ts(a("pk", 1, 2), a("pi", 1, 2), 4, OP.arith_shift_right)
     cp(a("kf"), a("pk", 0, 1))
     cp(a("pg"), a("pk", 1, 2))
-    fill(col(3), BETA)
-    fill(col(14), 1.0)
-    fill(col(15), -1.0)
-    for e in (1, 2, 3, 4):
-        fill(col(15 + e), 129.0 + (10240.0 + e - 1023.5) / 2048.0)
     ts(a("BO"), a("Bm"), a("pg"), OP.is_equal)
     fill(a("Z"), 0.0)
     cp(a("Z", 15, 143, 16), a("BO", 0, 128, 16))
@@ -238,7 +243,6 @@ def rank_program(g, core, T, topo):
         vop(lambda lo=lo, e=e, step=step: g.vector.memset(T[AT["CST"][0]][32:33, AT["CST"][1] + lo:AT["CST"][1] + 128 * e:step], float(e)), a("CST", lo, 128 * e), [], 64)
     fill(a("LC"), 0.0)
     fill(a("LC", 24, 32), -2048.0)
-    fill(col(22), 0.25)
     ts(col(20), kf, 16.0, OP.mult, -1.0, OP.add)
     ts(a("LC", 8, 16), a("li", 0, 8), 256.0, OP.mult, col(20), OP.add)
     ts(col(1), kf, -EPS, OP.mult)
@@ -288,9 +292,9 @@ def rank_program(g, core, T, topo):
         ts(a("RST", 256 * h, 256 * h + 256), a("rp"), 0, OP.is_gt)
     cp(a("crep2", 0, 16), a("li", 0, 16))
     ts(a("crep2", 16, 32), a("li", 0, 16), 1.0, OP.add, 15.0, OP.min)
-    act(a("paym"), a("pay_s"), ACT.Identity, bias=col(15))
-    zeros(a("send"))
+    act(a("paym"), a("pay_s"), ACT.Identity, bias=-1.0)
     for t in range(RO):
+        zeros(a("send%d" % t))
         zeros(a("zr%d" % t))
     for j in range(2, 6):
         sel(a("SEL", 128 * j, 128 * j + 128, rows=96), a("ONE", 0, 128, rows=96), [[-12, 8], [0, 16]], -home_te[j], 1)
@@ -301,15 +305,15 @@ def rank_program(g, core, T, topo):
                 s = 128 * (2 * t + j)
                 mm((a(b, 256 * j, 256 * j + 256), a("SEL", s, s + 128, rows=96), a(src, rows=96)))
             if src == "drb":
-                act(a("vb%d" % t), a(b), ACT.Identity, bias=col(3))
+                act(a("vb%d" % t), a(b), ACT.Identity, bias=BETA)
             else:
                 act(a("wt%d" % t), a(b), ACT.Relu, bias=col(1), scale=EPS)
         grp = []
         for src, j, row in (("drb", 0, 0), ("drb", 1, 1), ("wb", 0, 5), ("wb", 1, 6)):
             s = 144 * (2 * t + j) + 15 - row
-            grp.append((a("b7", 0, 256), a("ZT", s, s + 128, rows=96), a(src, rows=96)))
-        mm(*(grp + [(a("b7", 0, 256), a("Z", 11, 139), a("SIX"))]))
-        act(a("auxS%d" % t), a("b7", 0, 256))
+            grp.append((a("b5", 256, 512), a("ZT", s, s + 128, rows=96), a(src, rows=96)))
+        mm(*(grp + [(a("b5", 256, 512), a("Z", 11, 139), a("SIX"))]))
+        act(a("auxS%d" % t), a("b5", 256, 512))
 
     def lists(out, src, n, first=(), z="Z"):
         name, lo = src
@@ -324,7 +328,7 @@ def rank_program(g, core, T, topo):
         ts(ah, a("A%d" % e, lo, hi), -2048.0, OP.add)
         odd = e % 2
         mm((a(y, 0, 128), a("I5"), ah), *[(a(y, c0, c1), a(m), x) for c0, c1, m, _, x in node_terms])
-        act(a("fl", lo, hi), a(y, 0, 128), ACT.Identity, bias=col(15 + e), scale=2.0 ** -11)
+        act(a("fl", lo, hi), a(y, 0, 128), ACT.Identity, bias=129.0 + (10240.0 + e - 1023.5) / 2048.0, scale=2.0 ** -11)
         mm((a(y, 128, 256), a("D5" if odd else "I5"), ah), *([(a(y, 128 + c0, 128 + c1), a(m2 if odd else m), x) for c0, c1, m, m2, x in node_terms]
            + [(a(y, 128, 256), a("CST", 128 * e - 128, 128 * e, rows=64), a("ONE", 0, 128, rows=64)),
               (a(y, 128, 256), a("Dn" if odd else "In"), a("fl", lo, hi))]))
@@ -335,15 +339,23 @@ def rank_program(g, core, T, topo):
     def spread(win, lo, n):
         for l in range(0, n, CS):
             name, w0, _ = win[1][0]
-            act(a("xr", 16 * (lo + l), 16 * (lo + l + CS)), via(a(name, w0 + l, w0 + l + CS), a("crep", 0, CS)), ACT.Identity, bias=col(14))
-            ops[-1]["fill"] = 1 + lo // 128
+            act(a("xr", 16 * (lo + l), 16 * (lo + l + CS)), via(a(name, w0 + l, w0 + l + CS), a("crep", 0, CS)), ACT.Identity, bias=1.0)
+            stream()
 
     def weights(e, u, l0):
         for j in range(l0, l0 + 64, CG):
-            tt(a("W", 16 * j, 16 * (j + CG)), via(a("P"), a("A%d" % e, j, j + CG)), a("xr1" if e == 1 else "xr", 16 * j, 16 * (j + CG)), OP.min)
-            ops[-1]["fill"] = 1 + u
+            w, x, p = a("W", 16 * j, 16 * (j + CG)), a("xr1" if e == 1 else "xr", 16 * j, 16 * (j + CG)), via(a("P", 0, 4096), a("A%d" % e, j, j + CG))
+            if e == 1 and j // CG in BYS:
+                b = a("b%d" % (6 + BYS.index(j // CG) % 2))
+                act(w, p)
+                stream()
+                mm((b, a("ID"), x))
+                tt(w, b, w, OP.min)
+            else:
+                tt(w, p, x, OP.min)
+            stream()
         c = l0 - 128 * u
-        mm(*[(a("b%d" % u, c, c + 64), a("Z", 15 - k, 143 - k), a("W", 16 * l0 + k, 16 * l0 + 1024, 16)) for k in range(16)], fill=1 + u)
+        mm(*[(a("b%d" % u, c, c + 64), a("Z", 15 - k, 143 - k), a("W", 16 * l0 + k, 16 * l0 + 1024, 16)) for k in range(16)], fill=1)
 
     def choose(e, t, u):
         lo, hi = 128 * u, 128 * u + 128
@@ -384,8 +396,8 @@ def rank_program(g, core, T, topo):
         lists(a(z, 0, 16), (q, 128 if e == 2 else 0), 256, [(a(z, 0, 16), a("ID"), a("LC", 16, 32))] if e == 2 else [])
         ts(a(L), a(z, 0, 16), 2048.0, OP.add)
         c = 0 if e == 2 else 8
-        act(a("rf8" + "hf"[e // 4], 8 * u, 8 * u + 8), a(z, c, c + 8), ACT.Identity, bias=col(22), scale=2.0 ** -13)
-        tt(yout, via(a("P"), a(L, c, c + 8)), yin, OP.min)
+        act(a("rf8" + "hf"[e // 4], 8 * u, 8 * u + 8), a(z, c, c + 8), ACT.Identity, bias=0.25, scale=2.0 ** -13)
+        tt(yout, via(a("P", 0, 4096), a(L, c, c + 8)), yin, OP.min)
         if e == 2:
             mm((a(y, 128, 256), a("M23"), a("aux1", lo, hi)), (a(y, 128, 256), a("Z", 12, 140), a(q, 0, 128)))
             act(a("auxB", lo, hi), a(y, 128, 256))
@@ -404,9 +416,9 @@ def rank_program(g, core, T, topo):
         ts(a("off" + n, 0, 16, 2), a("u" + n, 0, 16, 2), 8192.0, OP.mult, col(6), OP.min)
         ts(a("off" + n, 1, 16, 2), a("u" + n, 1, 16, 2), 8192.0, OP.mult, col(21), OP.min)
 
-    def change(n, blocks, values):
+    def change(n, blocks, values, table="regs_s"):
         for c in blocks:
-            scatter(a("regs_s"), a("off" + n, 2 * c, 2 * c + 2), a(values, 32 * c, 32 * c + 32))
+            scatter(a(table), a("off" + n, 2 * c, 2 * c + 2), a(values, 32 * c, 32 * c + 32))
 
     draws(0)
     for u in (0, 1):
@@ -419,8 +431,6 @@ def rank_program(g, core, T, topo):
             ts(a("P", 2048, 3424), a("regs_s", 2048, 3424), 0.0, OP.max)
             act(a("P", 3424, 4096), a("regs_s", 3424, 4096), ACT.Relu)
         else:
-            ts(a("P", 0, PV), a("regs_s", 0, PV), 0.0, OP.max)
-            act(a("P", PV, 4096), a("regs_s", PV, 4096), ACT.Relu)
             for u in (0, 1):
                 mm((a("b%d" % (2 + u), 128, 256), a("ID"), a("TD1", 128 * u, 128 * u + 128)))
         for e in (1, 2):
@@ -428,21 +438,21 @@ def rank_program(g, core, T, topo):
                 weights(e, u, 128 * u)
                 weights(e, u, 128 * u + 64)
                 choose(e, t, u)
+        land, zr, out = "land%d" % t, "zr%d" % t, "send%d" % t
         for u in (0, 1):
-            scatter(a("send", 0, 1216), a("L2_%d" % u, 8, 16), a("auxB", 128 * u, 128 * u + 128))
+            scatter(a(out, 0, 1216), a("L2_%d" % u, 8, 16), a("auxB", 128 * u, 128 * u + 128))
         for u in (0, 1):
-            scatter(a("send", 64, 1280), a("L2_%d" % u, 8, 16), a("y3", 128 * u, 128 * u + 128))
-        land, zr = "land%d" % t, "zr%d" % t
+            scatter(a(out, 64, 1280), a("L2_%d" % u, 8, 16), a("y3", 128 * u, 128 * u + 128))
         for p, r in enumerate(others):
             s = 128 * places(r).index(me)
-            o = send(r, a("send", REG * r, REG * r + 128), T[land][:, s:s + 128], "a%d_%d" % (t, me), "la%d_%d" % (t, r), [(zr, 0, 1280)])
+            o = send(r, a(out, REG * r, REG * r + 128), T[land][:, s:s + 128], "a%d_%d" % (t, me), "la%d_%d" % (t, r), [(zr, 0, 1280)])
             arrives("a%d_%d" % (t, r), a(land, 128 * p + 128, 128 * p + 256), o)
         for u in (0, 1):
             ts(a("ng", 128 * u, 128 * u + 128), a("q2_%d" % u, 256, 384), col(5), OP.is_ge, 8192.0, OP.mult)
         first_of("h", 2, "CMh", [(0, 256, a("BO"), a("ng"))])
 
         def aux(p, lo=0, hi=64):
-            name, s = ("send", REG * me) if p == 0 else (land, 128 * p)
+            name, s = (out, REG * me) if p == 0 else (land, 128 * p)
             return a(name, s + lo, s + hi)
         for u in (0, 1):
             z, m, nF = "b%d" % (4 + u), "b%d" % (6 + u), "nF%d" % u
@@ -461,7 +471,7 @@ def rank_program(g, core, T, topo):
                     mm((a(m, 128 * j + 64 * h, 128 * j + 64 * h + 64), a("SR", 128 * j, 128 * j + 128), aux(p)))
                 act(a("yF", 64 * p, 64 * p + 64), aux(p, 64, 128))
                 weights(3, u, 64 * p)
-            act(a("vbF%d" % u), a(m, 0, 256), ACT.Identity, bias=col(3))
+            act(a("vbF%d" % u), a(m, 0, 256), ACT.Identity, bias=BETA)
             act(a("wtF%d" % u), a(m, 256, 512), ACT.Relu, bias=col(1), scale=EPS)
             next_nodes(3, u, [(64 * h, 64 * h + 64, "N13", "RN13", aux(2 * u + h)) for h in (0, 1)])
             choose(3, t, u)
@@ -485,14 +495,21 @@ def rank_program(g, core, T, topo):
             tt(a("NV", lo, hi), via(a("regs_s", 0, 4096), a(L, 8, 16)), a("zN", lo, hi), OP.subtract)
             ts(a("NV", lo, hi), a("NV", lo, hi), 15.0, OP.min, -15.0, OP.max)
         first_of("f", 4, "CMf", [(64 * p, 64 * p + 64, a("SR", 512, 640), aux(p)) for p in range(4)])
-        if t + 1 < RO:
-            zeros(a("send"))
         change("f", [2 * place.index(r) + c for r in (3, 2, 1, 0) for c in (1, 0)], "NV")
         for u in (1, 0):
+            act(a("old", 128 * u, 128 * u + 128), via(a("regs_s", 0, 4096), a("L2_%d" % u, 0, 8)))
+        if t + 1 < RO:
+            ts(a("P", 0, PV), a("regs_s", 0, PV), 0.0, OP.max)
+            act(a("P", PV, 4096), a("regs_s", PV, 4096), ACT.Relu)
+        for u in (1, 0):
             lo, hi = 128 * u, 128 * u + 128
-            act(a("old", lo, hi), via(a("regs_s", 0, 4096), a("L2_%d" % u, 0, 8)))
             tt(a("HV", lo, hi), via(a(zr), a("L2_%d" % u, 8, 16)), a("old", lo, hi), OP.add)
-            ts(a("HV", lo, hi), a("HV", lo, hi), 15.0, OP.min, -15.0, OP.max)
+            if t + 1 < RO:
+                ts(a("HP", lo, hi), a("HV", lo, hi), 15.0, OP.min, 0.0, OP.max)
+        if t + 1 < RO:
+            change("h", list(range(7, -1, -1)), "HP", "P")
+        for u in (1, 0):
+            ts(a("HV", 128 * u, 128 * u + 128), a("HV", 128 * u, 128 * u + 128), 15.0, OP.min, -15.0, OP.max)
         change("h", list(range(7, -1, -1)), "HV")
     put("Y", lambda: g.sync.dma_start(T.yr[:], T.regs_s[:, 0:4096]).then_inc(T.sem.yo, 16), [("regs_s", 0, 4128)], [], 100.0, ("yo", 16), 8000.0)
 
@@ -504,7 +521,7 @@ def rank_program(g, core, T, topo):
                 for j, l2, h2, w2 in seen.get(name, []):
                     if l2 < hi and lo < h2 and (w or w2) and j != i:
                         same = ops[j]["e"] == o["e"] and (not w2 or (w and o["e"] == "P"))
-                        pred[j] = max(pred.get(j, -1e9), -ops[j]["late"] if name[:4] == "turn" else 0.0 if same else WAKE)
+                        pred[j] = max(pred.get(j, -1e9), -ops[j]["late"] if name[:4] == "turn" else 0.0 if same else SELF if ops[j]["e"] == o["e"] else WAKE)
         for regs, w in ((o["r"], False), (o["w"], True)):
             for name, lo, hi in regs:
                 seen[name] = [x for x in seen.get(name, []) if not (w and lo <= x[1] and x[2] <= hi)] + [(i, lo, hi, w)]
@@ -548,7 +565,7 @@ def rank_program(g, core, T, topo):
             return max(ops[j]["end"] for j in o["after"])
         t = free[o["e"]]
         for s, v in needs(o["e"], o["r"], o["w"]).items():
-            t = max(t, when[(s, v)] + WAKE)
+            t = max(t, when[(s, v)] + (SELF if s == "e" + o["e"] else WAKE))
         return t
 
     def issue(o, t):
@@ -581,12 +598,26 @@ def rank_program(g, core, T, topo):
                 keep = [x for x in acc.get(name, []) if not (lo <= x[2] and x[3] <= hi and (w or (x[0] == who and not x[4])))]
                 acc[name] = keep + [(who, tok, lo, hi, w)]
 
+    def rank(j):
+        return ops[j]["way"] - FILL.get(ops[j]["e"], 0.0) * ops[j]["fill"]
+
     ready = [i for i, o in enumerate(ops) if not o["left"]]
     while ready:
         at = {i: start(ops[i]) for i in ready}
-        i = min(ready, key=lambda j: (at[j] + min(LOOK, ops[j]["d"]), -ops[j]["way"]))
-        soon = [j for j in ready if ops[j]["e"] == ops[i]["e"] and at[j] <= at[i] + min(LOOK, ops[i]["d"])]
-        i = max(soon, key=lambda j: ops[j]["way"] - FILL.get(ops[j]["e"], 0.0) * ops[j]["fill"])
+        near, edge = dict(at), ready
+        for _ in range(DEPTH):
+            nxt = []
+            for i in edge:
+                for j in ops[i]["succ"]:
+                    if j not in near and all(k in near or "end" in ops[k] for k in ops[j]["pred"]):
+                        near[j] = max([free[ops[j]["e"]]] + [(ops[k]["end"] if "end" in ops[k] else near[k] + ops[k]["d"] + ops[k]["late"]) + w
+                                                             for k, w in ops[j]["pred"].items()])
+                        nxt.append(j)
+            edge = nxt
+        order = sorted(ready, key=lambda j: (at[j], -rank(j)))
+        free_to_go = [i for i in order if not any(
+            ops[j]["e"] == ops[i]["e"] and rank(j) > rank(i) and near[j] - at[i] <= HOLD.get(ops[i]["e"], 0.0) * (10.0 if rank(j) > rank(i) + FAR else 1.0) * (at[i] + ops[i]["d"] - near[j]) for j in near)]
+        i = (free_to_go + order)[0]
         issue(ops[i], at[i])
         ready.remove(i)
         for j in ops[i]["succ"]:

@@ -6,14 +6,10 @@ RO = 3
 REG = 320
 EPS = 2.0 ** -30
 BETA = 2.0 ** -12
-CG, CS = 32, 32
-MG = 4
-SELF, FAR = 40.0, 6000.0
-FILL = {"V": 2000.0, "P": 500.0, "S": 2000.0}
-HOLD = {"V": 1.0, "S": 5.0, "P": 5.0, "G": 5.0}
-DEPTH = 3
+MG = 2
+PASSES = 4
 PCY = 0.45
-BYS = (1, 3, 4, 5, 6)
+BYS = (1, 3, 5, 6, 7)
 LAND = (2000.0, 2200.0, 6000.0, 2400.0, 7800.0, 9600.0, 11500.0)
 BANKS = ["b%d" % b for b in range(8)]
 PV = 2736
@@ -31,32 +27,35 @@ def _scratch():
             lo = s[big][1][1] if big in s else 0
             s[big] = ("sbuf", [128, lo + cols + -cols % 32], d)
             at[name] = (big, lo, cols)
-    sb("acts_i", 2048, I); sb("regs_s", 4128, B); sb("P", 4128, B); sb("pay_s", 2048, B); sb("paym", 2048, B)
+    sb("acts_i", 2048, I); sb("regs_s", 4384, B); sb("P", 4384, B); sb("who", 4128, B); sb("pay_s", 2048, B); sb("paym", 2048, B)
     sb("rch_s", 256, B); sb("n0_i", 16, I); sb("dr_i", 256, I); sb("w_i", 256, I)
     sb("drb", 256, B); sb("wb", 256, B); sb("n0f", 16, F); sb("n0u", 16, U); sb("q0", 256, H); sb("TD1", 256, H)
     sb("xr1", 4096, B); sb("xr", 4096, B); sb("W", 4096, B)
     for e in (1, 2, 3, 4):
         sb("A%d" % e, 256, U); sb("Ah%d" % e, 256, H)
         for u in (0, 1):
-            sb("q%d_%d" % (e, u), 384, H); sb("L%d_%d" % (e, u), 16, U)
+            if e != 2:
+                sb("q%d_%d" % (e, u), 256, H); sb("L%d_%d" % (e, u), 16, U)
+    sb("q2", 768, H); sb("L2", 32, U)
     for u in (0, 1):
         sb("TA%d" % u, 256, F); sb("nF%d" % u, 16, U); sb("vbF%d" % u, 256, F); sb("wtF%d" % u, 256, B)
-    for n in ("y1", "y2", "y3", "y4", "y5", "yF", "lv", "zN", "NV", "old", "HV", "HP", "ms", "fl", "aux1", "auxB", "ng"):
+    for n in ("y1", "y2", "y3", "y4", "y5", "yF", "lv", "zN", "NV", "zl", "HV", "HP", "NP", "ms", "fl", "aux1", "auxB", "ng"):
         sb(n, 256, B)
+    sb("o32", 16, F); sb("offw", 16, U); sb("own", 16, F); sb("ID32", 128, F); sb("lid", 256, B); sb("lost", 256, B)
     sb("t1", 256, F); sb("ind", 256, H); sb("cum", 256, F)
     for t in range(RO):
         sb("vb%d" % t, 512, F); sb("wt%d" % t, 512, B); sb("auxS%d" % t, 256, B); sb("land%d" % t, 512, B); sb("zr%d" % t, 1280, B)
         sb("send%d" % t, 1280, B)
     for n in ("h", "f"):
-        sb("rf8" + n, 16, F); sb("Y" + n, 512, F); sb("eq" + n, 512, B); sb("lc" + n, 512, B); sb("u" + n, 16, F); sb("off" + n, 16, U)
+        sb("D" + n, 384, F); sb("Y" + n, 384, F); sb("eq" + n, 384, B); sb("lc" + n, 384, F); sb("off" + n, 16, U); sb("CM" + n, 48, B)
     sb("Dm", 128, I); sb("Bm", 128, I); sb("pi", 2, I); sb("pk", 2, I); sb("rp", 256, I); sb("li", 64, I)
-    sb("crep", 64, U); sb("crep2", 32, U); sb("kf", 1, F); sb("pg", 1, F)
+    sb("crep", 64, U); sb("crep2", 24, U); sb("kf", 1, F); sb("pg", 1, F)
     for n in ("BO", "ID", "E1", "E2", "E3", "OHM", "DST", "TRI", "ZM", "I5", "In", "BO13", "N13", "D5", "Dn", "R13", "RN13", "M23", "DIF"):
         sb(n, 128, B)
-    sb("Z", 144, B); sb("ZN", 144, B); sb("CST", 512, B); sb("LC", 32, H)
+    sb("Z", 144, B); sb("ZN", 144, B); sb("CST", 512, B); sb("LC", 40, H)
     sb("cols", 24, F); sb("SR", 640, B); sb("SEL", 768, B); sb("ZT", 864, B)
-    sb("rd", 256, F); sb("ta", 256, F); sb("tb", 256, F); sb("CMh", 512, B); sb("CMf", 512, B); sb("MX", 256, B)
-    sb("RST", 512, B); sb("ONE", 256, B); sb("SIX", 256, B)
+    sb("rd", 256, F); sb("ta", 16, F); sb("tb", 16, F); sb("MX", 256, B)
+    sb("ONE", 256, B); sb("SIX", 256, B)
     for b in range(8):
         s["b%d" % b] = ("psum", [128, 512], F)
     return s, at
@@ -73,7 +72,7 @@ def rank_program(g, core, T, topo):
         return
     OP, ACT = AluOpType, ActivationFunctionType
     queue = {"V": g.vector, "P": g.tensor, "S": g.scalar, "G": g, "Y": g.sync}
-    CY, WAKE, GA, SC = 0.83, 110.0, 1.56, 3.8
+    CY, WAKE, GA, SC = 0.83, 120.0, 1.56, 3.8
     ops = []
 
     def a(name, lo=None, hi=None, step=1, rows=128):
@@ -131,8 +130,8 @@ def rank_program(g, core, T, topo):
     def fill(out, c):
         vop(lambda: g.vector.memset(out[0], c), out, [], out[2], 0.5)
 
-    def scan(out, d0, d1, init):
-        vop(lambda: g.vector.tensor_tensor_scan(out[0], d0[0], d1[0], val(init), OP.mult, OP.add), out,
+    def scan(out, d0, d1, init, op0=OP.mult, op1=OP.add):
+        vop(lambda: g.vector.tensor_tensor_scan(out[0], d0[0], d1[0], val(init), op0, op1), out,
             [d0, d1] + [x for x in (init,) if isinstance(x, tuple)], d1[2], 0.5 if narrow(out) and narrow(d1) else 1.0)
 
     def act(out, in_, func=None, bias=0.0, scale=1.0):
@@ -166,13 +165,18 @@ def rank_program(g, core, T, topo):
     def load(eng, sem, out, src, reg, late):
         put(eng, lambda: queue[eng].dma_start(out, src).then_inc(T.sem[sem], 16), [], reg + [("turn" + eng, 0, 1)], 100.0, (sem, 16), late)
 
-    def send(r, src, dst, sem, lsem, also=()):
-        rid, pid, _ = topo.addr(T.cores[r])
-        m = sum(1 << x for x in topo.engines(core, T.cores[r])[:8])
-        return put("G", lambda: g.remote_dma(dst, src[0], T.sem[sem], T.sem[lsem], pid, rid, m), regs_of(src) + list(also), [], 500.0, (lsem, 8), 2800.0)
+    def send(to, sem, lsem, also=()):
+        trs = []
+        for k, (r, src, dst) in enumerate(to):
+            rid, pid, _ = topo.addr(T.cores[r])
+            eng = topo.engines(core, T.cores[r])[:8]
+            n = len(eng) // len(to)
+            trs.append(RemoteDMATransfer(dst_ids=[DstId(rid=rid, pnc=pid)], dma_engine_mask=sum(1 << x for x in eng[n * k:n * k + n]),
+                                         remote_sem=T.sem[sem], src=src[0], dst=dst))
+        return put("G", lambda: g.remote_dma_fused(trs, local_sem=T.sem[lsem]), regs_of(*[x[1] for x in to]) + list(also), [], 500.0, (lsem, 8), 2500.0)
 
-    def arrives(sem, region, like):
-        put("R", None, [], region[1], 0.0, (sem, 8), 0.0, [like])
+    def arrives(sem, region, like, n):
+        put("R", None, [], region[1], 0.0, (sem, n), 0.0, [like])
 
     def places(q):
         def far_key(r):
@@ -180,7 +184,8 @@ def rank_program(g, core, T, topo):
             return 0 if topo.mates(c1, c2) else 1 if topo.same_plane(c1, c2) else 2
         return [q] + sorted([r for r in range(N) if r != q], key=far_key)
     place = places(me)
-    others = place[1:]
+    assert all(places(r).index(me) == p for p, r in enumerate(place))
+    CALLS = ((1,), (2, 3))
 
     load("Y", "ld0", T.n0_i[:], T.n0[:], [("n0_i", 0, 16)], LAND[0])
     load("S", "ld1", T.rch_s[:], T.rch[:], [("rch_s", 0, 256)], LAND[1])
@@ -282,20 +287,25 @@ def rank_program(g, core, T, topo):
         ts(a("SR", 128 * j, 128 * j + 128), a("BO"), col(9 + j), OP.mult)
     ts(a("ZM"), a("ID"), 16.0, OP.mult)
     tt(a("ZM"), a("ZM"), a("BO"), OP.subtract)
-    ts(a("ta"), a("rd"), 0.0, OP.is_gt, 16384.0, OP.mult)
-    ts(a("tb"), a("rd"), 0.0, OP.is_equal, -8192.0, OP.mult)
+    ts(a("ta"), a("rd", 0, 16), 0.0, OP.is_gt, 16384.0, OP.mult)
+    ts(a("tb"), a("rd", 0, 16), 0.0, OP.is_equal, -8192.0, OP.mult)
     tt(a("ta"), a("ta"), a("tb"), OP.add)
-    ts(a("CMh", 0, 256), a("ta"), 2048.0, OP.add)
-    fill(a("CMh", 256, 512), 2048.0)
-    ts(a("CMf"), a("CMh"), 8192.0, OP.add)
-    for h in (0, 1):
-        ts(a("RST", 256 * h, 256 * h + 256), a("rp"), 0, OP.is_gt)
-    cp(a("crep2", 0, 16), a("li", 0, 16))
-    ts(a("crep2", 16, 32), a("li", 0, 16), 1.0, OP.add, 15.0, OP.min)
+    for n, c in (("h", 2048.0), ("f", 10240.0)):
+        fill(a("CM" + n, 16, 32), c)
+        ts(a("CM" + n, 0, 16), a("ta"), c, OP.add)
+        ts(a("CM" + n, 32, 48), a("ta"), c, OP.add)
+        fill(a("D" + n), 0.0)
+        fill(a("D" + n, 0, 384, 48), -4.0)
+        fill(a("D" + n, 16, 384, 48), -4.0)
+    for j, c in enumerate((15.0, 47.0, 47.0)):
+        ts(a("crep2", j, 24, 3), a("li", 0, 8), 48.0, OP.mult, c, OP.add)
+    put("G", lambda: g.iota(a("lid")[0], [[1, 256]], 1, 0, allow_small_or_imprecise_dtypes=True), [], a("lid")[1], 560.0)
+    ts(a("ID32"), a("ID"), 2.0 ** -9, OP.mult)
+    ts(a("own"), a("li", 0, 16), 16.0, OP.mult, col(21), OP.add)
+    ts(a("own"), a("own"), 16.0, OP.add, 2.0 ** -9, OP.mult)
     act(a("paym"), a("pay_s"), ACT.Identity, bias=-1.0)
-    for t in range(RO):
-        zeros(a("send%d" % t))
-        zeros(a("zr%d" % t))
+    zeros(a("send0"))
+    zeros(a("zr0"))
     for j in range(2, 6):
         sel(a("SEL", 128 * j, 128 * j + 128, rows=96), a("ONE", 0, 128, rows=96), [[-12, 8], [0, 16]], -home_te[j], 1)
 
@@ -327,23 +337,27 @@ def rank_program(g, core, T, topo):
         ah = a("Ah%d" % e, lo, hi)
         ts(ah, a("A%d" % e, lo, hi), -2048.0, OP.add)
         odd = e % 2
+        c = 256 if (e, u) == (2, 1) else 128
         mm((a(y, 0, 128), a("I5"), ah), *[(a(y, c0, c1), a(m), x) for c0, c1, m, _, x in node_terms])
         act(a("fl", lo, hi), a(y, 0, 128), ACT.Identity, bias=129.0 + (10240.0 + e - 1023.5) / 2048.0, scale=2.0 ** -11)
-        mm((a(y, 128, 256), a("D5" if odd else "I5"), ah), *([(a(y, 128 + c0, 128 + c1), a(m2 if odd else m), x) for c0, c1, m, m2, x in node_terms]
-           + [(a(y, 128, 256), a("CST", 128 * e - 128, 128 * e, rows=64), a("ONE", 0, 128, rows=64)),
-              (a(y, 128, 256), a("Dn" if odd else "In"), a("fl", lo, hi))]))
+        mm((a(y, c, c + 128), a("D5" if odd else "I5"), ah), *([(a(y, c + c0, c + c1), a(m2 if odd else m), x) for c0, c1, m, m2, x in node_terms]
+           + [(a(y, c, c + 128), a("CST", 128 * e - 128, 128 * e, rows=64), a("ONE", 0, 128, rows=64)),
+              (a(y, c, c + 128), a("Dn" if odd else "In"), a("fl", lo, hi))]))
         if not odd:
-            mm((a(y, 256, 384), a("ID"), ah))
+            mm((a(y, 384 - c, 512 - c), a("ID"), ah))
             act(a("TA%d" % u), a(y, 128, 384))
 
+    def pieces(lo, n):
+        return [x for l in range(lo, lo + n, 32) for x in (((l, 16), (l + 16, 16)) if l % 128 == 0 else ((l, 32),))]
+
     def spread(win, lo, n):
-        for l in range(0, n, CS):
+        for l, c in pieces(lo, n):
             name, w0, _ = win[1][0]
-            act(a("xr", 16 * (lo + l), 16 * (lo + l + CS)), via(a(name, w0 + l, w0 + l + CS), a("crep", 0, CS)), ACT.Identity, bias=1.0)
+            act(a("xr", 16 * l, 16 * (l + c)), via(a(name, w0 + l - lo, w0 + l - lo + c), a("crep", 0, c)), ACT.Identity, bias=1.0)
             stream()
 
     def weights(e, u, l0):
-        for j in range(l0, l0 + 64, CG):
+        for j, CG in (pieces(l0, 64) if e > 1 else ((l0, 32), (l0 + 32, 32))):
             w, x, p = a("W", 16 * j, 16 * (j + CG)), a("xr1" if e == 1 else "xr", 16 * j, 16 * (j + CG)), via(a("P", 0, 4096), a("A%d" % e, j, j + CG))
             if e == 1 and j // CG in BYS:
                 b = a("b%d" % (6 + BYS.index(j // CG) % 2))
@@ -386,35 +400,49 @@ def rank_program(g, core, T, topo):
             mm((a(z, 128, 256), a("DST"), ind))
         mm((a(x, 128, 256), a("OHM"), ind))
         mm((a(x, 256, 384), a("OHM"), ind))
-        if e == 2:
+        if e == 4:
+            tt(a(q), a(x, 128, 384), a("TA%d" % u), OP.mult)
+            lists(a(z, 0, 16), (q, 0), 256)
+            ts(a(L), a(z, 0, 16), 2048.0, OP.add)
+            c, rec = 8, a(L, 8, 16)
+        else:
+            nodes = a("q2", 640 * u, 640 * u + 128)
             scan(a("cum", lo, hi), a("ONE", lo, hi), a(z, 128, 256), col(4) if u == 0 else a("cum", lo - 1, lo))
-            tt(a(q, 256, 384), a(z, 128, 256), a("cum", lo, hi), OP.mult)
-        tt(a(q, 0, 256), a(x, 128, 384), a("TA%d" % u), OP.mult)
-        if e == 2:
-            mm((a(y, 0, 128), a("ID"), a("auxS%d" % t, lo, hi)), (a(y, 0, 128), a("Z", 13, 141), a(q, 0, 128)))
+            tt(a("q2", 256 + lo, 256 + hi), a(z, 128, 256), a("cum", lo, hi), OP.mult)
+            tt(a("q2", 512 * u, 512 * u + 256), a(x, 128, 384), a("TA%d" % u), OP.mult)
+            mm((a(y, 0, 128), a("ID"), a("auxS%d" % t, lo, hi)), (a(y, 0, 128), a("Z", 13, 141), nodes))
             act(a("aux1", lo, hi), a(y, 0, 128))
-        lists(a(z, 0, 16), (q, 128 if e == 2 else 0), 256, [(a(z, 0, 16), a("ID"), a("LC", 16, 32))] if e == 2 else [])
-        ts(a(L), a(z, 0, 16), 2048.0, OP.add)
-        c = 0 if e == 2 else 8
-        act(a("rf8" + "hf"[e // 4], 8 * u, 8 * u + 8), a(z, c, c + 8), ACT.Identity, bias=0.25, scale=2.0 ** -13)
-        tt(yout, via(a("P", 0, 4096), a(L, c, c + 8)), yin, OP.min)
+            lists(a(z, 0, 16), ("q2", 128 + 256 * u), 256, [(a(z, 0, 16), a("ID"), a("LC", 16 + 8 * u, 32 + 8 * u))])
+            ts(a("L2", 16 * u, 16 * u + 16), a(z, 0, 16), 2048.0, OP.add)
+            c, rec = 8 * u, a("L2", 24 * u, 24 * u + 8)
+        for j in (0, 1):
+            act(a("D" + "hf"[e // 4], 192 * u + 15 + 32 * j, 192 * u + 192, 48), a(z, c + j, c + 8, 2), ACT.Identity, bias=0.25, scale=2.0 ** -13)
+        tt(yout, via(a("P", 0, 4096), rec), yin, OP.min)
         if e == 2:
-            mm((a(y, 128, 256), a("M23"), a("aux1", lo, hi)), (a(y, 128, 256), a("Z", 12, 140), a(q, 0, 128)))
+            mm((a(y, 128, 256), a("M23"), a("aux1", lo, hi)), (a(y, 128, 256), a("Z", 12, 140), nodes))
             act(a("auxB", lo, hi), a(y, 128, 256))
 
-    def first_of(n, e, cm, extra):
+    def first_of(n, e, cm, dead, src):
         b = "b7" if n == "h" else "b6"
-        for h in (0, 256):
-            mm((a(b, h, h + 256), a("ID"), a(cm, h, h + 256)),
-               *([(a(b, h + 128 * u, h + 128 * u + 128), a("BO"), a("q%d_%d" % (e, u), 128, 256)) for u in (0, 1)]
-                 + [(a(b, h + c0, h + c1), m, x) for c0, c1, m, x in extra]))
-        act(a("Y" + n), via(a("rf8" + n), a("crep2")), scale=8192.0)
-        tt(a("eq" + n), a(b), a("Y" + n), OP.is_equal)
-        scan(a("lc" + n), a("RST"), a("eq" + n), 0.0)
-        tt(a("u" + n), a("lc" + n, 15, 256, 16), a("rf8" + n), OP.add)
-        tt(a("u" + n, 1, 16, 2), a("u" + n, 1, 16, 2), a("lc" + n, 271, 512, 32), OP.add)
-        ts(a("off" + n, 0, 16, 2), a("u" + n, 0, 16, 2), 8192.0, OP.mult, col(6), OP.min)
-        ts(a("off" + n, 1, 16, 2), a("u" + n, 1, 16, 2), 8192.0, OP.mult, col(21), OP.min)
+        for j in range(8):
+            q, c = ("q2", 128 + 384 * (j // 4) + 32 * (j % 4)) if e == 2 else ("q4_%d" % (j // 4), 128 + 32 * (j % 4))
+            mm((a(b, 48 * j, 48 * j + 48), a("ID"), a(cm)),
+               (a(b, 48 * j, 48 * j + 16), a("BO"), a(q, c, c + 16)), (a(b, 48 * j + 16, 48 * j + 48), a("BO"), a(q, c, c + 32)),
+               (a(b, 48 * j, 48 * j + 16), dead, src(32 * j, 16)), (a(b, 48 * j + 16, 48 * j + 48), dead, src(32 * j, 32)))
+        act(a("Y" + n), via(a("D" + n), a("crep2")), scale=8192.0)
+        tt(a("eq" + n), a(b, 0, 384), a("Y" + n), OP.is_equal)
+        scan(a("lc" + n), a("D" + n), a("eq" + n), 0.0, OP.add, OP.max)
+        off = "offf" if n == "f" else "o32"
+        ts(a(off, 0, 16, 2), a("lc" + n, 15, 384, 48), 8192.0, OP.mult, col(6), OP.min)
+        ts(a(off, 1, 16, 2), a("lc" + n, 47, 384, 48), 8192.0, OP.mult, col(21), OP.min)
+
+    def first_of_all():
+        cp(a("offw"), a("o32"))
+        change("w", list(range(7, -1, -1)), "lid", "who")
+        tt(a("lost"), via(a("who"), a("offw")), a("lid"), OP.not_equal)
+        lists(a("b7", 0, 16), ("lost", 0), 256, [(a("b7", 0, 16), a("ID32"), a("o32"))])
+        tt(a("o32"), a("b7", 0, 16), a("own"), OP.min)
+        ts(a("offh"), a("o32"), 512.0, OP.mult)
 
     def change(n, blocks, values, table="regs_s"):
         for c in blocks:
@@ -440,16 +468,20 @@ def rank_program(g, core, T, topo):
                 choose(e, t, u)
         land, zr, out = "land%d" % t, "zr%d" % t, "send%d" % t
         for u in (0, 1):
-            scatter(a(out, 0, 1216), a("L2_%d" % u, 8, 16), a("auxB", 128 * u, 128 * u + 128))
-        for u in (0, 1):
-            scatter(a(out, 64, 1280), a("L2_%d" % u, 8, 16), a("y3", 128 * u, 128 * u + 128))
-        for p, r in enumerate(others):
-            s = 128 * places(r).index(me)
-            o = send(r, a(out, REG * r, REG * r + 128), T[land][:, s:s + 128], "a%d_%d" % (t, me), "la%d_%d" % (t, r), [(zr, 0, 1280)])
-            arrives("a%d_%d" % (t, r), a(land, 128 * p + 128, 128 * p + 256), o)
-        for u in (0, 1):
-            ts(a("ng", 128 * u, 128 * u + 128), a("q2_%d" % u, 256, 384), col(5), OP.is_ge, 8192.0, OP.mult)
-        first_of("h", 2, "CMh", [(0, 256, a("BO"), a("ng"))])
+            scatter(a(out, 0, 1216), a("L2", 8 + 8 * u, 16 + 8 * u), a("auxB", 128 * u, 128 * u + 128))
+        scatter(a(out, 64, 1280), a("L2", 8, 24), a("y3"))
+        for ps in CALLS:
+            o = send([(place[p], a(out, REG * place[p], REG * place[p] + 128), T[land][:, 128 * p:128 * p + 128]) for p in ps],
+                     "a%d_%d" % (t, me), "la%d_%d" % (t, ps[0]), [(zr, 0, 1280)])
+            for p in ps:
+                arrives("a%d_%d" % (t, place[p]), a(land, 128 * p, 128 * p + 128), o, 8 // len(ps))
+        fills = [a("who", 1032 * j, 1032 * j + 1032) for j in range(4)] * (t == 0)
+        for x in fills + ([a("send%d" % (t + 1)), a("zr%d" % (t + 1))] if t + 1 < RO else []):
+            zeros(x)
+            ops[-1]["after"].append(o)
+            ops[-1]["soon"] = 1
+        ts(a("ng"), a("q2", 256, 512), col(5), OP.is_ge, 8192.0, OP.mult)
+        first_of("h", 2, "CMh", a("BO"), lambda l, n: a("ng", l, l + n))
 
         def aux(p, lo=0, hi=64):
             name, s = (out, REG * me) if p == 0 else (land, 128 * p)
@@ -485,43 +517,41 @@ def rank_program(g, core, T, topo):
             tt(a("lv", lo, hi), via(a("paym"), a(L, 0, 8)), a("y5", lo, hi), OP.min)
             mm((a(x, 0, 128), a("ZM"), a("lv", lo, hi)))
             act(a("zN", lo, hi), a(x, 0, 128), ACT.Sign, scale=-1.0)
-            for p in (2 * u, 2 * u + 1):
-                r = place[p]
-                if p:
-                    o = send(r, a("zN", 64 * p, 64 * p + 64), T[zr][:, REG * me:REG * me + 64], "z%d_%d" % (t, me), "lz%d_%d" % (t, r))
-                    arrives("z%d_%d" % (t, r), a(zr, REG * r, REG * r + 64), o)
-                else:
-                    act(a(zr, REG * me, REG * me + 64), a("zN", 0, 64))
+            ps = CALLS[u]
+            o = send([(place[p], a("zN", 64 * p, 64 * p + 64), T[zr][:, REG * me:REG * me + 64]) for p in ps], "z%d_%d" % (t, me), "lz%d_%d" % (t, ps[0]))
+            for p in ps:
+                arrives("z%d_%d" % (t, place[p]), a(zr, REG * place[p], REG * place[p] + 64), o, 8 // len(ps))
+            if u == 0:
+                act(a(zr, REG * me, REG * me + 64), a("zN", 0, 64))
             tt(a("NV", lo, hi), via(a("regs_s", 0, 4096), a(L, 8, 16)), a("zN", lo, hi), OP.subtract)
-            ts(a("NV", lo, hi), a("NV", lo, hi), 15.0, OP.min, -15.0, OP.max)
-        first_of("f", 4, "CMf", [(64 * p, 64 * p + 64, a("SR", 512, 640), aux(p)) for p in range(4)])
-        change("f", [2 * place.index(r) + c for r in (3, 2, 1, 0) for c in (1, 0)], "NV")
-        for u in (1, 0):
-            act(a("old", 128 * u, 128 * u + 128), via(a("regs_s", 0, 4096), a("L2_%d" % u, 0, 8)))
+        first_of("f", 4, "CMf", a("SR", 512, 640), lambda l, n: aux(l // 64, l % 64, l % 64 + n))
         if t + 1 < RO:
-            ts(a("P", 0, PV), a("regs_s", 0, PV), 0.0, OP.max)
-            act(a("P", PV, 4096), a("regs_s", PV, 4096), ACT.Relu)
-        for u in (1, 0):
-            lo, hi = 128 * u, 128 * u + 128
-            tt(a("HV", lo, hi), via(a(zr), a("L2_%d" % u, 8, 16)), a("old", lo, hi), OP.add)
-            if t + 1 < RO:
-                ts(a("HP", lo, hi), a("HV", lo, hi), 15.0, OP.min, 0.0, OP.max)
+            ts(a("NP"), a("NV"), 15.0, OP.min, 0.0, OP.max)
+        ts(a("NV"), a("NV"), 15.0, OP.min, -15.0, OP.max)
+        first_of_all()
+        blocks = [2 * place.index(r) + c for r in (3, 2, 1, 0) for c in (1, 0)]
+        change("f", blocks, "NV")
         if t + 1 < RO:
-            change("h", list(range(7, -1, -1)), "HP", "P")
+            change("f", blocks, "NP", "P")
+        act(a("zl"), via(a(zr), a("L2", 8, 24)))
         for u in (1, 0):
-            ts(a("HV", 128 * u, 128 * u + 128), a("HV", 128 * u, 128 * u + 128), 15.0, OP.min, -15.0, OP.max)
-        change("h", list(range(7, -1, -1)), "HV")
-    put("Y", lambda: g.sync.dma_start(T.yr[:], T.regs_s[:, 0:4096]).then_inc(T.sem.yo, 16), [("regs_s", 0, 4128)], [], 100.0, ("yo", 16), 8000.0)
+            tt(a("HV", 128 * u, 128 * u + 128), via(a("regs_s", 0, 4096), a("L2", 24 * u, 24 * u + 8)), a("zl", 128 * u, 128 * u + 128), OP.add)
+        if t + 1 < RO:
+            ts(a("HP"), a("HV"), 15.0, OP.min, 0.0, OP.max)
+            scatter(a("P"), a("offh"), a("HP"))
+        ts(a("HV"), a("HV"), 15.0, OP.min, -15.0, OP.max)
+        scatter(a("regs_s"), a("offh"), a("HV"))
+    put("Y", lambda: g.sync.dma_start(T.yr[:], T.regs_s[:, 0:4096]).then_inc(T.sem.yo, 16), [("regs_s", 0, 4384)], [], 100.0, ("yo", 16), 8000.0)
 
     seen = {}
     for i, o in enumerate(ops):
-        pred = {j: WAKE for j in o["after"]}
+        pred = {j: -ops[j]["late"] if "soon" in o else WAKE for j in o["after"]}
         for regs, w in ((o["r"], False), (o["w"], True)):
             for name, lo, hi in regs:
                 for j, l2, h2, w2 in seen.get(name, []):
                     if l2 < hi and lo < h2 and (w or w2) and j != i:
                         same = ops[j]["e"] == o["e"] and (not w2 or (w and o["e"] == "P"))
-                        pred[j] = max(pred.get(j, -1e9), -ops[j]["late"] if name[:4] == "turn" else 0.0 if same else SELF if ops[j]["e"] == o["e"] else WAKE)
+                        pred[j] = max(pred.get(j, -1e9), -ops[j]["late"] if name[:4] == "turn" else 0.0 if same else WAKE)
         for regs, w in ((o["r"], False), (o["w"], True)):
             for name, lo, hi in regs:
                 seen[name] = [x for x in seen.get(name, []) if not (w and lo <= x[1] and x[2] <= hi)] + [(i, lo, hi, w)]
@@ -534,8 +564,7 @@ def rank_program(g, core, T, topo):
 
     count = {"eV": 0, "eP": 0, "eS": 0, "eG": 0}
     known = {e: {} for e in "VPSGYR"}
-    free = {e: 0.0 for e in "VPSGYR"}
-    snap, acc, when = {}, {}, {}
+    snap, acc = {}, {}
 
     def needs(eng, reads, writes):
         need = {}
@@ -560,15 +589,7 @@ def rank_program(g, core, T, topo):
                         need[tok[0]] = tok[1]
         return need
 
-    def start(o):
-        if o["e"] == "R":
-            return max(ops[j]["end"] for j in o["after"])
-        t = free[o["e"]]
-        for s, v in needs(o["e"], o["r"], o["w"]).items():
-            t = max(t, when[(s, v)] + (SELF if s == "e" + o["e"] else WAKE))
-        return t
-
-    def issue(o, t):
+    def issue(o):
         eng = o["e"]
         tok = o["tok"]
         if eng != "R":
@@ -581,7 +602,6 @@ def rank_program(g, core, T, topo):
                         known[eng][s3] = max(known[eng].get(s3, 0), v3)
                 else:
                     need[s] = 0
-            free[eng] = t + o["d"]
             for call in o["calls"]:
                 if tok:
                     call()
@@ -592,38 +612,57 @@ def rank_program(g, core, T, topo):
         tok = tok or ("e" + eng, count["e" + eng])
         snap[tok] = dict(known[eng])
         snap[tok][tok[0]] = tok[1]
-        o["end"] = when[tok] = t + o["d"] + o["late"]
         for regs, w in ((o["r"], False), (o["w"], True)):
             for name, lo, hi in regs:
                 keep = [x for x in acc.get(name, []) if not (lo <= x[2] and x[3] <= hi and (w or (x[0] == who and not x[4])))]
                 acc[name] = keep + [(who, tok, lo, hi, w)]
 
-    def rank(j):
-        return ops[j]["way"] - FILL.get(ops[j]["e"], 0.0) * ops[j]["fill"]
+    def cut(b, t):
+        lo, hi = 0, len(b)
+        while lo < hi:
+            m = (lo + hi) // 2
+            if b[m][0] <= t:
+                lo = m + 1
+            else:
+                hi = m
+        return lo
 
-    ready = [i for i, o in enumerate(ops) if not o["left"]]
-    while ready:
-        at = {i: start(ops[i]) for i in ready}
-        near, edge = dict(at), ready
-        for _ in range(DEPTH):
-            nxt = []
-            for i in edge:
-                for j in ops[i]["succ"]:
-                    if j not in near and all(k in near or "end" in ops[k] for k in ops[j]["pred"]):
-                        near[j] = max([free[ops[j]["e"]]] + [(ops[k]["end"] if "end" in ops[k] else near[k] + ops[k]["d"] + ops[k]["late"]) + w
-                                                             for k, w in ops[j]["pred"].items()])
-                        nxt.append(j)
-            edge = nxt
-        order = sorted(ready, key=lambda j: (at[j], -rank(j)))
-        free_to_go = [i for i in order if not any(
-            ops[j]["e"] == ops[i]["e"] and rank(j) > rank(i) and near[j] - at[i] <= HOLD.get(ops[i]["e"], 0.0) * (10.0 if rank(j) > rank(i) + FAR else 1.0) * (at[i] + ops[i]["d"] - near[j]) for j in near)]
-        i = (free_to_go + order)[0]
-        issue(ops[i], at[i])
-        ready.remove(i)
-        for j in ops[i]["succ"]:
-            ops[j]["left"] -= 1
-            if not ops[j]["left"]:
-                ready.append(j)
+    def lay(order, back):
+        at, busy = {}, {}
+        for i in order:
+            o = ops[i]
+            if back:
+                t = max([o["late"]] + [at[j] + ops[j]["d"] + ops[j]["pred"][i] + o["late"] for j in o["succ"]])
+            else:
+                t = max([0.0] + [at[j] + ops[j]["d"] + ops[j]["late"] + w for j, w in o["pred"].items()])
+            use = [] if o["e"] == "R" else [o["e"]] + sorted(set(r[0] for r in o["r"] + o["w"] if r[0] in BANKS))
+            moved = True
+            while moved:
+                moved = False
+                for r in use:
+                    b = busy.setdefault(r, [])
+                    for t0, t1, e in b[max(0, cut(b, t) - 2):]:
+                        pad = WAKE if e != o["e"] else 0.0
+                        if t0 - pad >= t + o["d"]:
+                            break
+                        if t1 + pad > t:
+                            t, moved = t1 + pad, True
+            for r in use:
+                busy[r].insert(cut(busy[r], t), (t, t + o["d"], o["e"]))
+            at[i] = t
+        return at
+
+    order = sorted(range(len(ops)), key=lambda i: (-ops[i]["way"], i))
+    best = None
+    for _ in range(PASSES):
+        at = lay(order, False)
+        end = max(at[i] + o["d"] + o["late"] for i, o in enumerate(ops))
+        if best is None or end < best[0]:
+            best = (end, at)
+        ta = lay(sorted(at, key=lambda i: (-at[i] - ops[i]["d"], -i)), True)
+        order = sorted(ta, key=lambda i: (-ta[i] - ops[i]["d"], i))
+    for i in sorted(best[1], key=lambda i: (best[1][i], i)):
+        issue(ops[i])
 
     g.sync.wait_ge(T.sem.yo, 16)
     for s in ("eV", "eP", "eS", "eG"):
@@ -631,6 +670,8 @@ def rank_program(g, core, T, topo):
     for i in range(7):
         g.sync.wait_ge(T.sem["ld%d" % i], 16)
     for t in range(RO):
-        for r in others:
-            for k in ("a", "z", "la", "lz"):
-                g.sync.wait_ge(T.sem["%s%d_%d" % (k, t, r)], 8)
+        for ps in CALLS:
+            for k in "az":
+                g.sync.wait_ge(T.sem["l%s%d_%d" % (k, t, ps[0])], 8)
+                for p in ps:
+                    g.sync.wait_ge(T.sem["%s%d_%d" % (k, t, place[p])], 8 // len(ps))

@@ -6,13 +6,14 @@ RO = 3
 REG = 320
 EPS = 2.0 ** -30
 BETA = 2.0 ** -12
+BYS = (2, 3, 5, 6, 7)
 MG = 2
-PASSES = 4
-PCY = 0.45
-BYS = (1, 3, 5, 6, 7)
-LAND = (2000.0, 2200.0, 6000.0, 2400.0, 7800.0, 9600.0, 11500.0)
 BANKS = ["b%d" % b for b in range(8)]
-PV = 2736
+CY, PCY, WAKE, GA, SC = 0.83, 0.45, 120.0, 1.56, 3.8
+FIRST, LATE = 2500.0, 2500.0
+LAND = (2000.0, 2200.0, 2400.0, 6000.0, 7800.0, 9150.0, 9500.0, 11500.0)
+PASSES, TRIES, AGAIN = 4, 1500, 300
+PLAN = {}
 
 F, B, H, I, U = "float32", "bfloat16", "float16", "int32", "uint16"
 
@@ -29,7 +30,7 @@ def _scratch():
             at[name] = (big, lo, cols)
     sb("acts_i", 2048, I); sb("regs_s", 4384, B); sb("P", 4384, B); sb("who", 4128, B); sb("pay_s", 2048, B); sb("paym", 2048, B)
     sb("rch_s", 256, B); sb("n0_i", 16, I); sb("dr_i", 256, I); sb("w_i", 256, I)
-    sb("drb", 256, B); sb("wb", 256, B); sb("n0f", 16, F); sb("n0u", 16, U); sb("q0", 256, H); sb("TD1", 256, H)
+    sb("drb", 256, B); sb("wb", 512, B); sb("n0f", 16, F); sb("n0u", 16, U); sb("q0", 256, H); sb("TD1", 256, H)
     sb("xr1", 4096, B); sb("xr", 4096, B); sb("W", 4096, B)
     for e in (1, 2, 3, 4):
         sb("A%d" % e, 256, U); sb("Ah%d" % e, 256, H)
@@ -38,26 +39,24 @@ def _scratch():
                 sb("q%d_%d" % (e, u), 256, H); sb("L%d_%d" % (e, u), 16, U)
     sb("q2", 768, H); sb("L2", 32, U)
     for u in (0, 1):
-        sb("TA%d" % u, 256, F); sb("nF%d" % u, 16, U); sb("vbF%d" % u, 256, F); sb("wtF%d" % u, 256, B)
-    for n in ("y1", "y2", "y3", "y4", "y5", "yF", "lv", "zN", "NV", "zl", "HV", "HP", "NP", "ms", "fl", "aux1", "auxB", "ng"):
+        sb("TA%d" % u, 256, F); sb("nF%d" % u, 16, U); sb("vbF%d" % u, 256, F)
+    for n in ("y1", "y2", "y3", "y4", "y5", "yF", "lv", "zN", "NV", "NP", "zl", "HV", "HP", "ms", "fl", "aux1", "auxB", "ng", "lid", "found"):
         sb(n, 256, B)
-    sb("o32", 16, F); sb("offw", 16, U); sb("own", 16, F); sb("ID32", 128, F); sb("lid", 256, B); sb("lost", 256, B)
-    sb("t1", 256, F); sb("ind", 256, H); sb("cum", 256, F)
+    sb("t1", 256, F); sb("ind", 256, H); sb("cum", 256, F); sb("o32", 16, F); sb("offw", 16, U)
     for t in range(RO):
-        sb("vb%d" % t, 512, F); sb("wt%d" % t, 512, B); sb("auxS%d" % t, 256, B); sb("land%d" % t, 512, B); sb("zr%d" % t, 1280, B)
-        sb("send%d" % t, 1280, B)
+        sb("vb%d" % t, 512, F); sb("auxS%d" % t, 256, B); sb("land%d" % t, 512, B); sb("zr%d" % t, 1280, B); sb("send%d" % t, 1280, B)
     for n in ("h", "f"):
-        sb("D" + n, 384, F); sb("Y" + n, 384, F); sb("eq" + n, 384, B); sb("lc" + n, 384, F); sb("off" + n, 16, U); sb("CM" + n, 48, B)
+        sb("D" + n, 384, F); sb("Y" + n, 384, F); sb("eq" + n, 384, B); sb("lc" + n, 384, F); sb("off" + n, 16, U); sb("CM" + n, 384, B)
     sb("Dm", 128, I); sb("Bm", 128, I); sb("pi", 2, I); sb("pk", 2, I); sb("rp", 256, I); sb("li", 64, I)
     sb("crep", 64, U); sb("crep2", 24, U); sb("kf", 1, F); sb("pg", 1, F)
-    for n in ("BO", "ID", "E1", "E2", "E3", "OHM", "DST", "TRI", "ZM", "I5", "In", "BO13", "N13", "D5", "Dn", "R13", "RN13", "M23", "DIF"):
+    for n in ("BO", "ID", "E1", "E2", "E3", "OHM", "DST", "TRI", "ZM", "IDn", "I5", "In", "BO13", "N13", "D5", "Dn", "R13", "RN13", "M23", "DIF", "CW"):
         sb(n, 128, B)
-    sb("Z", 144, B); sb("ZN", 144, B); sb("CST", 512, B); sb("LC", 40, H)
-    sb("cols", 24, F); sb("SR", 640, B); sb("SEL", 768, B); sb("ZT", 864, B)
-    sb("rd", 256, F); sb("ta", 16, F); sb("tb", 16, F); sb("MX", 256, B)
-    sb("ONE", 256, B); sb("SIX", 256, B)
-    for b in range(8):
-        s["b%d" % b] = ("psum", [128, 512], F)
+    sb("Z", 144, B); sb("ZN", 144, B); sb("Zs", 144, B); sb("CST", 512, B); sb("LC", 40, H)
+    sb("own", 16, F); sb("ownl", 16, F); sb("ID32", 128, F)
+    sb("cols", 16, F); sb("SR", 640, B); sb("SEL", 768, B); sb("ZT", 864, B)
+    sb("rd", 256, F); sb("ta", 16, F); sb("tb", 16, F); sb("MX", 256, B); sb("ONE", 256, B); sb("SIX", 256, B)
+    for b in BANKS:
+        s[b] = ("psum", [128, 512], F)
     return s, at
 
 
@@ -72,16 +71,15 @@ def rank_program(g, core, T, topo):
         return
     OP, ACT = AluOpType, ActivationFunctionType
     queue = {"V": g.vector, "P": g.tensor, "S": g.scalar, "G": g, "Y": g.sync}
-    CY, WAKE, GA, SC = 0.83, 120.0, 1.56, 3.8
-    ops = []
+    ops, now, ends = [], [0], []
 
-    def a(name, lo=None, hi=None, step=1, rows=128):
+    def a(name, lo=None, hi=None, step=1, rows=128, row=0):
         name, base, cols = AT.get(name, (name, 0, 0))
         t = T[name]
         if lo is None:
             lo, hi = 0, cols or SCRATCH[name][1][1]
         lo, hi = base + lo, base + hi
-        ap = t[0:rows, lo:hi] if step == 1 else t[0:rows, lo:hi:step]
+        ap = t[row:row + rows, lo:hi] if step == 1 else t[row:row + rows, lo:hi:step]
         return ap, [(name, lo, hi)], (hi - lo + step - 1) // step, 0
 
     def via(win, off):
@@ -96,19 +94,14 @@ def rank_program(g, core, T, topo):
     def val(x):
         return x[0] if isinstance(x, tuple) else x
 
-    def put(eng, call, reads, writes, dur, tok=None, late=0.0, after=()):
-        ops.append({"e": eng, "calls": [call], "r": reads, "w": writes, "d": dur, "tok": tok, "late": late, "after": list(after), "fill": 0})
+    def put(eng, calls, reads, writes, dur, tok=None, late=0.0, after=()):
+        ops.append({"e": eng, "calls": calls, "r": reads, "w": writes, "d": dur, "tok": tok, "late": late, "after": dict(after), "round": now[0]})
         return len(ops) - 1
-
-    def stream():
-        if ops[-1]["e"] == "V":
-            ops[-1]["w"] = ops[-1]["w"] + [("turnV", 0, 1)]
-        ops[-1]["fill"] = 1
 
     def vop(call, out, ins, n, wide=1.0):
         x = [i for i in ins if i[3]]
         d = x[0][2] * GA * CY if x else out[2] * SC * CY if out[3] else max(64.0, n * wide) * CY
-        put("V", call, regs_of(*ins), out[1], 50.0 + d)
+        put("V", [call], regs_of(*ins), out[1], 50.0 + d)
 
     def ts(out, in0, s1, op0, s2=None, op1=None):
         if op1 is None:
@@ -118,7 +111,7 @@ def rank_program(g, core, T, topo):
         vop(f, out, [in0] + [x for x in (s1, s2) if isinstance(x, tuple)], in0[2], 0.5 if narrow(out) and narrow(in0) else 1.0)
 
     def tt(out, in0, in1, op):
-        ps = any(SCRATCH[x[1][0][0]][0] == "psum" for x in (in0, in1))
+        ps = any(x[1][0][0] in BANKS for x in (in0, in1))
         vop(lambda: g.vector.tensor_tensor(out[0], in0[0], in1[0], op), out, [in0, in1], in1[2], 1.0 if ps else 2.0)
 
     def cp(out, in_):
@@ -138,32 +131,28 @@ def rank_program(g, core, T, topo):
         if func is None:
             f = lambda: g.scalar.activation(out[0], in_[0], ACT.Copy, scale=scale)
         else:
-            f = lambda: g.scalar.activation(out[0], in_[0], func, bias=val(bias), scale=scale)
-        put("S", f, regs_of(in_, bias), out[1], 65.0 + in_[2] * GA * CY if in_[3] else 120.0 + in_[2] * CY)
+            f = lambda: g.scalar.activation(out[0], in_[0], func, bias=bias, scale=scale)
+        put("S", [f], regs_of(in_), out[1], 65.0 + in_[2] * GA * CY if in_[3] else 120.0 + in_[2] * CY)
 
-    def mm(*terms, fill=0):
-        calls, reads, writes, d = [], [], [], 0.0
-        for k, (out, lhsT, rhs) in enumerate(terms):
-            calls.append(lambda out=out, lhsT=lhsT, rhs=rhs, k=k: g.tensor.matmul(out[0], lhsT[0], rhs[0], k == 0, k == len(terms) - 1))
-            reads += [r for r in regs_of(lhsT, rhs) if r not in reads]
-            writes += [r for r in out[1] if r not in writes]
-            d += 15.0 + max(64, rhs[2]) * PCY
-            if k % MG == MG - 1 or k == len(terms) - 1:
-                put("P", None, reads, writes + [("lock" + out[1][0][0], 0, 1)] + [("turnP", 0, 1)] * fill, d)
-                ops[-1]["calls"], ops[-1]["fill"] = calls, fill
-                calls, reads, writes, d = [], [], [], 0.0
+    def mm(*terms, start=True, stop=True, turn=()):
+        for k0 in range(0, len(terms), MG):
+            part = list(enumerate(terms))[k0:k0 + MG]
+            calls = [lambda k=k, x=x: g.tensor.matmul(x[0][0], x[1][0], x[2][0], start and k == 0, stop and k == len(terms) - 1) for k, x in part]
+            put("P", calls, [r for k, x in part for r in regs_of(x[1], x[2])],
+                [r for k, x in part for r in x[0][1]] + [("turn" + terms[0][0][1][0][0], 0, 1)] + list(turn),
+                sum(15.0 + max(64, x[2][2]) * PCY * (1 if narrow(x[2]) else 4) for k, x in part))
 
     def iota(out, pattern, base, ch):
-        put("G", lambda: g.iota(out[0], pattern, base, ch), [], out[1], 130.0 + 2 * out[2] * CY)
+        put("G", [lambda: g.iota(out[0], pattern, base, ch, allow_small_or_imprecise_dtypes=narrow(out))], [], out[1], 130.0 + 2 * out[2] * CY)
 
     def zeros(out):
-        put("G", lambda: g.iota(out[0], [[0, out[2]]], 0, 0, allow_small_or_imprecise_dtypes=True), [], out[1], 130.0 + 2 * out[2] * CY)
+        iota(out, [[0, out[2]]], 0, 0)
 
     def sel(out, in_, pattern, base, ch):
-        put("G", lambda: g.affine_select(out[0], in_[0], pattern, OP.is_equal, 0.0, base, ch), regs_of(in_), out[1], 170.0 + 2 * out[2] * CY)
+        put("G", [lambda: g.affine_select(out[0], in_[0], pattern, OP.is_equal, 0.0, base, ch)], regs_of(in_), out[1], 170.0 + 2 * out[2] * CY)
 
-    def load(eng, sem, out, src, reg, late):
-        put(eng, lambda: queue[eng].dma_start(out, src).then_inc(T.sem[sem], 16), [], reg + [("turn" + eng, 0, 1)], 100.0, (sem, 16), late)
+    def load(k, eng, out, src):
+        put(eng, [lambda: queue[eng].dma_start(out[0], src).then_inc(T.sem["ld%d" % k], 16)], [], out[1] + [("turn" + eng, 0, 1)], 100.0, ("ld%d" % k, 16), LAND[k])
 
     def send(to, sem, lsem, also=()):
         trs = []
@@ -173,27 +162,35 @@ def rank_program(g, core, T, topo):
             n = len(eng) // len(to)
             trs.append(RemoteDMATransfer(dst_ids=[DstId(rid=rid, pnc=pid)], dma_engine_mask=sum(1 << x for x in eng[n * k:n * k + n]),
                                          remote_sem=T.sem[sem], src=src[0], dst=dst))
-        return put("G", lambda: g.remote_dma_fused(trs, local_sem=T.sem[lsem]), regs_of(*[x[1] for x in to]) + list(also), [], 500.0, (lsem, 8), 2500.0)
+        return put("G", [lambda: g.remote_dma_fused(trs, local_sem=T.sem[lsem])], regs_of(*[x[1] for x in to]) + list(also), [],
+                   500.0 + FIRST * (lsem == "la0_1"), (lsem, 8), LATE)
 
-    def arrives(sem, region, like, n):
-        put("R", None, [], region[1], 0.0, (sem, n), 0.0, [like])
+    def arrives(kind, t, p, region, like):
+        put("R", [], [], region[1], 0.0, ("%s%d_%d" % (kind, t, place[p]), engines(p)), 0.0, {like: WAKE})
 
     def places(q):
-        def far_key(r):
+        def key(r):
             c1, c2 = topo.chip(T.cores[q]), topo.chip(T.cores[r])
-            return 0 if topo.mates(c1, c2) else 1 if topo.same_plane(c1, c2) else 2
-        return [q] + sorted([r for r in range(N) if r != q], key=far_key)
+            return r != max(x for x in range(N) if x != q), 0 if topo.mates(c1, c2) else 1 if topo.same_plane(c1, c2) else 2
+        return [q] + sorted([r for r in range(N) if r != q], key=key)
     place = places(me)
-    assert all(places(r).index(me) == p for p, r in enumerate(place))
     CALLS = ((1,), (2, 3))
 
-    load("Y", "ld0", T.n0_i[:], T.n0[:], [("n0_i", 0, 16)], LAND[0])
-    load("S", "ld1", T.rch_s[:], T.rch[:], [("rch_s", 0, 256)], LAND[1])
-    load("S", "ld3", T.dr_i[0:96, :], T.dr[:, :], [("dr_i", 0, 256)], LAND[3])
-    load("Y", "ld2", T.acts_i[:], T.acts[:], [("acts_i", 0, 2048)], LAND[2])
-    load("Y", "ld4", T.regs_s[:, 0:2048], T.regs[:, 0:2048], [("regs_s", 0, 2048)], LAND[4])
-    load("Y", "ld5", T.regs_s[:, 2048:4096], T.regs[:, 2048:4096], [("regs_s", 2048, 4096)], LAND[5])
-    load("Y", "ld6", T.pay_s[:], T.pay[:], [("pay_s", 0, 2048)], LAND[6])
+    def there(p):
+        return places(place[p]).index(me)
+
+    def engines(p):
+        return 8 // len([ps for ps in CALLS if there(p) in ps][0])
+
+    load(0, "Y", a("n0_i"), T.n0[:])
+    load(1, "S", a("rch_s"), T.rch[:])
+    load(2, "S", a("dr_i", rows=96), T.dr[:, :])
+    load(3, "Y", a("acts_i"), T.acts[:])
+    parts = ((0, 2048), (2048, 3584), (3584, 4096))
+    for k, (lo, hi) in enumerate(parts):
+        load(4 + k, "Y", a("regs_s", lo, hi), T.regs[:, lo:hi])
+        ts(a("P", lo, hi), a("regs_s", lo, hi), 0.0, OP.max)
+    load(7, "Y", a("pay_s"), T.pay[:])
 
     kf = a("kf")
     def col(j):
@@ -206,7 +203,9 @@ def rank_program(g, core, T, topo):
     iota(a("Bm"), [[1, 8], [0, 16]], 0, 0)
     iota(a("rp"), [[0, 16], [1, 16]], 0, 0)
     iota(a("Dm"), [[1, 128]], 0, -1)
+    iota(a("lid"), [[1, 256]], 1, 0)
     fill(a("ONE"), 1.0)
+    fill(a("SIX"), 0.0625)
     cp(a("crep"), a("li"))
     ts(a("pk", 0, 1), a("pi", 0, 1), 15, OP.bitwise_and)
     ts(a("pk", 1, 2), a("pi", 1, 2), 4, OP.arith_shift_right)
@@ -220,9 +219,7 @@ def rank_program(g, core, T, topo):
     ts(a("TRI"), a("Dm"), 0, OP.is_ge, 64.0, OP.mult)
     tt(a("TRI"), a("TRI"), a("BO"), OP.mult)
     fill(a("TRI", 15, 128, 16), 0.0)
-    ts(col(0), kf, 15.0, OP.is_lt)
-    fill(a("SIX"), 0.0625)
-    for j in (0, 1):
+    for j in range(6):
         sel(a("SEL", 128 * j, 128 * j + 128, rows=96), a("ONE", 0, 128, rows=96), [[-12, 8], [0, 16]], -home_te[j], 1)
     sel(a("ID"), a("ONE", 0, 128), [[-1, 128]], 0, 1)
     sel(a("E1"), a("BO"), [[1, 128]], -1, -1)
@@ -230,29 +227,27 @@ def rank_program(g, core, T, topo):
     sel(a("DIF"), a("BO"), [[1, 128]], 1, -1)
     sel(a("D5"), a("BO"), [[1, 128]], -15, -1)
     zeros(a("DST"))
+    ts(col(0), kf, 15.0, OP.is_lt)
     tt(a("E1"), a("E1"), a("E3"), OP.add)
     ts(a("E2"), a("ID"), col(0), OP.mult)
     tt(a("OHM"), a("E1"), a("E2"), OP.subtract)
     tt(a("DIF"), a("DIF"), a("D5"), OP.add)
     tt(a("DIF"), a("DIF"), a("E2"), OP.subtract)
-    ts(a("D5"), a("DIF"), 5.0, OP.mult)
-    ts(a("Dn"), a("DIF"), -2048.0, OP.mult)
-    ts(a("I5"), a("ID"), 5.0, OP.mult)
-    ts(a("In"), a("ID"), -2048.0, OP.mult)
-    ts(a("BO13"), a("BO"), 13.0, OP.mult)
+    for out, src, c in (("D5", "DIF", 5.0), ("Dn", "DIF", -2048.0), ("I5", "ID", 5.0), ("IDn", "ID", -1.0), ("In", "ID", -2048.0),
+                        ("BO13", "BO", 13.0), ("ID32", "ID", 1.0), ("ZM", "ID", 16.0), ("Zs", "Z", -2.0 ** -12)):
+        ts(a(out), a(src), c, OP.mult)
     ts(a("R13"), a("Z", 0, 128), 13.0, OP.mult)
+    tt(a("ZM"), a("BO"), a("ZM"), OP.subtract)
     fill(a("CST", rows=64), 0.0)
     for e, step, c in ((1, 16, 274432.0), (2, 1, 274432.0), (3, 16, 274432.0), (4, 1, 272384.0)):
-        lo = 128 * (e - 1) + step - 1
-        fill(a("CST", lo, 128 * e, step, rows=1), c)
-        vop(lambda lo=lo, e=e, step=step: g.vector.memset(T[AT["CST"][0]][32:33, AT["CST"][1] + lo:AT["CST"][1] + 128 * e:step], float(e)), a("CST", lo, 128 * e), [], 64)
+        fill(a("CST", 128 * (e - 1) + step - 1, 128 * e, step, rows=1), c)
+        fill(a("CST", 128 * (e - 1) + step - 1, 128 * e, step, rows=1, row=32), float(e))
     fill(a("LC"), 0.0)
     fill(a("LC", 24, 32), -2048.0)
-    ts(col(20), kf, 16.0, OP.mult, -1.0, OP.add)
-    ts(a("LC", 8, 16), a("li", 0, 8), 256.0, OP.mult, col(20), OP.add)
-    ts(col(1), kf, -EPS, OP.mult)
-    ts(col(2), kf, 15.0, OP.is_equal, 16 * EPS, OP.mult)
-    tt(col(1), col(1), col(2), OP.add)
+    ts(col(1), kf, 16.0, OP.mult, -1.0, OP.add)
+    ts(a("LC", 8, 16), a("li", 0, 8), 256.0, OP.mult, col(1), OP.add)
+    ts(a("CW", rows=1), a("rp", 0, 128, rows=1), 0.5, OP.add, -EPS, OP.mult)
+    fill(a("CW", 15, 128, 16, rows=1), EPS)
     cp(a("n0u"), a("n0_i"))
     cp(a("n0f"), a("n0_i"))
     tt(a("q0"), via(a("n0f"), a("crep", 0, 16)), a("MX"), OP.mult)
@@ -260,7 +255,8 @@ def rank_program(g, core, T, topo):
         act(a("xr1", 1024 * u, 1024 * u + 1024), via(a("rch_s", 64 * u, 64 * u + 64), a("crep", 0, 64)))
     cp(a("drb", rows=96), a("dr_i", rows=96))
     ts(a("w_i", rows=96), a("dr_i", rows=96), 15, OP.bitwise_and)
-    cp(a("wb", rows=96), a("w_i", rows=96))
+    cp(a("wb", 0, 256, rows=96), a("w_i", rows=96))
+    ts(a("wb", 256, 512, rows=96), a("w_i", rows=96), EPS, OP.mult)
     ts(a("y1"), a("rch_s"), -1.0, OP.add)
     tt(a("DST", 0, 116), a("OHM", 0, 116), a("OHM", 4, 120), OP.add)
     tt(a("E1", 0, 116), a("OHM", 8, 124), a("OHM", 12, 128), OP.add)
@@ -269,24 +265,21 @@ def rank_program(g, core, T, topo):
     tt(a("DST", 0, 116), a("DST", 0, 116), a("E3", 0, 116), OP.mult)
     ts(col(4), kf, float(REG), OP.mult, -1.0, OP.add)
     ts(col(5), kf, float(REG), OP.mult, 64.0, OP.add)
-    ts(col(6), kf, 4096.0, OP.add)
-    ts(col(21), kf, 4112.0, OP.add)
+    ts(col(2), kf, 4096.0, OP.add)
+    ts(col(3), kf, 4112.0, OP.add)
     zeros(a("ZT"))
     for j in range(6):
         sel(a("ZT", 144 * j + 15, 144 * j + 143, 16, rows=96), a("ONE", 0, 8, rows=96), [[-12, 8]], -far_te[j], 1)
     ts(col(7), kf, 2.0, OP.is_equal)
     ts(col(8), kf, 3.0, OP.is_equal)
     tt(col(8), col(7), col(8), OP.add)
-    ts(a("ZN"), a("Z"), col(8), OP.mult)
-    ts(a("N13"), a("BO13"), col(8), OP.mult)
-    ts(a("RN13"), a("R13"), col(8), OP.mult)
+    for out, src in (("ZN", "Z"), ("N13", "BO13"), ("RN13", "R13")):
+        ts(a(out), a(src), col(8), OP.mult)
     ts(a("M23"), a("Z", 12, 140), col(7), OP.mult)
     tt(a("M23"), a("ID"), a("M23"), OP.subtract)
-    for j, (row, w) in enumerate(((0, 1.0), (1, 1.0), (5, 1.0), (6, 1.0), (4, -8192.0))):
+    for j, (row, w) in enumerate(((0, 1.0), (1, 1.0), (5, EPS), (6, EPS), (4, -8192.0))):
         ts(col(9 + j), kf, float(row), OP.is_equal, w, OP.mult)
         ts(a("SR", 128 * j, 128 * j + 128), a("BO"), col(9 + j), OP.mult)
-    ts(a("ZM"), a("ID"), 16.0, OP.mult)
-    tt(a("ZM"), a("ZM"), a("BO"), OP.subtract)
     ts(a("ta"), a("rd", 0, 16), 0.0, OP.is_gt, 16384.0, OP.mult)
     ts(a("tb"), a("rd", 0, 16), 0.0, OP.is_equal, -8192.0, OP.mult)
     tt(a("ta"), a("ta"), a("tb"), OP.add)
@@ -294,34 +287,29 @@ def rank_program(g, core, T, topo):
         fill(a("CM" + n, 16, 32), c)
         ts(a("CM" + n, 0, 16), a("ta"), c, OP.add)
         ts(a("CM" + n, 32, 48), a("ta"), c, OP.add)
+        for c in (48, 96, 192):
+            cp(a("CM" + n, c, 2 * c), a("CM" + n, 0, c))
         fill(a("D" + n), 0.0)
         fill(a("D" + n, 0, 384, 48), -4.0)
         fill(a("D" + n, 16, 384, 48), -4.0)
     for j, c in enumerate((15.0, 47.0, 47.0)):
         ts(a("crep2", j, 24, 3), a("li", 0, 8), 48.0, OP.mult, c, OP.add)
-    put("G", lambda: g.iota(a("lid")[0], [[1, 256]], 1, 0, allow_small_or_imprecise_dtypes=True), [], a("lid")[1], 560.0)
-    ts(a("ID32"), a("ID"), 2.0 ** -9, OP.mult)
-    ts(a("own"), a("li", 0, 16), 16.0, OP.mult, col(21), OP.add)
-    ts(a("own"), a("own"), 16.0, OP.add, 2.0 ** -9, OP.mult)
+    ts(a("ownl"), a("li", 0, 16), 16.0, OP.mult, kf, OP.add)
+    ts(a("own"), a("ownl"), 4128.0, OP.add, 2.0 ** -21, OP.mult)
+    ts(a("ownl"), a("ownl"), 1.0, OP.add, 2.0 ** -8, OP.mult)
     act(a("paym"), a("pay_s"), ACT.Identity, bias=-1.0)
     zeros(a("send0"))
     zeros(a("zr0"))
-    for j in range(2, 6):
-        sel(a("SEL", 128 * j, 128 * j + 128, rows=96), a("ONE", 0, 128, rows=96), [[-12, 8], [0, 16]], -home_te[j], 1)
 
     def draws(t):
-        for src, b in (("drb", "b6"), ("wb", "b7")):
-            for j in (0, 1):
-                s = 128 * (2 * t + j)
-                mm((a(b, 256 * j, 256 * j + 256), a("SEL", s, s + 128, rows=96), a(src, rows=96)))
-            if src == "drb":
-                act(a("vb%d" % t), a(b), ACT.Identity, bias=BETA)
-            else:
-                act(a("wt%d" % t), a(b), ACT.Relu, bias=col(1), scale=EPS)
+        for j in (0, 1):
+            s = 128 * (2 * t + j)
+            mm((a("b6", 256 * j, 256 * j + 256), a("SEL", s, s + 128, rows=96), a("drb", rows=96)))
+        act(a("vb%d" % t), a("b6"), ACT.Identity, bias=BETA)
         grp = []
         for src, j, row in (("drb", 0, 0), ("drb", 1, 1), ("wb", 0, 5), ("wb", 1, 6)):
             s = 144 * (2 * t + j) + 15 - row
-            grp.append((a("b5", 256, 512), a("ZT", s, s + 128, rows=96), a(src, rows=96)))
+            grp.append((a("b5", 256, 512), a("ZT", s, s + 128, rows=96), a(src, 0, 256, rows=96)))
         mm(*(grp + [(a("b5", 256, 512), a("Z", 11, 139), a("SIX"))]))
         act(a("auxS%d" % t), a("b5", 256, 512))
 
@@ -351,39 +339,41 @@ def rank_program(g, core, T, topo):
         return [x for l in range(lo, lo + n, 32) for x in (((l, 16), (l + 16, 16)) if l % 128 == 0 else ((l, 32),))]
 
     def spread(win, lo, n):
+        name, w0, _ = win[1][0]
         for l, c in pieces(lo, n):
-            name, w0, _ = win[1][0]
             act(a("xr", 16 * l, 16 * (l + c)), via(a(name, w0 + l - lo, w0 + l - lo + c), a("crep", 0, c)), ACT.Identity, bias=1.0)
-            stream()
 
     def weights(e, u, l0):
-        for j, CG in (pieces(l0, 64) if e > 1 else ((l0, 32), (l0 + 32, 32))):
-            w, x, p = a("W", 16 * j, 16 * (j + CG)), a("xr1" if e == 1 else "xr", 16 * j, 16 * (j + CG)), via(a("P", 0, 4096), a("A%d" % e, j, j + CG))
-            if e == 1 and j // CG in BYS:
-                b = a("b%d" % (6 + BYS.index(j // CG) % 2))
+        for j, n in (pieces(l0, 64) if e > 1 else ((l0, 32), (l0 + 32, 32))):
+            w, x = a("W", 16 * j, 16 * (j + n)), a("xr1" if e == 1 else "xr", 16 * j, 16 * (j + n))
+            p = via(a("P", 0, 4096), a("A%d" % e, j, j + n))
+            if e == 1 and j // 32 in BYS:
+                b = a("b%d" % (6 + BYS.index(j // 32) % 2))
                 act(w, p)
-                stream()
                 mm((b, a("ID"), x))
                 tt(w, b, w, OP.min)
             else:
                 tt(w, p, x, OP.min)
-            stream()
+            ops[-1]["w"] = ops[-1]["w"] + [("turnV", 0, 1)]
         c = l0 - 128 * u
-        mm(*[(a("b%d" % u, c, c + 64), a("Z", 15 - k, 143 - k), a("W", 16 * l0 + k, 16 * l0 + 1024, 16)) for k in range(16)], fill=1)
+        mm(*[(a("b%d" % u, c, c + 64), a("Z", 15 - k, 143 - k), a("W", 16 * l0 + k, 16 * l0 + 1024, 16)) for k in range(16)], turn=[("turnP", 0, 1)])
 
-    def choose(e, t, u):
+    def choose(e, t, u, aux=None):
         lo, hi = 128 * u, 128 * u + 128
         x, y, z, q, L = "b%d" % u, "b%d" % (2 + u), "b%d" % (4 + u), "q%d_%d" % (e, u), "L%d_%d" % (e, u)
         if e < 3:
-            vb, wt = [a(n % t, 256 * (e - 1) + lo, 256 * (e - 1) + hi) for n in ("vb%d", "wt%d")]
+            vb = a("vb%d" % t, 256 * (e - 1) + lo, 256 * (e - 1) + hi)
+            mod16 = [(a(y, 384, 512), a("SEL", 256 * t + 128 * e - 128, 256 * t + 128 * e, rows=96), a("wb", 256 + lo, 256 + hi, rows=96))]
         else:
-            vb, wt = [a(n % u, 128 * (e - 3), 128 * (e - 2)) for n in ("vbF%d", "wtF%d")]
+            vb = a("vbF%d" % u, 128 * (e - 3), 128 * (e - 2))
+            mod16 = [(a(y, 384 + 64 * h, 448 + 64 * h), a("SR", 128 * e - 128, 128 * e), aux(2 * u + h)) for h in (0, 1)]
         odd = e % 2
         ind = a(q, 128, 256) if odd else a("ind", lo, hi)
         act(a("ms", lo, hi), a(x, 0, 128))
-        mm((a(x, 128, 256), a("ID"), wt), (a(x, 128, 256), a("BO"), a("ms", lo, hi)))
+        mm((a(y, 384, 512), a("CW", rows=1), a("ONE", 0, 128, rows=1)), *mod16, stop=False)
+        mm((a(y, 384, 512), a("BO"), a("ms", lo, hi)), start=False)
         mm((a(x, 256, 384), a("TRI"), a("ms", lo, hi)))
-        tt(a("t1", lo, hi), a(x, 128, 256), vb, OP.mult)
+        tt(a("t1", lo, hi), a(y, 384, 512), vb, OP.mult)
         tt(ind, a(x, 256, 384), a("t1", lo, hi), OP.is_lt)
         yin = a("yF" if e == 3 else "y%d" % e, lo, hi)
         yout = a("y%d" % (e + 1), lo, hi)
@@ -416,37 +406,38 @@ def rank_program(g, core, T, topo):
             ts(a("L2", 16 * u, 16 * u + 16), a(z, 0, 16), 2048.0, OP.add)
             c, rec = 8 * u, a("L2", 24 * u, 24 * u + 8)
         for j in (0, 1):
-            act(a("D" + "hf"[e // 4], 192 * u + 15 + 32 * j, 192 * u + 192, 48), a(z, c + j, c + 8, 2), ACT.Identity, bias=0.25, scale=2.0 ** -13)
+            act(a("D" + "hf"[e // 4], 192 * u + 15 + 32 * j, 192 * u + 192, 48), a(z, c + j, c + 8, 2), ACT.Identity, bias=2.0 ** -10, scale=2.0 ** -21)
         tt(yout, via(a("P", 0, 4096), rec), yin, OP.min)
         if e == 2:
             mm((a(y, 128, 256), a("M23"), a("aux1", lo, hi)), (a(y, 128, 256), a("Z", 12, 140), nodes))
             act(a("auxB", lo, hi), a(y, 128, 256))
 
-    def first_of(n, e, cm, dead, src):
-        b = "b7" if n == "h" else "b6"
-        for j in range(8):
-            q, c = ("q2", 128 + 384 * (j // 4) + 32 * (j % 4)) if e == 2 else ("q4_%d" % (j // 4), 128 + 32 * (j % 4))
-            mm((a(b, 48 * j, 48 * j + 48), a("ID"), a(cm)),
-               (a(b, 48 * j, 48 * j + 16), a("BO"), a(q, c, c + 16)), (a(b, 48 * j + 16, 48 * j + 48), a("BO"), a(q, c, c + 32)),
-               (a(b, 48 * j, 48 * j + 16), dead, src(32 * j, 16)), (a(b, 48 * j + 16, 48 * j + 48), dead, src(32 * j, 32)))
-        act(a("Y" + n), via(a("D" + n), a("crep2")), scale=8192.0)
-        tt(a("eq" + n), a(b, 0, 384), a("Y" + n), OP.is_equal)
-        scan(a("lc" + n), a("D" + n), a("eq" + n), 0.0, OP.add, OP.max)
-        off = "offf" if n == "f" else "o32"
-        ts(a(off, 0, 16, 2), a("lc" + n, 15, 384, 48), 8192.0, OP.mult, col(6), OP.min)
-        ts(a(off, 1, 16, 2), a("lc" + n, 47, 384, 48), 8192.0, OP.mult, col(21), OP.min)
+    def first_of(n, b, j0, j1, dead, alive, rec):
+        lo, hi = 48 * j0, 48 * j1
+        terms = [(a(b, lo, hi), a("ID"), a("CM" + n, lo, hi))]
+        for m, x in ((dead, alive), (a("BO"), rec)):
+            for j in range(j0, j1):
+                terms += [(a(b, 48 * j, 48 * j + 16), m, x(32 * j, 16)), (a(b, 48 * j + 16, 48 * j + 48), m, x(32 * j, 32))]
+        mm(*terms[:1], stop=False)
+        mm(*terms[1:], start=False)
+        off = "offf" if n == "f" else "offw"
+        act(a("Y" + n, lo, hi), via(a("D" + n, lo, hi), a("crep2", 0, (hi - lo) // 16)), scale=2.0 ** 21)
+        tt(a("eq" + n, lo, hi), a(b, lo, hi), a("Y" + n, lo, hi), OP.is_equal)
+        scan(a("lc" + n, lo, hi), a("D" + n, lo, hi), a("eq" + n, lo, hi), 0.0, OP.add, OP.max)
+        ts(a(off, 2 * j0, 2 * j1, 2), a("lc" + n, lo + 15, hi, 48), 2.0 ** 21, OP.mult, col(2), OP.min)
+        ts(a(off, 2 * j0 + 1, 2 * j1, 2), a("lc" + n, lo + 47, hi, 48), 2.0 ** 21, OP.mult, col(3), OP.min)
+
+    def change(off, blocks, values, table):
+        for c in blocks:
+            scatter(a(table), a(off, 2 * c, 2 * c + 2), a(values, 32 * c, 32 * c + 32))
 
     def first_of_all():
-        cp(a("offw"), a("o32"))
-        change("w", list(range(7, -1, -1)), "lid", "who")
-        tt(a("lost"), via(a("who"), a("offw")), a("lid"), OP.not_equal)
-        lists(a("b7", 0, 16), ("lost", 0), 256, [(a("b7", 0, 16), a("ID32"), a("o32"))])
-        tt(a("o32"), a("b7", 0, 16), a("own"), OP.min)
-        ts(a("offh"), a("o32"), 512.0, OP.mult)
-
-    def change(n, blocks, values, table="regs_s"):
-        for c in blocks:
-            scatter(a(table), a("off" + n, 2 * c, 2 * c + 2), a(values, 32 * c, 32 * c + 32))
+        change("offw", range(7, -1, -1), "lid", "who")
+        act(a("found"), via(a("who"), a("offw")))
+        lists(a("b4", 32, 48), ("found", 0), 256, [(a("b4", 32, 48), a("ID32"), a("ownl")), (a("b4", 32, 48, 2), a("ID32"), a("lch", 15, 384, 48)),
+                                                   (a("b4", 33, 48, 2), a("ID32"), a("lch", 47, 384, 48))], z="Zs")
+        tt(a("o32"), a("b4", 32, 48), a("own"), OP.min)
+        ts(a("offh"), a("o32"), 2.0 ** 21, OP.mult)
 
     draws(0)
     for u in (0, 1):
@@ -454,34 +445,28 @@ def rank_program(g, core, T, topo):
         next_nodes(1, u, [(0, 128, "BO13", "R13", a("q0", 128 * u, 128 * u + 128))])
         cp(a("TD1", 128 * u, 128 * u + 128), a("b%d" % (2 + u), 128, 256))
     for t in range(RO):
-        if t == 0:
-            ts(a("P", 0, 2048), a("regs_s", 0, 2048), 0.0, OP.max)
-            ts(a("P", 2048, 3424), a("regs_s", 2048, 3424), 0.0, OP.max)
-            act(a("P", 3424, 4096), a("regs_s", 3424, 4096), ACT.Relu)
-        else:
-            for u in (0, 1):
-                mm((a("b%d" % (2 + u), 128, 256), a("ID"), a("TD1", 128 * u, 128 * u + 128)))
+        more = t + 1 < RO
+        land, zr, out = "land%d" % t, "zr%d" % t, "send%d" % t
         for e in (1, 2):
             for u in (0, 1):
+                if e == 1 and t:
+                    mm((a("b%d" % (2 + u), 128, 256), a("ID"), a("TD1", 128 * u, 128 * u + 128)))
                 weights(e, u, 128 * u)
                 weights(e, u, 128 * u + 64)
                 choose(e, t, u)
-        land, zr, out = "land%d" % t, "zr%d" % t, "send%d" % t
         for u in (0, 1):
             scatter(a(out, 0, 1216), a("L2", 8 + 8 * u, 16 + 8 * u), a("auxB", 128 * u, 128 * u + 128))
         scatter(a(out, 64, 1280), a("L2", 8, 24), a("y3"))
         for ps in CALLS:
-            o = send([(place[p], a(out, REG * place[p], REG * place[p] + 128), T[land][:, 128 * p:128 * p + 128]) for p in ps],
+            o = send([(place[p], a(out, REG * place[p], REG * place[p] + 128), T[land][:, 128 * there(p):128 * there(p) + 128]) for p in ps],
                      "a%d_%d" % (t, me), "la%d_%d" % (t, ps[0]), [(zr, 0, 1280)])
             for p in ps:
-                arrives("a%d_%d" % (t, place[p]), a(land, 128 * p, 128 * p + 128), o, 8 // len(ps))
-        fills = [a("who", 1032 * j, 1032 * j + 1032) for j in range(4)] * (t == 0)
-        for x in fills + ([a("send%d" % (t + 1)), a("zr%d" % (t + 1))] if t + 1 < RO else []):
+                arrives("a", t, p, a(land, 128 * p, 128 * p + 128), o)
+        for x in [a("who", 1032 * j, 1032 * j + 1032) for j in range(4)] * (t == 0) + ([a("send%d" % (t + 1)), a("zr%d" % (t + 1))] if more else []):
             zeros(x)
-            ops[-1]["after"].append(o)
-            ops[-1]["soon"] = 1
+            ops[-1]["after"][o] = -LATE
         ts(a("ng"), a("q2", 256, 512), col(5), OP.is_ge, 8192.0, OP.mult)
-        first_of("h", 2, "CMh", a("BO"), lambda l, n: a("ng", l, l + n))
+        first_of("h", "b7", 0, 8, a("BO"), lambda l, n: a("ng", l, l + n), lambda l, n: a("q2", 128 + l + 256 * (l // 128), 128 + l + 256 * (l // 128) + n))
 
         def aux(p, lo=0, hi=64):
             name, s = (out, REG * me) if p == 0 else (land, 128 * p)
@@ -494,73 +479,179 @@ def rank_program(g, core, T, topo):
             for h in (0, 1):
                 p = 2 * u + h
                 if u == 0:
-                    src = aux(p)[1][0]
-                    lists(a(z, 8 * h, 8 * h + 4), (src[0], src[1]), 64, z="ZN")
+                    lists(a(z, 8 * h, 8 * h + 4), aux(p)[1][0][:2], 64, z="ZN")
                     cp(a(nF, 8 * h, 8 * h + 4), a(z, 8 * h, 8 * h + 4))
                 acts_at(3, 64 * p, 64 * p + 64, a(nF, 8 * h, 8 * h + 4))
                 spread(aux(p, 64, 128), 64 * p, 64)
-                for j in range(4):
+                for j in (0, 1):
                     mm((a(m, 128 * j + 64 * h, 128 * j + 64 * h + 64), a("SR", 128 * j, 128 * j + 128), aux(p)))
-                act(a("yF", 64 * p, 64 * p + 64), aux(p, 64, 128))
+                sel(a("yF", 64 * p, 64 * p + 64), aux(p, 64, 128), [[0, 64]], 0, 0)
                 weights(3, u, 64 * p)
             act(a("vbF%d" % u), a(m, 0, 256), ACT.Identity, bias=BETA)
-            act(a("wtF%d" % u), a(m, 256, 512), ACT.Relu, bias=col(1), scale=EPS)
             next_nodes(3, u, [(64 * h, 64 * h + 64, "N13", "RN13", aux(2 * u + h)) for h in (0, 1)])
-            choose(3, t, u)
-        if t + 1 < RO:
-            draws(t + 1)
+            choose(3, t, u, aux)
         for u in (0, 1):
-            lo, hi, x, L = 128 * u, 128 * u + 128, "b%d" % u, "L4_%d" % u
+            lo, hi, x, y, L = 128 * u, 128 * u + 128, "b%d" % u, "b%d" % (2 + u), "L4_%d" % u
             weights(4, u, lo)
             weights(4, u, lo + 64)
-            choose(4, t, u)
+            choose(4, t, u, aux)
             tt(a("lv", lo, hi), via(a("paym"), a(L, 0, 8)), a("y5", lo, hi), OP.min)
             mm((a(x, 0, 128), a("ZM"), a("lv", lo, hi)))
-            act(a("zN", lo, hi), a(x, 0, 128), ACT.Sign, scale=-1.0)
+            ts(a("zN", lo, hi), a(x, 0, 128), 1.0, OP.min, -1.0, OP.max)
             ps = CALLS[u]
             o = send([(place[p], a("zN", 64 * p, 64 * p + 64), T[zr][:, REG * me:REG * me + 64]) for p in ps], "z%d_%d" % (t, me), "lz%d_%d" % (t, ps[0]))
             for p in ps:
-                arrives("z%d_%d" % (t, place[p]), a(zr, REG * place[p], REG * place[p] + 64), o, 8 // len(ps))
+                arrives("z", t, p, a(zr, REG * place[p], REG * place[p] + 64), o)
             if u == 0:
                 act(a(zr, REG * me, REG * me + 64), a("zN", 0, 64))
-            tt(a("NV", lo, hi), via(a("regs_s", 0, 4096), a(L, 8, 16)), a("zN", lo, hi), OP.subtract)
-        first_of("f", 4, "CMf", a("SR", 512, 640), lambda l, n: aux(l // 64, l % 64, l % 64 + n))
-        if t + 1 < RO:
-            ts(a("NP"), a("NV"), 15.0, OP.min, 0.0, OP.max)
-        ts(a("NV"), a("NV"), 15.0, OP.min, -15.0, OP.max)
+            act(a("NV", lo, hi), via(a("regs_s", 0, 4096), a(L, 8, 16)))
+            mm((a(y, 384, 512), a("ID"), a("NV", lo, hi)), (a(y, 384, 512), a("IDn"), a("zN", lo, hi)))
+            ts(a("NV", lo, hi), a(y, 384, 512), 15.0, OP.min, -15.0, OP.max)
+            if more:
+                act(a("NP", lo, hi), a("NV", lo, hi), ACT.Relu)
+            first_of("f", "b%d" % (6 + u), 4 * u, 4 * u + 4, a("SR", 512, 640), lambda l, n: aux(l // 64, l % 64, l % 64 + n),
+                     lambda l, n: a("q4_%d" % (l // 128), 128 + l % 128, 128 + l % 128 + n))
         first_of_all()
+        if more:
+            draws(t + 1)
         blocks = [2 * place.index(r) + c for r in (3, 2, 1, 0) for c in (1, 0)]
-        change("f", blocks, "NV")
-        if t + 1 < RO:
-            change("f", blocks, "NP", "P")
+        change("offf", blocks, "NV", "regs_s")
+        if more:
+            change("offf", blocks, "NP", "P")
         act(a("zl"), via(a(zr), a("L2", 8, 24)))
         for u in (1, 0):
             tt(a("HV", 128 * u, 128 * u + 128), via(a("regs_s", 0, 4096), a("L2", 24 * u, 24 * u + 8)), a("zl", 128 * u, 128 * u + 128), OP.add)
-        if t + 1 < RO:
+        if more:
             ts(a("HP"), a("HV"), 15.0, OP.min, 0.0, OP.max)
             scatter(a("P"), a("offh"), a("HP"))
+            ends.append(len(ops) - 1)
+            now[0] += 1
         ts(a("HV"), a("HV"), 15.0, OP.min, -15.0, OP.max)
         scatter(a("regs_s"), a("offh"), a("HV"))
-    put("Y", lambda: g.sync.dma_start(T.yr[:], T.regs_s[:, 0:4096]).then_inc(T.sem.yo, 16), [("regs_s", 0, 4384)], [], 100.0, ("yo", 16), 8000.0)
+    ends.append(put("Y", [lambda: g.sync.dma_start(T.yr[:], T.regs_s[:, 0:4096]).then_inc(T.sem.yo, 16)], [("regs_s", 0, 4384)], [], 100.0, ("yo", 16), 8000.0))
 
     seen = {}
     for i, o in enumerate(ops):
-        pred = {j: -ops[j]["late"] if "soon" in o else WAKE for j in o["after"]}
+        pred = dict(o["after"])
         for regs, w in ((o["r"], False), (o["w"], True)):
             for name, lo, hi in regs:
                 for j, l2, h2, w2 in seen.get(name, []):
                     if l2 < hi and lo < h2 and (w or w2) and j != i:
-                        same = ops[j]["e"] == o["e"] and (not w2 or (w and o["e"] == "P"))
+                        same = w and ops[j]["e"] == o["e"] == "P"
                         pred[j] = max(pred.get(j, -1e9), -ops[j]["late"] if name[:4] == "turn" else 0.0 if same else WAKE)
         for regs, w in ((o["r"], False), (o["w"], True)):
             for name, lo, hi in regs:
                 seen[name] = [x for x in seen.get(name, []) if not (w and lo <= x[1] and x[2] <= hi)] + [(i, lo, hi, w)]
-        o["pred"], o["succ"], o["left"] = pred, [], len(pred)
-        for j in pred:
-            ops[j]["succ"].append(i)
-    for i in range(len(ops) - 1, -1, -1):
-        o = ops[i]
-        o["way"] = o["d"] + o["late"] + max([ops[j]["way"] + ops[j]["pred"][i] for j in o["succ"]] + [0.0])
+        o["in"], o["out"] = {j: ops[j]["d"] + ops[j]["late"] + w for j, w in pred.items()}, {}
+        o["use"] = [] if o["e"] == "R" else [o["e"]] + sorted(set(r[0] for r in o["r"] + o["w"] if r[0] in BANKS))
+        for j, w in pred.items():
+            ops[j]["out"][i] = o["d"] + ops[j]["late"] + w
+    for o in reversed(ops):
+        o["way"] = o["d"] + max([o["late"]] + [ops[j]["way"] + w - ops[j]["d"] for j, w in o["out"].items()])
+
+    def lay(order, at, busy, back=False):
+        for i in order:
+            o = ops[i]
+            t, d, eng = (o["late"] if back else 0.0), o["d"], o["e"]
+            for j, w in o["out" if back else "in"].items():
+                if j in at and at[j] + w > t:
+                    t = at[j] + w
+            moved = True
+            while moved:
+                moved = False
+                for r in o["use"]:
+                    b = busy[r]
+                    k = len(b)
+                    while k and b[k - 1][1] + WAKE > t:
+                        k -= 1
+                    for t0, t1, e in b[k:]:
+                        pad = WAKE if e != eng else 0.0
+                        if t0 - pad >= t + d:
+                            break
+                        if t1 + pad > t:
+                            t, moved = t1 + pad, True
+            for r in o["use"]:
+                b = busy[r]
+                k = len(b)
+                while k and b[k - 1][0] > t:
+                    k -= 1
+                b.insert(k, (t, t + d, eng))
+            at[i] = t
+        return at
+
+    def in_order(part, key):
+        k = {}
+        for i in sorted(part):
+            k[i] = max([key[i]] + [k[j] + 0.001 for j in ops[i]["in"] if j in k])
+        return sorted(part, key=lambda i: (k[i], i))
+
+    def blockers(part, at, i):
+        before, last, pairs = {}, {}, []
+        for j in sorted(part, key=lambda j: at[j]):
+            before[j], last[ops[j]["e"]] = last.get(ops[j]["e"]), j
+        while i in before:
+            c = [(round(at[j] + w), 1, j) for j, w in ops[i]["in"].items()]
+            j = before[i]
+            if j is not None and ops[i]["use"]:
+                c.append((round(at[j] + ops[j]["d"]), 0, j))
+            if not c:
+                break
+            _, dep, j = max(c)
+            if not dep and j not in ops[i]["in"]:
+                pairs.append((j, i))
+            i = j
+        return pairs
+
+    seed = [1]
+    def chance(lo, hi):
+        seed[0] = (seed[0] * 1103515245 + 12345) % 2147483648
+        return lo + (hi - lo) * seed[0] / 2147483648.0
+
+    def idle():
+        return {r: [] for r in list("VPSGY") + BANKS}
+
+    done, busy = {}, idle()
+    for t in range(RO):
+        part = [i for i, o in enumerate(ops) if o["round"] == t]
+        def trial(order):
+            b = {r: list(x) for r, x in busy.items()}
+            at = lay(order, dict(done), b)
+            return at[ends[t]], at, b
+        if t in PLAN:
+            best, tries = trial(in_order(part, PLAN[t])), AGAIN
+        else:
+            order, best, tries = sorted(part, key=lambda i: (-ops[i]["way"], i)), None, TRIES
+            for _ in range(PASSES):
+                x = trial(order)
+                if best is None or x[0] < best[0]:
+                    best = x
+                ta = lay(sorted(part, key=lambda i: (-x[1][i] - ops[i]["d"], -i)), {}, idle(), True)
+                order = sorted(part, key=lambda i: (-ta[i] - ops[i]["d"], i))
+        while tries > 0:
+            at = best[1]
+            pairs = blockers(part, at, ends[t])
+            if not pairs:
+                break
+            for _ in range(8):
+                j, i = pairs[int(chance(0, len(pairs)))]
+                key = {k: at[k] for k in part}
+                kind = int(chance(0, 3))
+                k, key_k = ((i, at[j] - 1.0), (j, at[j] - chance(300, 3000)), (j, at[i] + chance(1, 1500)))[kind]
+                key[k], up = key_k, [k]
+                while up:
+                    k = up.pop()
+                    for p in ops[k]["in"]:
+                        if p in key and key[p] > key[k]:
+                            key[p] = key[k] - 0.01
+                            up.append(p)
+                x = trial(in_order(part, key))
+                tries -= 1
+                if x[0] <= best[0] + 1.0:
+                    best = x
+                    break
+        PLAN.setdefault(t, {k: best[1][k] for k in part})
+        done = best[1]
+        busy = {r: [x for x in b if x[1] > best[0] - 6000.0] for r, b in best[2].items()}
 
     count = {"eV": 0, "eP": 0, "eS": 0, "eG": 0}
     known = {e: {} for e in "VPSGYR"}
@@ -570,30 +661,23 @@ def rank_program(g, core, T, topo):
         need = {}
         for regs, w in ((reads, False), (writes, True)):
             for name, lo, hi in regs:
-                bank = name in BANKS
                 for (e2, tok, l2, h2, w2) in acc.get(name, []):
-                    if name not in SCRATCH:
-                        hit = False
-                    elif bank and e2 != eng:
+                    if name in BANKS and e2 != eng:
                         hit = True
                     elif l2 < hi and lo < h2:
-                        if w and w2:
-                            hit = not (eng == "P" and e2 == "P")
-                        elif w:
-                            hit = e2 != eng
-                        else:
-                            hit = w2
+                        hit = (w or w2) and not (w and eng == "P" and e2 == "P")
                     else:
                         hit = False
                     if hit and known[eng].get(tok[0], 0) < tok[1] and need.get(tok[0], 0) < tok[1]:
                         need[tok[0]] = tok[1]
         return need
 
-    def issue(o):
-        eng = o["e"]
-        tok = o["tok"]
+    for i in sorted(done, key=lambda i: (done[i], i)):
+        o = ops[i]
+        eng, tok = o["e"], o["tok"]
+        writes = [r for r in o["w"] if r[0] in SCRATCH]
         if eng != "R":
-            need = needs(eng, o["r"], o["w"])
+            need = needs(eng, o["r"], writes)
             for s in sorted(need):
                 v = need[s]
                 if not any(s2 != s and need[s2] and snap[(s2, need[s2])].get(s, 0) >= v for s2 in need):
@@ -602,76 +686,29 @@ def rank_program(g, core, T, topo):
                         known[eng][s3] = max(known[eng].get(s3, 0), v3)
                 else:
                     need[s] = 0
-            for call in o["calls"]:
-                if tok:
-                    call()
-                else:
-                    count["e" + eng] += 1
-                    call().then_inc(T.sem["e" + eng], 1)
+        for call in o["calls"]:
+            if tok:
+                call()
+            else:
+                count["e" + eng] += 1
+                call().then_inc(T.sem["e" + eng], 1)
         who = eng if not tok else "D" + tok[0]
         tok = tok or ("e" + eng, count["e" + eng])
         snap[tok] = dict(known[eng])
         snap[tok][tok[0]] = tok[1]
-        for regs, w in ((o["r"], False), (o["w"], True)):
+        for regs, w in ((o["r"], False), (writes, True)):
             for name, lo, hi in regs:
                 keep = [x for x in acc.get(name, []) if not (lo <= x[2] and x[3] <= hi and (w or (x[0] == who and not x[4])))]
                 acc[name] = keep + [(who, tok, lo, hi, w)]
 
-    def cut(b, t):
-        lo, hi = 0, len(b)
-        while lo < hi:
-            m = (lo + hi) // 2
-            if b[m][0] <= t:
-                lo = m + 1
-            else:
-                hi = m
-        return lo
-
-    def lay(order, back):
-        at, busy = {}, {}
-        for i in order:
-            o = ops[i]
-            if back:
-                t = max([o["late"]] + [at[j] + ops[j]["d"] + ops[j]["pred"][i] + o["late"] for j in o["succ"]])
-            else:
-                t = max([0.0] + [at[j] + ops[j]["d"] + ops[j]["late"] + w for j, w in o["pred"].items()])
-            use = [] if o["e"] == "R" else [o["e"]] + sorted(set(r[0] for r in o["r"] + o["w"] if r[0] in BANKS))
-            moved = True
-            while moved:
-                moved = False
-                for r in use:
-                    b = busy.setdefault(r, [])
-                    for t0, t1, e in b[max(0, cut(b, t) - 2):]:
-                        pad = WAKE if e != o["e"] else 0.0
-                        if t0 - pad >= t + o["d"]:
-                            break
-                        if t1 + pad > t:
-                            t, moved = t1 + pad, True
-            for r in use:
-                busy[r].insert(cut(busy[r], t), (t, t + o["d"], o["e"]))
-            at[i] = t
-        return at
-
-    order = sorted(range(len(ops)), key=lambda i: (-ops[i]["way"], i))
-    best = None
-    for _ in range(PASSES):
-        at = lay(order, False)
-        end = max(at[i] + o["d"] + o["late"] for i, o in enumerate(ops))
-        if best is None or end < best[0]:
-            best = (end, at)
-        ta = lay(sorted(at, key=lambda i: (-at[i] - ops[i]["d"], -i)), True)
-        order = sorted(ta, key=lambda i: (-ta[i] - ops[i]["d"], i))
-    for i in sorted(best[1], key=lambda i: (best[1][i], i)):
-        issue(ops[i])
-
     g.sync.wait_ge(T.sem.yo, 16)
     for s in ("eV", "eP", "eS", "eG"):
         g.sync.wait_ge(T.sem[s], count[s])
-    for i in range(7):
+    for i in range(8):
         g.sync.wait_ge(T.sem["ld%d" % i], 16)
     for t in range(RO):
         for ps in CALLS:
             for k in "az":
                 g.sync.wait_ge(T.sem["l%s%d_%d" % (k, t, ps[0])], 8)
                 for p in ps:
-                    g.sync.wait_ge(T.sem["%s%d_%d" % (k, t, place[p])], 8 // len(ps))
+                    g.sync.wait_ge(T.sem["%s%d_%d" % (k, t, place[p])], engines(p))

@@ -1,18 +1,27 @@
+import math
 from concourse.bass import DstId, RemoteDMATransfer
 from concourse.mybir import dt, AluOpType, AxisListType, ActivationFunctionType
 
 N = 4
 RO = 3
-REG = 320
+REG = 256
+FAR = (((0, 64), (64, 64)), ((128, 128),))
 EPS = 2.0 ** -30
 BETA = 2.0 ** -12
-BYS = (2, 3, 5, 6, 7)
-MG = 2
+EVEN = [((64, "V"), (64, "S")), ((32, "V+"), (32, "G"), (64, "G"))]
+WAYS = {1: [((96, "V"), (32, "S"))] * 2, 2: EVEN, 3: [((64, "G"),), ((64, "G"),), ((64, "G"), (64, "G"))], 4: EVEN}
+TWO = {1: (96, 96), 2: (64, 64), 3: (64, 64), 4: (64, 64)}
+MG = 4
 BANKS = ["b%d" % b for b in range(8)]
-CY, PCY, WAKE, GA, SC = 0.83, 0.45, 120.0, 1.56, 3.8
-FIRST, LATE = 2500.0, 2500.0
-LAND = (2000.0, 2200.0, 2400.0, 6000.0, 7800.0, 9150.0, 9500.0, 11500.0)
-PASSES, TRIES, AGAIN = 4, 1500, 300
+CY, PCY, WAKE, GA, SC = 0.83, 0.43, 120.0, 1.45, 3.5
+PFIX, SFIX = 8.0, 140.0
+FIRST, LATE, ROW = 2500.0, 2000.0, 6.4
+LAND = (2000.0, 2200.0, 2400.0, 6000.0, 7800.0, 9150.0, 9500.0)
+CASES = ((0.95, 3.0, 1.3, 150.0), (1.7, 3.8, 1.05, 120.0))
+SLOW = ((1.2, 1.5), (1.0, 0.9))
+PASSES, TRIES, LONG, AGAIN = 3, (22000, 3, 24000, 8000, 8000), 16000, 500
+HOT, MILD, WARM, COLD = 300.0, 90.0, 80.0, 20.0
+SEED, PACK, RUN, PULL = 3, 300, 0.2, 0.2
 PLAN = {}
 
 F, B, H, I, U = "float32", "bfloat16", "float16", "int32", "uint16"
@@ -28,40 +37,45 @@ def _scratch():
             lo = s[big][1][1] if big in s else 0
             s[big] = ("sbuf", [128, lo + cols + -cols % 32], d)
             at[name] = (big, lo, cols)
-    sb("acts_i", 2048, I); sb("regs_s", 4384, B); sb("P", 4384, B); sb("who", 4128, B); sb("pay_s", 2048, B); sb("paym", 2048, B)
+    sb("acts_i", 2056, I); sb("regs_s", 4384, B); sb("P", 4384, B); sb("who", 4128, B); sb("pay_s", 2048, B); sb("paym", 2056, B)
+    sb("NN", 2056, F); sb("AH", 2048, H); sb("fl", 2048, B); sb("NR", 512, H); sb("T13", 128, B)
     sb("rch_s", 256, B); sb("n0_i", 16, I); sb("dr_i", 256, I); sb("w_i", 256, I)
-    sb("drb", 256, B); sb("wb", 512, B); sb("n0f", 16, F); sb("n0u", 16, U); sb("q0", 256, H); sb("TD1", 256, H)
-    sb("xr1", 4096, B); sb("xr", 4096, B); sb("W", 4096, B)
+    sb("drb", 256, B); sb("wb", 256, B); sb("n0u", 16, U); sb("TD1", 256, H)
+    sb("xr1", 4096, B); sb("xr", 4096, B); sb("W", 4096, B); sb("xz", 4096, B); sb("nil", 1040, B); sb("ms", 384, B)
+    for j in range(8):
+        sb("yT%d" % j, 128, B); sb("xT%d" % j, 128, B)
     for e in (1, 2, 3, 4):
-        sb("A%d" % e, 256, U); sb("Ah%d" % e, 256, H)
+        sb("A%d" % e, 256, U)
         for u in (0, 1):
             if e != 2:
                 sb("q%d_%d" % (e, u), 256, H); sb("L%d_%d" % (e, u), 16, U)
     sb("q2", 768, H); sb("L2", 32, U)
+    sb("Ly", 16, U); sb("Lz", 16, U)
     for u in (0, 1):
-        sb("TA%d" % u, 256, F); sb("nF%d" % u, 16, U); sb("vbF%d" % u, 256, F)
-    for n in ("y1", "y2", "y3", "y4", "y5", "yF", "lv", "zN", "NV", "NP", "zl", "HV", "HP", "ms", "fl", "aux1", "auxB", "ng", "lid", "found"):
+        sb("TA%d" % u, 256, H); sb("nF%d" % u, 16, U); sb("vbF%d" % u, 256, F)
+    for n in ("y1", "y3", "y5", "lv", "zN", "NV", "NP", "HR", "HV", "HP", "aux1", "auxB", "ng", "lid", "found"):
         sb(n, 256, B)
     sb("t1", 256, F); sb("ind", 256, H); sb("cum", 256, F); sb("o32", 16, F); sb("offw", 16, U)
     for t in range(RO):
-        sb("vb%d" % t, 512, F); sb("auxS%d" % t, 256, B); sb("land%d" % t, 512, B); sb("zr%d" % t, 1280, B); sb("send%d" % t, 1280, B)
+        sb("vb%d" % t, 512, F); sb("auxS%d" % t, 256, B); sb("land%d" % t, 512, B); sb("zr%d" % t, 1040, B); sb("send%d" % t, 2048, B)
     for n in ("h", "f"):
         sb("D" + n, 384, F); sb("Y" + n, 384, F); sb("eq" + n, 384, B); sb("lc" + n, 384, F); sb("off" + n, 16, U); sb("CM" + n, 384, B)
-    sb("Dm", 128, I); sb("Bm", 128, I); sb("pi", 2, I); sb("pk", 2, I); sb("rp", 256, I); sb("li", 64, I)
-    sb("crep", 64, U); sb("crep2", 24, U); sb("kf", 1, F); sb("pg", 1, F)
-    for n in ("BO", "ID", "E1", "E2", "E3", "OHM", "DST", "TRI", "ZM", "IDn", "I5", "In", "BO13", "N13", "D5", "Dn", "R13", "RN13", "M23", "DIF", "CW"):
+    sb("Bm", 128, I); sb("pi", 2, I); sb("pk", 2, I); sb("rp", 128, I); sb("li", 64, I)
+    sb("crep", 64, U); sb("crep16", 32, U); sb("crep2", 32, U); sb("crep48", 24, U); sb("kf", 1, F); sb("pg", 1, F)
+    for n in ("BO", "BO2", "BO8", "ID", "E1", "OHM", "DST", "TRI", "TRa", "TRb", "ZM", "IDn", "I5", "In", "M23", "DIF", "CW"):
         sb(n, 128, B)
-    sb("Z", 144, B); sb("ZN", 144, B); sb("Zs", 144, B); sb("CST", 512, B); sb("LC", 40, H)
-    sb("own", 16, F); sb("ownl", 16, F); sb("ID32", 128, F)
-    sb("cols", 16, F); sb("SR", 640, B); sb("SEL", 768, B); sb("ZT", 864, B)
-    sb("rd", 256, F); sb("ta", 16, F); sb("tb", 16, F); sb("MX", 256, B); sb("ONE", 256, B); sb("SIX", 256, B)
+    for n in ("Z", "Z2", "Zm", "ZN", "Zs"):
+        sb(n, 144, B)
+    sb("LC", 56, H); sb("own", 16, F); sb("ownl", 16, F); sb("ID32", 128, F)
+    sb("cols", 16, F); sb("SR", 640, B); sb("SEL", 768, B); sb("ZT", 864, B); sb("K0", 1024, B); sb("EX", 1024, B)
+    sb("rd", 16, F); sb("ta", 16, F); sb("tb", 16, F); sb("ONE", 256, B); sb("SIX", 256, B); sb("C16", 512, B)
     for b in BANKS:
         s[b] = ("psum", [128, 512], F)
     return s, at
 
 
 SCRATCH, AT = _scratch()
-SEMAPHORES = (["eV", "eP", "eS", "eG"] + ["ld%d" % i for i in range(8)] + ["yo"]
+SEMAPHORES = (["eV", "eP", "eS", "eG"] + ["ld%d" % i for i in range(22)] + ["yo"]
               + ["%s%d_%d" % (k, t, r) for k in ("a", "z", "la", "lz") for t in range(RO) for r in range(N)])
 
 
@@ -94,14 +108,16 @@ def rank_program(g, core, T, topo):
     def val(x):
         return x[0] if isinstance(x, tuple) else x
 
-    def put(eng, calls, reads, writes, dur, tok=None, late=0.0, after=()):
-        ops.append({"e": eng, "calls": calls, "r": reads, "w": writes, "d": dur, "tok": tok, "late": late, "after": dict(after), "round": now[0]})
+    def put(eng, calls, reads, writes, dur, tok=None, late=0.0, after=(), gathered=0, scattered=0):
+        ds = [f * (dur + (gathered * ga + scattered * sc) * CY) for ga, sc, f, _ in CASES]
+        dur += (gathered * GA + scattered * SC) * CY
+        ops.append({"ds": ds, "e": eng, "calls": calls, "r": reads, "w": writes, "d": dur, "tok": tok, "late": late, "after": dict(after), "round": now[0]})
         return len(ops) - 1
 
     def vop(call, out, ins, n, wide=1.0):
         x = [i for i in ins if i[3]]
-        d = x[0][2] * GA * CY if x else out[2] * SC * CY if out[3] else max(64.0, n * wide) * CY
-        put("V", [call], regs_of(*ins), out[1], 50.0 + d)
+        put("V", [call], regs_of(*ins), out[1], 50.0 + (0.0 if x or out[3] else max(64.0, n * wide) * CY),
+            gathered=x[0][2] if x else 0, scattered=out[2] if out[3] else 0)
 
     def ts(out, in0, s1, op0, s2=None, op1=None):
         if op1 is None:
@@ -132,27 +148,29 @@ def rank_program(g, core, T, topo):
             f = lambda: g.scalar.activation(out[0], in_[0], ACT.Copy, scale=scale)
         else:
             f = lambda: g.scalar.activation(out[0], in_[0], func, bias=bias, scale=scale)
-        put("S", [f], regs_of(in_), out[1], 65.0 + in_[2] * GA * CY if in_[3] else 120.0 + in_[2] * CY)
+        put("S", [f], regs_of(in_), out[1], 65.0 if in_[3] else SFIX + in_[2] * CY, gathered=in_[2] * in_[3])
 
-    def mm(*terms, start=True, stop=True, turn=()):
+    def mm(*terms, start=True, stop=True, free=False):
         for k0 in range(0, len(terms), MG):
             part = list(enumerate(terms))[k0:k0 + MG]
             calls = [lambda k=k, x=x: g.tensor.matmul(x[0][0], x[1][0], x[2][0], start and k == 0, stop and k == len(terms) - 1) for k, x in part]
-            put("P", calls, [r for k, x in part for r in regs_of(x[1], x[2])],
-                [r for k, x in part for r in x[0][1]] + [("turn" + terms[0][0][1][0][0], 0, 1)] + list(turn),
-                sum(15.0 + max(64, x[2][2]) * PCY * (1 if narrow(x[2]) else 4) for k, x in part))
+            turn = [("turn" + terms[0][0][1][0][0], 0, 1)]
+            put("P", calls, [r for k, x in part for r in regs_of(x[1], x[2])] + turn * free,
+                [r for k, x in part for r in x[0][1]] + turn * (not free),
+                sum(PFIX + max(64, x[2][2]) * PCY * (1 if narrow(x[2]) else 4) for k, x in part))
 
     def iota(out, pattern, base, ch):
-        put("G", [lambda: g.iota(out[0], pattern, base, ch, allow_small_or_imprecise_dtypes=narrow(out))], [], out[1], 130.0 + 2 * out[2] * CY)
+        put("G", [lambda: g.iota(out[0], pattern, base, ch, allow_small_or_imprecise_dtypes=SCRATCH[out[1][0][0]][2] != I)], [], out[1], 130.0 + 2 * out[2] * CY)
 
     def zeros(out):
         iota(out, [[0, out[2]]], 0, 0)
 
-    def sel(out, in_, pattern, base, ch):
-        put("G", [lambda: g.affine_select(out[0], in_[0], pattern, OP.is_equal, 0.0, base, ch)], regs_of(in_), out[1], 170.0 + 2 * out[2] * CY)
+    def sel(out, in_, pattern, base, ch, op=OP.is_equal, other=0.0):
+        put("G", [lambda: g.affine_select(out[0], in_[0], pattern, op, other, base, ch)], regs_of(in_), out[1], 170.0 + 2 * out[2] * CY)
 
     def load(k, eng, out, src):
-        put(eng, [lambda: queue[eng].dma_start(out[0], src).then_inc(T.sem["ld%d" % k], 16)], [], out[1] + [("turn" + eng, 0, 1)], 100.0, ("ld%d" % k, 16), LAND[k])
+        put(eng, [lambda: queue[eng].dma_start(out[0], src).then_inc(T.sem["ld%d" % k], 16)], [], out[1] + [("turn" + eng, 0, 1)], 100.0, ("ld%d" % k, 16),
+            LAND[k] if k < 7 else LAND[6] + 1800.0 * (k - 6))
 
     def send(to, sem, lsem, also=()):
         trs = []
@@ -163,7 +181,7 @@ def rank_program(g, core, T, topo):
             trs.append(RemoteDMATransfer(dst_ids=[DstId(rid=rid, pnc=pid)], dma_engine_mask=sum(1 << x for x in eng[n * k:n * k + n]),
                                          remote_sem=T.sem[sem], src=src[0], dst=dst))
         return put("G", [lambda: g.remote_dma_fused(trs, local_sem=T.sem[lsem])], regs_of(*[x[1] for x in to]) + list(also), [],
-                   500.0 + FIRST * (lsem == "la0_1"), (lsem, 8), LATE)
+                   500.0 + FIRST * (lsem == "la0_1"), (lsem, 8), LATE + ROW * len(to) * to[0][1][2])
 
     def arrives(kind, t, p, region, like):
         put("R", [], [], region[1], 0.0, ("%s%d_%d" % (kind, t, place[p]), engines(p)), 0.0, {like: WAKE})
@@ -185,12 +203,11 @@ def rank_program(g, core, T, topo):
     load(0, "Y", a("n0_i"), T.n0[:])
     load(1, "S", a("rch_s"), T.rch[:])
     load(2, "S", a("dr_i", rows=96), T.dr[:, :])
-    load(3, "Y", a("acts_i"), T.acts[:])
+    load(3, "Y", a("acts_i", 0, 2048), T.acts[:])
     parts = ((0, 2048), (2048, 3584), (3584, 4096))
     for k, (lo, hi) in enumerate(parts):
         load(4 + k, "Y", a("regs_s", lo, hi), T.regs[:, lo:hi])
         ts(a("P", lo, hi), a("regs_s", lo, hi), 0.0, OP.max)
-    load(7, "Y", a("pay_s"), T.pay[:])
 
     kf = a("kf")
     def col(j):
@@ -201,12 +218,14 @@ def rank_program(g, core, T, topo):
     iota(a("li"), [[1, 64]], 0, 0)
     iota(a("pi"), [[0, 2]], 0, 1)
     iota(a("Bm"), [[1, 8], [0, 16]], 0, 0)
-    iota(a("rp"), [[0, 16], [1, 16]], 0, 0)
-    iota(a("Dm"), [[1, 128]], 0, -1)
+    iota(a("rp", 0, 128), [[0, 8], [1, 16]], 0, 0)
     iota(a("lid"), [[1, 256]], 1, 0)
     fill(a("ONE"), 1.0)
     fill(a("SIX"), 0.0625)
+    fill(a("C16", 0, 256, rows=1), 0.0)
+    fill(a("C16", 256, 512, rows=1), 16.0)
     cp(a("crep"), a("li"))
+    ts(a("crep16"), a("li", 0, 32), 16.0, OP.mult)
     ts(a("pk", 0, 1), a("pi", 0, 1), 15, OP.bitwise_and)
     ts(a("pk", 1, 2), a("pi", 1, 2), 4, OP.arith_shift_right)
     cp(a("kf"), a("pk", 0, 1))
@@ -214,92 +233,119 @@ def rank_program(g, core, T, topo):
     ts(a("BO"), a("Bm"), a("pg"), OP.is_equal)
     fill(a("Z"), 0.0)
     cp(a("Z", 15, 143, 16), a("BO", 0, 128, 16))
-    ts(a("rd"), a("rp"), kf, OP.subtract)
-    ts(a("MX"), a("rd"), 0.0, OP.is_equal)
-    ts(a("TRI"), a("Dm"), 0, OP.is_ge, 64.0, OP.mult)
-    tt(a("TRI"), a("TRI"), a("BO"), OP.mult)
-    fill(a("TRI", 15, 128, 16), 0.0)
+    fill(a("nil"), 0.0)
+    ts(a("TRI"), a("Bm"), a("pg"), OP.is_equal, 64.0, OP.mult)
+    sel(a("TRI"), a("TRI"), [[1, 128]], 0, -1, OP.is_ge)
+    zeros(a("TRI", 15, 128, 16))
+    ts(col(0), kf, 8.0, OP.is_lt)
+    ts(a("BO8"), a("BO"), col(0), OP.mult)
+    for n, k in (("TRa", 0), ("TRb", 8)):
+        ts(a(n), a("BO8"), 64.0, OP.mult)
+        sel(a(n), a(n), [[1, 128]], -k, -1, OP.is_ge)
+        zeros(a(n, 15, 128, 16))
     for j in range(6):
         sel(a("SEL", 128 * j, 128 * j + 128, rows=96), a("ONE", 0, 128, rows=96), [[-12, 8], [0, 16]], -home_te[j], 1)
     sel(a("ID"), a("ONE", 0, 128), [[-1, 128]], 0, 1)
-    sel(a("E1"), a("BO"), [[1, 128]], -1, -1)
-    sel(a("E3"), a("BO"), [[1, 128]], 15, -1)
-    sel(a("DIF"), a("BO"), [[1, 128]], 1, -1)
-    sel(a("D5"), a("BO"), [[1, 128]], -15, -1)
-    zeros(a("DST"))
-    ts(col(0), kf, 15.0, OP.is_lt)
-    tt(a("E1"), a("E1"), a("E3"), OP.add)
-    ts(a("E2"), a("ID"), col(0), OP.mult)
-    tt(a("OHM"), a("E1"), a("E2"), OP.subtract)
-    tt(a("DIF"), a("DIF"), a("D5"), OP.add)
-    tt(a("DIF"), a("DIF"), a("E2"), OP.subtract)
-    for out, src, c in (("D5", "DIF", 5.0), ("Dn", "DIF", -2048.0), ("I5", "ID", 5.0), ("IDn", "ID", -1.0), ("In", "ID", -2048.0),
-                        ("BO13", "BO", 13.0), ("ID32", "ID", 1.0), ("ZM", "ID", 16.0), ("Zs", "Z", -2.0 ** -12)):
+
+    def entry(n, c, row, value, src=None):
+        sel(a(n, c, c + 113, 16), src or a("nil", 0, 8), [[-16, 8]], -row, 1, OP.not_equal, value)
+    for n, side in (("OHM", -1), ("DIF", 1)):
+        sel(a(n), a("nil", 0, 128), [[1, 128]], side, -1, OP.not_equal, 1.0)
+        sel(a(n), a(n), [[1, 128]], 0, -1, OP.not_equal, -1.0)
+    entry("OHM", 0, 0, -1.0)
+    entry("OHM", 0, 15, 1.0, a("OHM", 0, 113, 16))
+    entry("OHM", 15, 14, 1.0)
+    entry("DIF", 15, 0, 1.0)
+    for out, src, c in (("I5", "ID", 5.0), ("IDn", "ID", -1.0), ("In", "ID", -2048.0), ("Zm", "Z", -1.0), ("Z2", "Z", 2.0)):
         ts(a(out), a(src), c, OP.mult)
-    ts(a("R13"), a("Z", 0, 128), 13.0, OP.mult)
-    tt(a("ZM"), a("BO"), a("ZM"), OP.subtract)
-    fill(a("CST", rows=64), 0.0)
-    for e, step, c in ((1, 16, 274432.0), (2, 1, 274432.0), (3, 16, 274432.0), (4, 1, 272384.0)):
-        fill(a("CST", 128 * (e - 1) + step - 1, 128 * e, step, rows=1), c)
-        fill(a("CST", 128 * (e - 1) + step - 1, 128 * e, step, rows=1, row=32), float(e))
-    fill(a("LC"), 0.0)
-    fill(a("LC", 24, 32), -2048.0)
+    fill(a("T13", rows=1), 13.0)
+    iota(a("NR", rows=1), [[1, 512]], 0, 0)
+    for lo, hi, c in ((0, 8, 1.0), (16, 40, 0.0), (24, 32, -2048.0), (40, 48, 3.0)):
+        fill(a("LC", lo, hi), c)
     ts(col(1), kf, 16.0, OP.mult, -1.0, OP.add)
-    ts(a("LC", 8, 16), a("li", 0, 8), 256.0, OP.mult, col(1), OP.add)
+    for c in (8, 48):
+        ts(a("LC", c, c + 8), a("li", 0, 8), 256.0, OP.mult, col(1), OP.add)
     ts(a("CW", rows=1), a("rp", 0, 128, rows=1), 0.5, OP.add, -EPS, OP.mult)
     fill(a("CW", 15, 128, 16, rows=1), EPS)
     cp(a("n0u"), a("n0_i"))
-    cp(a("n0f"), a("n0_i"))
-    tt(a("q0"), via(a("n0f"), a("crep", 0, 16)), a("MX"), OP.mult)
-    for u in range(4):
-        act(a("xr1", 1024 * u, 1024 * u + 1024), via(a("rch_s", 64 * u, 64 * u + 64), a("crep", 0, 64)))
+    l = 0
+    for n, way in WAYS[1][0] + WAYS[1][1]:
+        if way == "V":
+            for j in range(l, l + n, 48):
+                m = min(48, l + n - j)
+                act(a("xr1", 16 * j, 16 * (j + m)), via(a("rch_s", j, j + m), a("crep", 0, m)))
+        else:
+            mm((a("b%d" % (l // 128), 0, 128, rows=n), a("rch_s", l, l + n), a("ID")))
+            cp(a("xT%d" % (l // 32), rows=n), a("b%d" % (l // 128), 0, 128, rows=n))
+        l += n
     cp(a("drb", rows=96), a("dr_i", rows=96))
     ts(a("w_i", rows=96), a("dr_i", rows=96), 15, OP.bitwise_and)
-    cp(a("wb", 0, 256, rows=96), a("w_i", rows=96))
-    ts(a("wb", 256, 512, rows=96), a("w_i", rows=96), EPS, OP.mult)
+    ts(a("wb", rows=96), a("w_i", rows=96), EPS, OP.mult)
     ts(a("y1"), a("rch_s"), -1.0, OP.add)
-    tt(a("DST", 0, 116), a("OHM", 0, 116), a("OHM", 4, 120), OP.add)
-    tt(a("E1", 0, 116), a("OHM", 8, 124), a("OHM", 12, 128), OP.add)
-    ts(a("E3"), a("rp", 0, 128), 4, OP.is_lt)
-    tt(a("DST", 0, 116), a("DST", 0, 116), a("E1", 0, 116), OP.add)
-    tt(a("DST", 0, 116), a("DST", 0, 116), a("E3", 0, 116), OP.mult)
+    zeros(a("DST", 112, 128))
+    tt(a("E1", 0, 124), a("OHM", 0, 124), a("OHM", 4, 128), OP.add)
+    tt(a("DST", 0, 116), a("E1", 0, 116), a("E1", 8, 124), OP.add)
+    sel(a("DST"), a("DST"), [[0, 8], [-1, 16]], 3, 0, OP.is_ge)
     ts(col(4), kf, float(REG), OP.mult, -1.0, OP.add)
-    ts(col(5), kf, float(REG), OP.mult, 64.0, OP.add)
-    ts(col(2), kf, 4096.0, OP.add)
-    ts(col(3), kf, 4112.0, OP.add)
-    zeros(a("ZT"))
+    fill(a("ZT"), 0.0)
     for j in range(6):
         sel(a("ZT", 144 * j + 15, 144 * j + 143, 16, rows=96), a("ONE", 0, 8, rows=96), [[-12, 8]], -far_te[j], 1)
-    ts(col(7), kf, 2.0, OP.is_equal)
-    ts(col(8), kf, 3.0, OP.is_equal)
-    tt(col(8), col(7), col(8), OP.add)
-    for out, src in (("ZN", "Z"), ("N13", "BO13"), ("RN13", "R13")):
-        ts(a(out), a(src), col(8), OP.mult)
-    ts(a("M23"), a("Z", 12, 140), col(7), OP.mult)
-    tt(a("M23"), a("ID"), a("M23"), OP.subtract)
-    for j, (row, w) in enumerate(((0, 1.0), (1, 1.0), (5, EPS), (6, EPS), (4, -8192.0))):
-        ts(col(9 + j), kf, float(row), OP.is_equal, w, OP.mult)
-        ts(a("SR", 128 * j, 128 * j + 128), a("BO"), col(9 + j), OP.mult)
-    ts(a("ta"), a("rd", 0, 16), 0.0, OP.is_gt, 16384.0, OP.mult)
-    ts(a("tb"), a("rd", 0, 16), 0.0, OP.is_equal, -8192.0, OP.mult)
-    tt(a("ta"), a("ta"), a("tb"), OP.add)
-    for n, c in (("h", 2048.0), ("f", 10240.0)):
-        fill(a("CM" + n, 16, 32), c)
-        ts(a("CM" + n, 0, 16), a("ta"), c, OP.add)
-        ts(a("CM" + n, 32, 48), a("ta"), c, OP.add)
-        for c in (48, 96, 192):
-            cp(a("CM" + n, c, 2 * c), a("CM" + n, 0, c))
-        fill(a("D" + n), 0.0)
-        fill(a("D" + n, 0, 384, 48), -4.0)
-        fill(a("D" + n, 16, 384, 48), -4.0)
-    for j, c in enumerate((15.0, 47.0, 47.0)):
-        ts(a("crep2", j, 24, 3), a("li", 0, 8), 48.0, OP.mult, c, OP.add)
-    ts(a("ownl"), a("li", 0, 16), 16.0, OP.mult, kf, OP.add)
-    ts(a("own"), a("ownl"), 4128.0, OP.add, 2.0 ** -21, OP.mult)
-    ts(a("ownl"), a("ownl"), 1.0, OP.add, 2.0 ** -8, OP.mult)
-    act(a("paym"), a("pay_s"), ACT.Identity, bias=-1.0)
-    zeros(a("send0"))
-    zeros(a("zr0"))
+    sel(a("M23"), a("ONE", 0, 128), [[-1, 128]], 0, 1)
+    entry("M23", 3, 2, -1.0, a("ID", 3, 116, 16))
+    zeros(a("ZN"))
+    entry("ZN", 15, 2, 1.0)
+    entry("ZN", 15, 3, 1.0, a("ZN", 15, 128, 16))
+    for j, (row, w) in enumerate(((0, 1.0), (1, 1.0), (5, 1.0), (6, 1.0), (4, -8192.0))):
+        sel(a("SR", 128 * j, 128 * j + 128), a("nil", 0, 128), [[-16, 8], [0, 16]], -row, 1, OP.not_equal, w)
+    sel(a("ZM"), a("BO"), [[-1, 128]], 0, 1, OP.not_equal, -15.0)
+    for n in "hf":
+        zeros(a("D" + n))
+        for c in (0, 16):
+            iota(a("D" + n, c, 384, 48), [[0, 8]], -4, 0)
+    iota(a("K0"), [[0, 64], [16, 16]], 1, 0)
+    for j in range(4):
+        sel(a("EX", 256 * j, 256 * j + 256, rows=64), a("ONE", rows=64), [[-1, 16], [0, 16]], -16 * j, 1)
+
+    def later(after):
+        first = len(ops)
+        ts(col(5), kf, float(REG), OP.mult, 64.0, OP.add)
+        ts(col(2), kf, 4096.0, OP.add)
+        ts(col(3), kf, 4112.0, OP.add)
+        ts(a("rd", 0, 16), a("rp", 0, 16), kf, OP.subtract)
+        ts(a("ta"), a("rd", 0, 16), 0.0, OP.is_gt, 16384.0, OP.mult)
+        ts(a("tb"), a("rd", 0, 16), 0.0, OP.is_equal, -8192.0, OP.mult)
+        tt(a("ta"), a("ta"), a("tb"), OP.add)
+        for n, c in (("h", 2048.0), ("f", 10240.0)):
+            fill(a("CM" + n, 16, 32), c)
+            ts(a("CM" + n, 0, 16), a("ta"), c, OP.add)
+            ts(a("CM" + n, 32, 48), a("ta"), c, OP.add)
+            for c in (48, 96, 192):
+                cp(a("CM" + n, c, 2 * c), a("CM" + n, 0, c))
+        for j, c in enumerate((15.0, 47.0, 47.0)):
+            ts(a("crep48", j, 24, 3), a("li", 0, 8), 48.0, OP.mult, c, OP.add)
+        ts(a("ownl"), a("li", 0, 16), 16.0, OP.mult, kf, OP.add)
+        ts(a("own"), a("ownl"), 4128.0, OP.add, 2.0 ** -21, OP.mult)
+        ts(a("ownl"), a("ownl"), 1.0, OP.add, 2.0 ** -8, OP.mult)
+        ts(a("ID32"), a("ID"), 1.0, OP.mult)
+        ts(a("BO2"), a("BO"), 2.0, OP.mult)
+        ts(a("crep2"), a("li", 0, 32), 2.0, OP.mult, 1.0, OP.add)
+        ts(a("Zs"), a("Z"), -2.0 ** -12, OP.mult)
+        cp(a("paym", 2048, 2056), a("paym", 0, 8))
+        for o in ops[first:]:
+            o["after"][after] = 0.0
+    for c in (0, 2048):
+        act(a("xz", c, c + 1024), a("nil", 0, 1024))
+    hop = [[a("send%d" % t, 0, 1024), a("send%d" % t, 1024, 2048), a("zr%d" % t)] for t in range(RO)]
+    blank = [a("xz", 3072, 4096)] + hop[0] + [a("who", 1032 * j, 1032 * j + 1032) for j in range(4)] + [a("pay_s")] + hop[1] + hop[2]
+    for k, x in enumerate(blank):
+        if k == 8:
+            load(7 + k, "Y", x, T.pay[:])
+        else:
+            load(7 + k, "Y", x, a("nil", 0, x[2])[0])
+            ops[-1]["r"] = [("nil", 0, 1040)]
+    for j in range(4):
+        act(a("paym", 512 * j, 512 * j + 512), a("pay_s", 512 * j, 512 * j + 512), ACT.Identity, bias=-1.0)
+
 
     def draws(t):
         for j in (0, 1):
@@ -309,82 +355,143 @@ def rank_program(g, core, T, topo):
         grp = []
         for src, j, row in (("drb", 0, 0), ("drb", 1, 1), ("wb", 0, 5), ("wb", 1, 6)):
             s = 144 * (2 * t + j) + 15 - row
-            grp.append((a("b5", 256, 512), a("ZT", s, s + 128, rows=96), a(src, 0, 256, rows=96)))
-        mm(*(grp + [(a("b5", 256, 512), a("Z", 11, 139), a("SIX"))]))
-        act(a("auxS%d" % t), a("b5", 256, 512))
+            grp.append((a("b7", 256, 512), a("ZT", s, s + 128, rows=96), a(src, 0, 256, rows=96)))
+        mm(*(grp + [(a("b7", 256, 512), a("Z", 11, 139), a("SIX"))]))
+        act(a("auxS%d" % t), a("b7", 256, 512))
 
-    def lists(out, src, n, first=(), z="Z"):
+    def lists(out, src, n, first=(), z="Z", step=1):
         name, lo = src
-        mm(*(list(first) + [(out, a(z, 15 - r, 143 - r), a(name, lo + r, lo + n, 16)) for r in range(16)]))
+        mm(*(list(first) + [(out, a(z, 15 - r, 143 - r), a(name, lo + step * r, lo + n, 16 * step)) for r in range(16)]))
 
     def acts_at(e, lo, hi, nodes):
         cp(a("A%d" % e, lo, hi), via(a("acts_i"), nodes))
 
-    def next_nodes(e, u, node_terms):
-        lo, hi, y = 128 * u, 128 * u + 128, "b%d" % (2 + u)
-        ah = a("Ah%d" % e, lo, hi)
-        ts(ah, a("A%d" % e, lo, hi), -2048.0, OP.add)
-        odd = e % 2
-        c = 256 if (e, u) == (2, 1) else 128
-        mm((a(y, 0, 128), a("I5"), ah), *[(a(y, c0, c1), a(m), x) for c0, c1, m, _, x in node_terms])
-        act(a("fl", lo, hi), a(y, 0, 128), ACT.Identity, bias=129.0 + (10240.0 + e - 1023.5) / 2048.0, scale=2.0 ** -11)
-        mm((a(y, c, c + 128), a("D5" if odd else "I5"), ah), *([(a(y, c + c0, c + c1), a(m2 if odd else m), x) for c0, c1, m, m2, x in node_terms]
-           + [(a(y, c, c + 128), a("CST", 128 * e - 128, 128 * e, rows=64), a("ONE", 0, 128, rows=64)),
-              (a(y, c, c + 128), a("Dn" if odd else "In"), a("fl", lo, hi))]))
-        if not odd:
-            mm((a(y, 384 - c, 512 - c), a("ID"), ah))
-            act(a("TA%d" % u), a(y, 128, 384))
-
-    def pieces(lo, n):
-        return [x for l in range(lo, lo + n, 32) for x in (((l, 16), (l + 16, 16)) if l % 128 == 0 else ((l, 32),))]
-
-    def spread(win, lo, n):
-        name, w0, _ = win[1][0]
-        for l, c in pieces(lo, n):
-            act(a("xr", 16 * l, 16 * (l + c)), via(a(name, w0 + l - lo, w0 + l - lo + c), a("crep", 0, c)), ACT.Identity, bias=1.0)
-
-    def weights(e, u, l0):
-        for j, n in (pieces(l0, 64) if e > 1 else ((l0, 32), (l0 + 32, 32))):
-            w, x = a("W", 16 * j, 16 * (j + n)), a("xr1" if e == 1 else "xr", 16 * j, 16 * (j + n))
-            p = via(a("P", 0, 4096), a("A%d" % e, j, j + n))
-            if e == 1 and j // 32 in BYS:
-                b = a("b%d" % (6 + BYS.index(j // 32) % 2))
-                act(w, p)
-                mm((b, a("ID"), x))
-                tt(w, b, w, OP.min)
+    def node_table():
+        for j in range(4):
+            lo, hi, b = 512 * j, 512 * j + 512, a("b%d" % (4, 5, 2, 3)[j])
+            ts(a("AH", lo, hi), a("acts_i", lo, hi), -2048.0, OP.add)
+            u = [(b, a("I5"), a("AH", lo, hi)), (b, a("T13", rows=1), a("NR", rows=1))]
+            mm(*u)
+            act(a("fl", lo, hi), b, ACT.Identity, bias=129.0 + (10240.0 + 6656 * j - 1023.5) / 2048.0, scale=2.0 ** -11)
+            mm(*(u + [(b, a("In"), a("fl", lo, hi))]))
+            if j > 1:
+                ts(a("NN", lo, hi), b, 274432.0 + 6656 * j, OP.add)
             else:
-                tt(w, p, x, OP.min)
-            ops[-1]["w"] = ops[-1]["w"] + [("turnV", 0, 1)]
-        c = l0 - 128 * u
-        mm(*[(a("b%d" % u, c, c + 64), a("Z", 15 - k, 143 - k), a("W", 16 * l0 + k, 16 * l0 + 1024, 16)) for k in range(16)], turn=[("turnP", 0, 1)])
+                act(a("NN", lo, hi), b, ACT.Identity, bias=274432.0 + 6656 * j)
+        for n in ("NN", "acts_i"):
+            cp(a(n, 2048, 2056), a(n, 0, 8))
+
+    def next_nodes(e, u, nodes):
+        ta, c = "TA%d" % u, 128 * ((e, u) == (2, 0))
+        if e % 2:
+            act(a(ta, 0, 128), via(a("NN"), nodes))
+            mm((a("b%d" % (2 + u), 128, 256), a("DIF"), a(ta, 0, 128)))
+        else:
+            act(a(ta, c, c + 128), via(a("NN"), nodes), ACT.Identity, bias=e - 2048.0)
+            half = e / 4.0
+            act(a(ta, 128 - c, 256 - c), via(a("acts_i"), nodes), ACT.Identity, bias=-2048.0 * half, scale=half)
+
+    def yz(lo, hi):
+        return a("xz", 16 * lo, 16 * hi - 15, 16)
+
+    def weights(e, u, l0, n, way, y, last, lead):
+        c, x, yT = l0 - 128 * u, "b%d" % u, "%sT%d" % ("xy"[e > 1], l0 // 32)
+        y = y or yz(l0, l0 + n)
+        out = a(x, c, c + n)
+        if e > 1 and way == "V":
+            scan(a("xr", 16 * l0, 16 * (l0 + n)), a("K0", 0, 16 * n), a("xz", 16 * l0, 16 * (l0 + n)), 1.0, OP.min, OP.add)
+        elif e > 1 and way == "G":
+            name, w0, w1 = y[1][0]
+            st, w0 = (16, w0) if name == "xz" else (2, w0 - 1)
+            for l, m in [x for l in range(0, n, 32) for x in (((l, 16), (l + 16, 16)) if (l0 + l) % 128 == 0 else ((l, 32),))]:
+                act(a("xr", 16 * (l0 + l), 16 * (l0 + l + m)), via(a(name, w0 + st * l, w0 + st * (l + m)), a("crep%d" % st, 0, m)), ACT.Identity, bias=1.0)
+        elif e > 1:
+            z = a("b%d" % (4 + u), 128, 256, rows=n)
+            mm((z, y, a("ID")))
+            act(a(yT, rows=n), z, ACT.Identity, bias=1.0)
+        for j, m in [x for l in range(l0, l0 + n, 32) for x in (((l, 16), (l + 16, 16)) if l % 128 == 0 and way == "G" else ((l, 32),))]:
+            w, xr = a("W", 16 * j, 16 * (j + m)), a("xr1" if e == 1 else "xr", 16 * j, 16 * (j + m))
+            p = via(a("P", 0, 4096), a("A%d" % e, j, j + m))
+            if way in "VG":
+                tt(w, p, xr, OP.min)
+                ops[-1]["w"] = ops[-1]["w"] + [("turnV", 0, 1)]
+            else:
+                b = a("b%d" % (6 + (j // 32 + (e > 1 or u)) % 2), 0, 16 * m)
+                if e == 1 and now[0] == 0:
+                    act(w, via(a("regs_s", 0, 4096), a("A1", j, j + m)), ACT.Relu)
+                else:
+                    act(w, p)
+                ops[-1]["w"] = ops[-1]["w"] + [("turnS", 0, 1)]
+                mm((b, a(yT, rows=n), a("EX", 16 * (j - l0), 16 * (j - l0 + m), rows=n)), stop=False)
+                mm((b, a("IDn"), w), start=False)
+                act(a("xr", 16 * j, 16 * (j + m)), b, ACT.Relu)
+        two = c >= TWO[e][u]
+        if way == "S":
+            for o in (a(x, wide(e, u, c), wide(e, u, c + n), 2), a(x, wide(e, u, c) + 1, wide(e, u, c + n), 2)) if two else (out,):
+                mm((o, a("BO"), a("rch_s", l0, l0 + n) if e == 1 else y), start=False, stop=False, free=True)
+        z, src = ("Zm", "xr") if way == "S" else ("Z", "W")
+        if lead < 0:
+            return
+        l0, n, c = l0 - lead, n + lead, c - lead
+        first = len(ops)
+        if two:
+            groups = [[(a(x, wide(e, u, c + j), wide(e, u, c + j + 32)), a(z, 15 - k, 143 - k), a(src, 16 * (l0 + j) + k, 16 * (l0 + j + 32), 8)) for k in range(8)]
+                      for j in range(0, n, 32)]
+        else:
+            groups = [[(a(x, c, c + n), a(z, 15 - k, 143 - k), a(src, 16 * l0 + k, 16 * (l0 + n), 16)) for k in range(16)]]
+        end = groups[-1].pop() if last else None
+        for terms in groups:
+            mm(*terms, start=False, stop=False, free=True)
+        for o in ops[first:]:
+            o["r"] = o["r"] + [("turnP", 0, 1)]
+        if last:
+            mm(end, start=False)
+            ops[-1]["w"] = ops[-1]["w"] + [("turnP", 0, 1)]
+
+    def wide(e, u, c):
+        return c + max(0, c - TWO[e][u])
+
+    def unit(e, u, l0=None, ways=None, y=None):
+        l0, ways = (128 * u, WAYS[e][u]) if ways is None else (l0, ways)
+        c, n, x = l0 - 128 * u, sum(w[0] for w in ways), "b%d" % u
+        lo, hi = wide(e, u, c), wide(e, u, c + n)
+        v = wide(e, u, c + sum(w[0] for w in ways if w[1] != "S")) - lo if e > 1 else 256
+        mm((a(x, lo, hi), a("ONE", 0, 128, rows=1), a("C16", 256 - v, 256 - v + hi - lo, rows=1)), stop=False)
+        l, lead = l0, 0
+        for m, way in ways:
+            weights(e, u, l, m, way[0], y and y(l - l0, m), l + m == l0 + n, -1 if way[1:] else lead)
+            l, lead = l + m, lead + m if way[1:] else 0
 
     def choose(e, t, u, aux=None):
         lo, hi = 128 * u, 128 * u + 128
         x, y, z, q, L = "b%d" % u, "b%d" % (2 + u), "b%d" % (4 + u), "q%d_%d" % (e, u), "L%d_%d" % (e, u)
         if e < 3:
             vb = a("vb%d" % t, 256 * (e - 1) + lo, 256 * (e - 1) + hi)
-            mod16 = [(a(y, 384, 512), a("SEL", 256 * t + 128 * e - 128, 256 * t + 128 * e, rows=96), a("wb", 256 + lo, 256 + hi, rows=96))]
+            mod16 = [(a(y, 384, 512), a("SEL", 256 * t + 128 * e - 128, 256 * t + 128 * e, rows=96), a("wb", lo, hi, rows=96))]
         else:
             vb = a("vbF%d" % u, 128 * (e - 3), 128 * (e - 2))
-            mod16 = [(a(y, 384 + 64 * h, 448 + 64 * h), a("SR", 128 * e - 128, 128 * e), aux(2 * u + h)) for h in (0, 1)]
+            mod16 = [(a(y, 384 + l - lo, 384 + l - lo + n), a("SR", 128 * e - 128, 128 * e), aux(l, n)) for l, n in FAR[u]]
         odd = e % 2
         ind = a(q, 128, 256) if odd else a("ind", lo, hi)
-        act(a("ms", lo, hi), a(x, 0, 128))
+        c, m = TWO[e][u], 192 * u
+        act(a("ms", m, m + 256 - c), a(x, 0, 256 - c))
         mm((a(y, 384, 512), a("CW", rows=1), a("ONE", 0, 128, rows=1)), *mod16, stop=False)
-        mm((a(y, 384, 512), a("BO"), a("ms", lo, hi)), start=False)
-        mm((a(x, 256, 384), a("TRI"), a("ms", lo, hi)))
+        halves = [a("ms", m + c + h, m + 256 - c, 2) for h in (0, 1)] * (c < 128)
+        mm((a(y, 384, 384 + c), a("BO"), a("ms", m, m + c)), *[(a(y, 384 + c, 512), a("BO8"), h) for h in halves], start=False)
+        mm((a(x, 256, 256 + c), a("TRI"), a("ms", m, m + c)))
+        if halves:
+            mm((a(x, 256 + c, 384), a("TRa"), halves[0]), (a(x, 256 + c, 384), a("TRb"), halves[1]))
         tt(a("t1", lo, hi), a(y, 384, 512), vb, OP.mult)
         tt(ind, a(x, 256, 384), a("t1", lo, hi), OP.is_lt)
-        yin = a("yF" if e == 3 else "y%d" % e, lo, hi)
-        yout = a("y%d" % (e + 1), lo, hi)
+        yin = a("y1", lo, hi) if e == 1 else yz(lo, hi)
+        yout = yz(lo, hi) if odd else a("y%d" % (e + 1), lo, hi)
         if odd:
             tt(a(q, 0, 128), a(y, 128, 256), ind, OP.mult)
-            lists(a(z, 0, 16), (q, 0), 256, [(a(z, 0, 16), a("ID"), a("LC", 0, 16))])
+            lists(a(z, 0, 16), (q, 0), 256, [(a(z, 0, 16), a("ID"), a("LC", 20 * e - 20, 20 * e - 4))])
             cp(a(L), a(z, 0, 16))
-            tt(yout, via(a("W", 16 * lo, 16 * hi), a(L, 8, 16)), yin, OP.min)
             acts_at(e + 1, lo, hi, a(L, 0, 8))
-            spread(yout, lo, 128)
-            next_nodes(e + 1, u, [(0, 128, "BO13", "R13", a(q, 0, 128))])
+            tt(yout, via(a("W", 16 * lo, 16 * hi), a(L, 8, 16)), yin, OP.min)
+            next_nodes(e + 1, u, a(L, 0, 8))
             return
         if e == 2:
             mm((a(z, 128, 256), a("DST"), ind))
@@ -396,15 +503,16 @@ def rank_program(g, core, T, topo):
             ts(a(L), a(z, 0, 16), 2048.0, OP.add)
             c, rec = 8, a(L, 8, 16)
         else:
-            nodes = a("q2", 640 * u, 640 * u + 128)
+            nodes = a("q2", 256 + lo, 256 + hi)
             scan(a("cum", lo, hi), a("ONE", lo, hi), a(z, 128, 256), col(4) if u == 0 else a("cum", lo - 1, lo))
-            tt(a("q2", 256 + lo, 256 + hi), a(z, 128, 256), a("cum", lo, hi), OP.mult)
-            tt(a("q2", 512 * u, 512 * u + 256), a(x, 128, 384), a("TA%d" % u), OP.mult)
+            tt(a("q2", 640 * u, 640 * u + 128), a(z, 128, 256), a("cum", lo, hi), OP.mult)
+            tt(a("q2", 128 + 256 * u, 384 + 256 * u), a(x, 128, 384), a("TA%d" % u), OP.mult)
             mm((a(y, 0, 128), a("ID"), a("auxS%d" % t, lo, hi)), (a(y, 0, 128), a("Z", 13, 141), nodes))
             act(a("aux1", lo, hi), a(y, 0, 128))
-            lists(a(z, 0, 16), ("q2", 128 + 256 * u), 256, [(a(z, 0, 16), a("ID"), a("LC", 16 + 8 * u, 32 + 8 * u))])
+            lists(a(z, 0, 16), ("q2", 512 * u), 256, [(a(z, 0, 16), a("ID"), a("LC", 24 - 8 * u, 40 - 8 * u))], z="Z2")
             ts(a("L2", 16 * u, 16 * u + 16), a(z, 0, 16), 2048.0, OP.add)
-            c, rec = 8 * u, a("L2", 24 * u, 24 * u + 8)
+            ts(a("Ly", 8 * u, 8 * u + 8), a(z, 8 * u, 8 * u + 8), 2049.0, OP.add)
+            c, rec = 8 - 8 * u, a("L2", 8 + 8 * u, 16 + 8 * u)
         for j in (0, 1):
             act(a("D" + "hf"[e // 4], 192 * u + 15 + 32 * j, 192 * u + 192, 48), a(z, c + j, c + 8, 2), ACT.Identity, bias=2.0 ** -10, scale=2.0 ** -21)
         tt(yout, via(a("P", 0, 4096), rec), yin, OP.min)
@@ -414,15 +522,17 @@ def rank_program(g, core, T, topo):
 
     def first_of(n, b, j0, j1, dead, alive, rec):
         lo, hi = 48 * j0, 48 * j1
-        terms = [(a(b, lo, hi), a("ID"), a("CM" + n, lo, hi))]
-        for m, x in ((dead, alive), (a("BO"), rec)):
+        at = a(b, 128, 128 + hi - lo)
+        terms = [(at, a("ID"), a("CM" + n, lo, hi))]
+        for m, x in ((dead, alive), (a("BO2" if n == "h" else "BO"), rec)):
             for j in range(j0, j1):
-                terms += [(a(b, 48 * j, 48 * j + 16), m, x(32 * j, 16)), (a(b, 48 * j + 16, 48 * j + 48), m, x(32 * j, 32))]
+                c = 128 + 48 * (j - j0)
+                terms += [(a(b, c, c + 16), m, x(32 * j, 16)), (a(b, c + 16, c + 48), m, x(32 * j, 32))]
         mm(*terms[:1], stop=False)
         mm(*terms[1:], start=False)
         off = "offf" if n == "f" else "offw"
-        act(a("Y" + n, lo, hi), via(a("D" + n, lo, hi), a("crep2", 0, (hi - lo) // 16)), scale=2.0 ** 21)
-        tt(a("eq" + n, lo, hi), a(b, lo, hi), a("Y" + n, lo, hi), OP.is_equal)
+        act(a("Y" + n, lo, hi), via(a("D" + n, lo, hi), a("crep48", 0, (hi - lo) // 16)), scale=2.0 ** 21)
+        tt(a("eq" + n, lo, hi), at, a("Y" + n, lo, hi), OP.is_equal)
         scan(a("lc" + n, lo, hi), a("D" + n, lo, hi), a("eq" + n, lo, hi), 0.0, OP.add, OP.max)
         ts(a(off, 2 * j0, 2 * j1, 2), a("lc" + n, lo + 15, hi, 48), 2.0 ** 21, OP.mult, col(2), OP.min)
         ts(a(off, 2 * j0 + 1, 2 * j1, 2), a("lc" + n, lo + 47, hi, 48), 2.0 ** 21, OP.mult, col(3), OP.min)
@@ -434,70 +544,67 @@ def rank_program(g, core, T, topo):
     def first_of_all():
         change("offw", range(7, -1, -1), "lid", "who")
         act(a("found"), via(a("who"), a("offw")))
-        lists(a("b4", 32, 48), ("found", 0), 256, [(a("b4", 32, 48), a("ID32"), a("ownl")), (a("b4", 32, 48, 2), a("ID32"), a("lch", 15, 384, 48)),
-                                                   (a("b4", 33, 48, 2), a("ID32"), a("lch", 47, 384, 48))], z="Zs")
-        tt(a("o32"), a("b4", 32, 48), a("own"), OP.min)
+        lists(a("b7", 32, 48), ("found", 0), 256, [(a("b7", 32, 48), a("ID32"), a("ownl")), (a("b7", 32, 48, 2), a("ID32"), a("lch", 15, 384, 48)),
+                                                   (a("b7", 33, 48, 2), a("ID32"), a("lch", 47, 384, 48))], z="Zs")
+        tt(a("o32"), a("b7", 32, 48), a("own"), OP.min)
         ts(a("offh"), a("o32"), 2.0 ** 21, OP.mult)
 
     draws(0)
-    for u in (0, 1):
-        acts_at(1, 128 * u, 128 * u + 128, a("n0u", 8 * u, 8 * u + 8))
-        next_nodes(1, u, [(0, 128, "BO13", "R13", a("q0", 128 * u, 128 * u + 128))])
-        cp(a("TD1", 128 * u, 128 * u + 128), a("b%d" % (2 + u), 128, 256))
+    node_table()
+    cp(a("A1"), via(a("acts_i", 0, 2048), a("n0u")))
+    act(a("TD1"), via(a("NN", 0, 2048), a("n0u")))
     for t in range(RO):
         more = t + 1 < RO
         land, zr, out = "land%d" % t, "zr%d" % t, "send%d" % t
         for e in (1, 2):
             for u in (0, 1):
-                if e == 1 and t:
-                    mm((a("b%d" % (2 + u), 128, 256), a("ID"), a("TD1", 128 * u, 128 * u + 128)))
-                weights(e, u, 128 * u)
-                weights(e, u, 128 * u + 64)
+                if e == 1:
+                    mm((a("b%d" % (2 + u), 128, 256), a("DIF"), a("TD1", 128 * u, 128 * u + 128)))
+                unit(e, u)
                 choose(e, t, u)
         for u in (0, 1):
-            scatter(a(out, 0, 1216), a("L2", 8 + 8 * u, 16 + 8 * u), a("auxB", 128 * u, 128 * u + 128))
-        scatter(a(out, 64, 1280), a("L2", 8, 24), a("y3"))
+            scatter(a(out), a("L2", 24 * u, 24 * u + 8), a("auxB", 128 * u, 128 * u + 128))
+            scatter(a(out), a("Ly", 8 * u, 8 * u + 8), a("y3", 128 * u, 128 * u + 128))
+        if t == 0:
+            later(len(ops) - 1)
         for ps in CALLS:
-            o = send([(place[p], a(out, REG * place[p], REG * place[p] + 128), T[land][:, 128 * there(p):128 * there(p) + 128]) for p in ps],
-                     "a%d_%d" % (t, me), "la%d_%d" % (t, ps[0]), [(zr, 0, 1280)])
+            o = send([(place[p], a(out, 2 * REG * place[p], 2 * REG * place[p] + 128), T[land][:, 128 * there(p):128 * there(p) + 128]) for p in ps],
+                     "a%d_%d" % (t, me), "la%d_%d" % (t, ps[0]), [(zr, 0, 1040)])
             for p in ps:
                 arrives("a", t, p, a(land, 128 * p, 128 * p + 128), o)
-        for x in [a("who", 1032 * j, 1032 * j + 1032) for j in range(4)] * (t == 0) + ([a("send%d" % (t + 1)), a("zr%d" % (t + 1))] if more else []):
-            zeros(x)
-            ops[-1]["after"][o] = -LATE
-        ts(a("ng"), a("q2", 256, 512), col(5), OP.is_ge, 8192.0, OP.mult)
-        first_of("h", "b7", 0, 8, a("BO"), lambda l, n: a("ng", l, l + n), lambda l, n: a("q2", 128 + l + 256 * (l // 128), 128 + l + 256 * (l // 128) + n))
-
-        def aux(p, lo=0, hi=64):
-            name, s = (out, REG * me) if p == 0 else (land, 128 * p)
-            return a(name, s + lo, s + hi)
+        ts(a("Lz"), a("Ly"), -1.0, OP.add, 0.5, OP.mult)
+        ops[-1]["after"][o] = -ops[o]["late"]
         for u in (0, 1):
-            z, m, nF = "b%d" % (4 + u), "b%d" % (6 + u), "nF%d" % u
-            if u == 1:
-                lists(a(z, 0, 12), (land, 256), 192, z="ZN")
-                cp(a(nF, 0, 12), a(z, 0, 12))
-            for h in (0, 1):
-                p = 2 * u + h
-                if u == 0:
-                    lists(a(z, 8 * h, 8 * h + 4), aux(p)[1][0][:2], 64, z="ZN")
-                    cp(a(nF, 8 * h, 8 * h + 4), a(z, 8 * h, 8 * h + 4))
-                acts_at(3, 64 * p, 64 * p + 64, a(nF, 8 * h, 8 * h + 4))
-                spread(aux(p, 64, 128), 64 * p, 64)
+            ts(a("ng", 128 * u, 128 * u + 128), a("q2", 640 * u, 640 * u + 128), col(5), OP.is_ge, 8192.0, OP.mult)
+        for u in (0, 1):
+            first_of("h", "b%d" % u, 4 * u, 4 * u + 4, a("BO"), lambda l, n: a("ng", l, l + n), lambda l, n: a("q2", 128 + l + 256 * (l // 128), 128 + l + 256 * (l // 128) + n))
+
+        def aux(l, n, odd=0):
+            name, s = (out, 2 * REG * me + 2 * l + odd) if l < 64 else (land, 2 * l + odd)
+            return a(name, s, s + 2 * n - 1, 2)
+        for u in (0, 1):
+            z, m, nF = "b%d" % (4 + u), "b%d" % (2 + u), "nF%d" % u
+            for k, (l, n) in enumerate(FAR[u]):
+                c = l % 128 // 16
+                lists(a(z, c, c + n // 16), aux(l, n)[1][0][:2], 2 * n, z="ZN", step=2)
+                ts(a(nF, c, c + n // 16), a(z, c, c + n // 16), 2048.0, OP.add)
+                acts_at(3, l, l + n, a(nF, c, c + n // 16))
+                sel(yz(l, l + n), aux(l, n, 1), [[0, n]], 0, 0)
+                ops[-1]["after"][o] = -ops[o]["late"]
+                unit(3, u, l, WAYS[3][2 * u + k], lambda j, n: aux(l + j, n, 1))
+            for l, n in FAR[u]:
                 for j in (0, 1):
-                    mm((a(m, 128 * j + 64 * h, 128 * j + 64 * h + 64), a("SR", 128 * j, 128 * j + 128), aux(p)))
-                sel(a("yF", 64 * p, 64 * p + 64), aux(p, 64, 128), [[0, 64]], 0, 0)
-                weights(3, u, 64 * p)
+                    mm((a(m, 128 * j + l % 128, 128 * j + l % 128 + n), a("SR", 128 * j, 128 * j + 128), aux(l, n)))
             act(a("vbF%d" % u), a(m, 0, 256), ACT.Identity, bias=BETA)
-            next_nodes(3, u, [(64 * h, 64 * h + 64, "N13", "RN13", aux(2 * u + h)) for h in (0, 1)])
+            next_nodes(3, u, a(nF, 0, 8))
             choose(3, t, u, aux)
         for u in (0, 1):
             lo, hi, x, y, L = 128 * u, 128 * u + 128, "b%d" % u, "b%d" % (2 + u), "L4_%d" % u
-            weights(4, u, lo)
-            weights(4, u, lo + 64)
+            unit(4, u)
             choose(4, t, u, aux)
             tt(a("lv", lo, hi), via(a("paym"), a(L, 0, 8)), a("y5", lo, hi), OP.min)
             mm((a(x, 0, 128), a("ZM"), a("lv", lo, hi)))
-            ts(a("zN", lo, hi), a(x, 0, 128), 1.0, OP.min, -1.0, OP.max)
+            act(a("zN", lo, hi), a(x, 0, 128), ACT.Sign)
             ps = CALLS[u]
             o = send([(place[p], a("zN", 64 * p, 64 * p + 64), T[zr][:, REG * me:REG * me + 64]) for p in ps], "z%d_%d" % (t, me), "lz%d_%d" % (t, ps[0]))
             for p in ps:
@@ -508,26 +615,29 @@ def rank_program(g, core, T, topo):
             mm((a(y, 384, 512), a("ID"), a("NV", lo, hi)), (a(y, 384, 512), a("IDn"), a("zN", lo, hi)))
             ts(a("NV", lo, hi), a(y, 384, 512), 15.0, OP.min, -15.0, OP.max)
             if more:
-                act(a("NP", lo, hi), a("NV", lo, hi), ACT.Relu)
-            first_of("f", "b%d" % (6 + u), 4 * u, 4 * u + 4, a("SR", 512, 640), lambda l, n: aux(l // 64, l % 64, l % 64 + n),
+                act(a("NP", lo, hi), a(y, 384, 512), ACT.Relu)
+            first_of("f", "b%d" % (4 + u), 4 * u, 4 * u + 4, a("SR", 512, 640), aux,
                      lambda l, n: a("q4_%d" % (l // 128), 128 + l % 128, 128 + l % 128 + n))
         first_of_all()
         if more:
+            first = len(ops)
             draws(t + 1)
+            for x in ops[first:]:
+                x["after"][o] = -ops[o]["late"] - 500.0
         blocks = [2 * place.index(r) + c for r in (3, 2, 1, 0) for c in (1, 0)]
         change("offf", blocks, "NV", "regs_s")
         if more:
             change("offf", blocks, "NP", "P")
-        act(a("zl"), via(a(zr), a("L2", 8, 24)))
-        for u in (1, 0):
-            tt(a("HV", 128 * u, 128 * u + 128), via(a("regs_s", 0, 4096), a("L2", 24 * u, 24 * u + 8)), a("zl", 128 * u, 128 * u + 128), OP.add)
+        act(a("HR"), via(a("regs_s", 0, 4096), a("L2", 8, 24)))
+        tt(a("HV"), via(a(zr), a("Lz")), a("HR"), OP.add)
         if more:
             ts(a("HP"), a("HV"), 15.0, OP.min, 0.0, OP.max)
             scatter(a("P"), a("offh"), a("HP"))
             ends.append(len(ops) - 1)
             now[0] += 1
         ts(a("HV"), a("HV"), 15.0, OP.min, -15.0, OP.max)
-        scatter(a("regs_s"), a("offh"), a("HV"))
+        for lo, hi in ((0, 8), (8, 16)) if more else ((0, 16),):
+            scatter(a("regs_s"), a("offh", lo, hi), a("HV", 16 * lo, 16 * hi))
     ends.append(put("Y", [lambda: g.sync.dma_start(T.yr[:], T.regs_s[:, 0:4096]).then_inc(T.sem.yo, 16)], [("regs_s", 0, 4384)], [], 100.0, ("yo", 16), 8000.0))
 
     seen = {}
@@ -543,6 +653,8 @@ def rank_program(g, core, T, topo):
             for name, lo, hi in regs:
                 seen[name] = [x for x in seen.get(name, []) if not (w and lo <= x[1] and x[2] <= hi)] + [(i, lo, hi, w)]
         o["in"], o["out"] = {j: ops[j]["d"] + ops[j]["late"] + w for j, w in pred.items()}, {}
+        o["ins"] = [{j: ops[j]["ds"][c] + (ops[j]["late"] * SLOW[c][ops[j]["e"] == "G"] + x[3] if w == WAKE else ops[j]["late"] + w) for j, w in pred.items()}
+                    for c, x in enumerate(CASES)]
         o["use"] = [] if o["e"] == "R" else [o["e"]] + sorted(set(r[0] for r in o["r"] + o["w"] if r[0] in BANKS))
         for j, w in pred.items():
             ops[j]["out"][i] = o["d"] + ops[j]["late"] + w
@@ -585,73 +697,152 @@ def rank_program(g, core, T, topo):
             k[i] = max([key[i]] + [k[j] + 0.001 for j in ops[i]["in"] if j in k])
         return sorted(part, key=lambda i: (k[i], i))
 
-    def blockers(part, at, i):
-        before, last, pairs = {}, {}, []
-        for j in sorted(part, key=lambda j: at[j]):
-            before[j], last[ops[j]["e"]] = last.get(ops[j]["e"]), j
-        while i in before:
-            c = [(round(at[j] + w), 1, j) for j, w in ops[i]["in"].items()]
-            j = before[i]
-            if j is not None and ops[i]["use"]:
-                c.append((round(at[j] + ops[j]["d"]), 0, j))
-            if not c:
-                break
-            _, dep, j = max(c)
-            if not dep and j not in ops[i]["in"]:
-                pairs.append((j, i))
-            i = j
-        return pairs
-
-    seed = [1]
+    seed = [SEED]
     def chance(lo, hi):
         seed[0] = (seed[0] * 1103515245 + 12345) % 2147483648
         return lo + (hi - lo) * seed[0] / 2147483648.0
 
+    def improve(part, end, tries, hot):
+        n, idx, cases = len(part), {i: k for k, i in enumerate(part)}, range(len(CASES))
+        base = [[max([0.0] + [past[c][j] + w for j, w in ops[i]["ins"][c].items() if j not in idx]) for i in part] for c in cases]
+        pred = [[[(idx[j], w) for j, w in ops[i]["ins"][c].items() if j in idx] for i in part] for c in cases]
+        before, after = [set(j for j, w in p) for p in pred[0]], [[idx[j] for j in ops[i]["out"] if j in idx] for i in part]
+        use, eng = [[NAMES.index(r) for r in ops[i]["use"]] for i in part], [ops[i]["e"] for i in part]
+        dur, end = [[ops[i]["ds"][c] for i in part] for c in cases], idx[end]
+
+        def times(c, seq, old=None, lo=0):
+            if old:
+                at, why, marks = old[0][:], old[1][:], old[4][:lo // 32 + 1]
+            else:
+                at, why, marks = [0.0] * n, [-1] * n, [(ready[c], [-1] * len(NAMES))]
+            free, last = marks[-1][0][:], marks[-1][1][:]
+            b, p, d, wake = base[c], pred[c], dur[c], CASES[c][3]
+            for lo in range(32 * len(marks) - 32, n, 32):
+                for k in seq[lo:lo + 32]:
+                    t, y, e, u = b[k], -1, eng[k], use[k]
+                    for j, w in p[k]:
+                        w += at[j]
+                        if w > t:
+                            t, y = w, j
+                    for r in u:
+                        j = last[r]
+                        x = free[r] if j < 0 or eng[j] == e else free[r] + wake
+                        if x > t:
+                            t, y = x, j
+                    at[k], why[k] = t, y
+                    t += d[k]
+                    for r in u:
+                        free[r], last[r] = t, k
+                marks.append((free[:], last[:]))
+            return at, why, free, max((at[end], end), *[(free[r] + x, last[r]) for r, x in ((1, 600.0), (2, -d[end]), (3, -3000.0)) if last[r] >= 0]), marks
+
+        def worth(x):
+            return sum((y[3][0] + PULL * sum(y[0]) / n) / z for y, z in zip(x, scale))
+        seq = best = list(range(n))
+        cur = [times(c, seq) for c in cases]
+        scale = [len(CASES) * (x[3][0] - ready[c][0]) / 45000.0 for c, x in enumerate(cur)]
+        now = least = worth(cur)
+        for m in range(tries):
+            _, why, _, (_, k), _ = cur[m % len(CASES)]
+            pairs = []
+            while why[k] >= 0:
+                if why[k] not in before[k]:
+                    pairs.append((why[k], k))
+                k = why[k]
+            if not pairs:
+                break
+            x = y = int(chance(0, len(pairs)))
+            if chance(0, 1) < RUN:
+                while x and pairs[x - 1][0] == pairs[x][1] and chance(0, 1) < 0.8:
+                    x -= 1
+                while y + 1 < len(pairs) and pairs[y + 1][1] == pairs[y][0] and chance(0, 1) < 0.8:
+                    y += 1
+            j, i = pairs[y][0], pairs[x][1]
+            lo, hi, far = seq.index(j), seq.index(i), int(chance(1, 30)) * (chance(0, 1) < 0.3)
+            if chance(0, 1) < 0.5:
+                lo, move = max(0, lo - far), {i}
+                for k in reversed(seq[lo:hi + 1]):
+                    if k in move:
+                        move.update(before[k])
+                if j in move:
+                    continue
+                new = [k for k in seq[lo:hi + 1] if k in move] + [k for k in seq[lo:hi + 1] if k not in move]
+            else:
+                hi, move = min(n - 1, hi + far), {j}
+                for k in seq[lo:hi + 1]:
+                    if k in move:
+                        move.update(after[k])
+                if i in move:
+                    continue
+                new = [k for k in seq[lo:hi + 1] if k not in move] + [k for k in seq[lo:hi + 1] if k in move]
+            new = seq[:lo] + new + seq[hi + 1:]
+            if m % PACK == 0:
+                at = lay([part[k] for k in seq], dict(past[0]), {r: [(-1e7, ready[0][k], "")] for k, r in enumerate(NAMES)})
+                new, lo = sorted(seq, key=lambda k: at[part[k]]), 0
+            x = [times(c, new, cur[c], lo) for c in cases]
+            w = worth(x)
+            if w - now <= -hot * (COLD / hot) ** (m / tries) * math.log(chance(1e-9, 1)):
+                cur, now, seq = x, w, new
+                if m % 16 == 0:
+                    seq = sorted(new, key=lambda k: x[0][0][k])
+                    cur = [times(c, seq) for c in cases]
+                if now < least:
+                    least, best = now, seq
+        return least, [part[k] for k in best], [times(c, best) for c in cases], part
+
     def idle():
         return {r: [] for r in list("VPSGY") + BANKS}
 
-    done, busy = {}, idle()
-    for t in range(RO):
-        part = [i for i, o in enumerate(ops) if o["round"] == t]
-        def trial(order):
-            b = {r: list(x) for r, x in busy.items()}
-            at = lay(order, dict(done), b)
-            return at[ends[t]], at, b
+    def laid(part, end):
+        order, best = sorted(part, key=lambda i: (-ops[i]["way"], i)), None
+        for _ in range(PASSES):
+            at = lay(order, {}, idle())
+            if best is None or at[end] < best[end]:
+                best = at
+            ta = lay(sorted(part, key=lambda i: (-at[i] - ops[i]["d"], -i)), {}, idle(), True)
+            order = sorted(part, key=lambda i: (-ta[i] - ops[i]["d"], i))
+        return best
+
+    seen = {}
+    for o in ops:
+        n, lo, _ = (o["w"] or o["r"])[0]
+        for m in ("vb%d", "auxS%d"):
+            for t in range(RO):
+                if n == AT[m % t][0] and 0 <= lo - AT[m % t][1] < AT[m % t][2]:
+                    n, lo = m, 0
+        x = o["e"], n[:-1] if n[:-1] in ("send", "land", "zr") else n, lo
+        seen[o["round"], x] = seen.get((o["round"], x), 0) + 1
+        o["name"] = x, seen[o["round"], x]
+    for o in ops:
+        if o["round"] == 0:
+            x, k = o["name"]
+            o["name"] = x, k - seen[0, x] + seen.get((1, x), 0)
+    rounds = [[i for i, o in enumerate(ops) if o["round"] == t] for t in range(RO)]
+    NAMES = list("VPSGY") + BANKS
+    past, ready, calls = [{} for c in CASES], [[0.0] * len(NAMES) for c in CASES], []
+    if not PLAN:
+        past = [{i: -1e6 for i in rounds[0]} for c in CASES]
+        at = laid(rounds[1], ends[1])
+        x = min(improve(sorted(rounds[1], key=lambda i: (at[i], i)), ends[1], TRIES[0], HOT) for _ in range(TRIES[1]))
+        x = improve(x[1], ends[1], LONG, MILD)
+        PLAN["model"] = {ops[i]["name"]: x[2][0][0][k] - x[2][0][3][0] for k, i in enumerate(x[3])}
+        PLAN["worth"] = [y[3][0] for y in x[2]]
+        past = [{} for c in CASES]
+    for t, part in enumerate(rounds):
         if t in PLAN:
-            best, tries = trial(in_order(part, PLAN[t])), AGAIN
+            at, tries = PLAN[t], AGAIN
         else:
-            order, best, tries = sorted(part, key=lambda i: (-ops[i]["way"], i)), None, TRIES
-            for _ in range(PASSES):
-                x = trial(order)
-                if best is None or x[0] < best[0]:
-                    best = x
-                ta = lay(sorted(part, key=lambda i: (-x[1][i] - ops[i]["d"], -i)), {}, idle(), True)
-                order = sorted(part, key=lambda i: (-ta[i] - ops[i]["d"], i))
-        while tries > 0:
-            at = best[1]
-            pairs = blockers(part, at, ends[t])
-            if not pairs:
-                break
-            for _ in range(8):
-                j, i = pairs[int(chance(0, len(pairs)))]
-                key = {k: at[k] for k in part}
-                kind = int(chance(0, 3))
-                k, key_k = ((i, at[j] - 1.0), (j, at[j] - chance(300, 3000)), (j, at[i] + chance(1, 1500)))[kind]
-                key[k], up = key_k, [k]
-                while up:
-                    k = up.pop()
-                    for p in ops[k]["in"]:
-                        if p in key and key[p] > key[k]:
-                            key[p] = key[k] - 0.01
-                            up.append(p)
-                x = trial(in_order(part, key))
-                tries -= 1
-                if x[0] <= best[0] + 1.0:
-                    best = x
-                    break
-        PLAN.setdefault(t, {k: best[1][k] for k in part})
-        done = best[1]
-        busy = {r: [x for x in b if x[1] > best[0] - 6000.0] for r, b in best[2].items()}
+            at, tries, like = laid(part, ends[t]), TRIES[2 + t], PLAN["model"]
+            shift = min(at[i] - like[ops[i]["name"]] for i in part if ops[i]["name"] in like and ops[i]["w"][:1] == [("W", 0, 512)])
+            at = {i: like[ops[i]["name"]] + shift if ops[i]["name"] in like else at[i] for i in part}
+        x = improve(in_order(part, at), ends[t], tries, WARM)
+        for c, y in enumerate(x[2]):
+            past[c].update(zip(x[3], y[0]))
+            ready[c] = y[2]
+        if t == 1 and t not in PLAN:
+            PLAN["model"] = {ops[i]["name"]: past[0][i] for i in part}
+        PLAN.setdefault(t, {i: past[0][i] for i in part})
+        calls += x[1]
 
     count = {"eV": 0, "eP": 0, "eS": 0, "eG": 0}
     known = {e: {} for e in "VPSGYR"}
@@ -672,7 +863,7 @@ def rank_program(g, core, T, topo):
                         need[tok[0]] = tok[1]
         return need
 
-    for i in sorted(done, key=lambda i: (done[i], i)):
+    for i in calls:
         o = ops[i]
         eng, tok = o["e"], o["tok"]
         writes = [r for r in o["w"] if r[0] in SCRATCH]
@@ -704,8 +895,9 @@ def rank_program(g, core, T, topo):
     g.sync.wait_ge(T.sem.yo, 16)
     for s in ("eV", "eP", "eS", "eG"):
         g.sync.wait_ge(T.sem[s], count[s])
-    for i in range(8):
-        g.sync.wait_ge(T.sem["ld%d" % i], 16)
+    for o in ops:
+        if o["tok"] and o["tok"][0][:2] == "ld":
+            g.sync.wait_ge(T.sem[o["tok"][0]], 16)
     for t in range(RO):
         for ps in CALLS:
             for k in "az":

import math
from concourse.bass import DstId, RemoteDMATransfer
from concourse.mybir import dt, AluOpType, AxisListType, ActivationFunctionType

N = 4
RO = 3
REG = 256
FAR = (((0, 64), (64, 64)), ((128, 128),))
EPS = 2.0 ** -30
BETA = 2.0 ** -12
EVEN = [((64, "V"), (64, "S")), ((32, "V+"), (32, "G"), (64, "G"))]
WAYS = {1: [((96, "V"), (32, "S"))] * 2, 2: EVEN, 3: [((64, "G"),), ((64, "G"),), ((64, "G"), (64, "G"))], 4: EVEN}
TWO = {1: (96, 96), 2: (64, 64), 3: (64, 64), 4: (64, 64)}
MG = 4
BANKS = ["b%d" % b for b in range(8)]
CY, PCY, WAKE, GA, SC = 0.83, 0.43, 120.0, 1.45, 3.5
PFIX, SFIX = 8.0, 140.0
FIRST, LATE, ROW = 2500.0, 2000.0, 6.4
LAND = (2000.0, 2200.0, 2400.0, 6000.0, 7800.0, 9150.0, 9500.0)
CASES = ((0.95, 3.0, 1.3, 150.0), (1.7, 3.8, 1.05, 120.0))
SLOW = ((1.2, 1.5), (1.0, 0.9))
PASSES, TRIES, LONG, AGAIN = 3, (22000, 3, 24000, 8000, 8000), 16000, 500
HOT, MILD, WARM, COLD = 300.0, 90.0, 80.0, 20.0
SEED, PACK, RUN, PULL = 3, 300, 0.2, 0.2
PLAN = {}

F, B, H, I, U = "float32", "bfloat16", "float16", "int32", "uint16"


def _scratch():
    s, at = {}, {}
    def sb(name, cols, d):
        if cols > 1024 or name in ("rch_s", "n0_i", "dr_i") or name[:4] == "land":
            s[name] = ("sbuf", [128, cols], d)
        else:
            big = "p" + d
            lo = s[big][1][1] if big in s else 0
            s[big] = ("sbuf", [128, lo + cols + -cols % 32], d)
            at[name] = (big, lo, cols)
    sb("acts_i", 2056, I); sb("regs_s", 4384, B); sb("P", 4384, B); sb("who", 4128, B); sb("pay_s", 2048, B); sb("paym", 2056, B)
    sb("NN", 2056, F); sb("AH", 2048, H); sb("fl", 2048, B); sb("NR", 512, H); sb("T13", 128, B)
    sb("rch_s", 256, B); sb("n0_i", 16, I); sb("dr_i", 256, I); sb("w_i", 256, I)
    sb("drb", 256, B); sb("wb", 256, B); sb("n0u", 16, U); sb("TD1", 256, H)
    sb("xr1", 4096, B); sb("xr", 4096, B); sb("W", 4096, B); sb("xz", 4096, B); sb("nil", 1040, B); sb("ms", 384, B)
    for j in range(8):
        sb("yT%d" % j, 128, B); sb("xT%d" % j, 128, B)
    for e in (1, 2, 3, 4):
        sb("A%d" % e, 256, U)
        for u in (0, 1):
            if e != 2:
                sb("q%d_%d" % (e, u), 256, H); sb("L%d_%d" % (e, u), 16, U)
    sb("q2", 768, H); sb("L2", 32, U)
    sb("Ly", 16, U); sb("Lz", 16, U)
    for u in (0, 1):
        sb("TA%d" % u, 256, H); sb("nF%d" % u, 16, U); sb("vbF%d" % u, 256, F)
    for n in ("y1", "y3", "y5", "lv", "zN", "NV", "NP", "HR", "HV", "HP", "aux1", "auxB", "ng", "lid", "found"):
        sb(n, 256, B)
    sb("t1", 256, F); sb("ind", 256, H); sb("cum", 256, F); sb("o32", 16, F); sb("offw", 16, U)
    for t in range(RO):
        sb("vb%d" % t, 512, F); sb("auxS%d" % t, 256, B); sb("land%d" % t, 512, B); sb("zr%d" % t, 1040, B); sb("send%d" % t, 2048, B)
    for n in ("h", "f"):
        sb("D" + n, 384, F); sb("Y" + n, 384, F); sb("eq" + n, 384, B); sb("lc" + n, 384, F); sb("off" + n, 16, U); sb("CM" + n, 384, B)
    sb("Bm", 128, I); sb("pi", 2, I); sb("pk", 2, I); sb("rp", 128, I); sb("li", 64, I)
    sb("crep", 64, U); sb("crep16", 32, U); sb("crep2", 32, U); sb("crep48", 24, U); sb("kf", 1, F); sb("pg", 1, F)
    for n in ("BO", "BO2", "BO8", "ID", "E1", "OHM", "DST", "TRI", "TRa", "TRb", "ZM", "IDn", "I5", "In", "M23", "DIF", "CW"):
        sb(n, 128, B)
    for n in ("Z", "Z2", "Zm", "ZN", "Zs"):
        sb(n, 144, B)
    sb("LC", 56, H); sb("own", 16, F); sb("ownl", 16, F); sb("ID32", 128, F)
    sb("cols", 16, F); sb("SR", 640, B); sb("SEL", 768, B); sb("ZT", 864, B); sb("K0", 1024, B); sb("EX", 1024, B)
    sb("rd", 16, F); sb("ta", 16, F); sb("tb", 16, F); sb("ONE", 256, B); sb("SIX", 256, B); sb("C16", 512, B)
    for b in BANKS:
        s[b] = ("psum", [128, 512], F)
    return s, at


SCRATCH, AT = _scratch()
SEMAPHORES = (["eV", "eP", "eS", "eG"] + ["ld%d" % i for i in range(22)] + ["yo"]
              + ["%s%d_%d" % (k, t, r) for k in ("a", "z", "la", "lz") for t in range(RO) for r in range(N)])


def rank_program(g, core, T, topo):
    me = T.rank_of(core)
    if me is None:
        return
    OP, ACT = AluOpType, ActivationFunctionType
    queue = {"V": g.vector, "P": g.tensor, "S": g.scalar, "G": g, "Y": g.sync}
    ops, now, ends = [], [0], []

    def a(name, lo=None, hi=None, step=1, rows=128, row=0):
        name, base, cols = AT.get(name, (name, 0, 0))
        t = T[name]
        if lo is None:
            lo, hi = 0, cols or SCRATCH[name][1][1]
        lo, hi = base + lo, base + hi
        ap = t[row:row + rows, lo:hi] if step == 1 else t[row:row + rows, lo:hi:step]
        return ap, [(name, lo, hi)], (hi - lo + step - 1) // step, 0

    def via(win, off):
        return win[0].indirect(off[0]), win[1] + off[1], 16 * off[2], 1

    def narrow(x):
        return SCRATCH[x[1][0][0]][2] in (B, U, H)

    def regs_of(*xs):
        return [r for x in xs if isinstance(x, tuple) for r in x[1]]

    def val(x):
        return x[0] if isinstance(x, tuple) else x

    def put(eng, calls, reads, writes, dur, tok=None, late=0.0, after=(), gathered=0, scattered=0):
        ds = [f * (dur + (gathered * ga + scattered * sc) * CY) for ga, sc, f, _ in CASES]
        dur += (gathered * GA + scattered * SC) * CY
        ops.append({"ds": ds, "e": eng, "calls": calls, "r": reads, "w": writes, "d": dur, "tok": tok, "late": late, "after": dict(after), "round": now[0]})
        return len(ops) - 1

    def vop(call, out, ins, n, wide=1.0):
        x = [i for i in ins if i[3]]
        put("V", [call], regs_of(*ins), out[1], 50.0 + (0.0 if x or out[3] else max(64.0, n * wide) * CY),
            gathered=x[0][2] if x else 0, scattered=out[2] if out[3] else 0)

    def ts(out, in0, s1, op0, s2=None, op1=None):
        if op1 is None:
            f = lambda: g.vector.tensor_scalar(out[0], in0[0], val(s1), None, op0)
        else:
            f = lambda: g.vector.tensor_scalar(out[0], in0[0], val(s1), val(s2), op0, op1)
        vop(f, out, [in0] + [x for x in (s1, s2) if isinstance(x, tuple)], in0[2], 0.5 if narrow(out) and narrow(in0) else 1.0)

    def tt(out, in0, in1, op):
        ps = any(x[1][0][0] in BANKS for x in (in0, in1))
        vop(lambda: g.vector.tensor_tensor(out[0], in0[0], in1[0], op), out, [in0, in1], in1[2], 1.0 if ps else 2.0)

    def cp(out, in_):
        vop(lambda: g.vector.tensor_copy(out[0], in_[0]), out, [in_], in_[2], 0.5 if narrow(out) and narrow(in_) else 1.0)

    def scatter(win, off, in_):
        vop(lambda: g.vector.tensor_copy(win[0].indirect(off[0]), in_[0]), (None, win[1], in_[2], 1), [in_, off], in_[2])

    def fill(out, c):
        vop(lambda: g.vector.memset(out[0], c), out, [], out[2], 0.5)

    def scan(out, d0, d1, init, op0=OP.mult, op1=OP.add):
        vop(lambda: g.vector.tensor_tensor_scan(out[0], d0[0], d1[0], val(init), op0, op1), out,
            [d0, d1] + [x for x in (init,) if isinstance(x, tuple)], d1[2], 0.5 if narrow(out) and narrow(d1) else 1.0)

    def act(out, in_, func=None, bias=0.0, scale=1.0):
        if func is None:
            f = lambda: g.scalar.activation(out[0], in_[0], ACT.Copy, scale=scale)
        else:
            f = lambda: g.scalar.activation(out[0], in_[0], func, bias=bias, scale=scale)
        put("S", [f], regs_of(in_), out[1], 65.0 if in_[3] else SFIX + in_[2] * CY, gathered=in_[2] * in_[3])

    def mm(*terms, start=True, stop=True, free=False):
        for k0 in range(0, len(terms), MG):
            part = list(enumerate(terms))[k0:k0 + MG]
            calls = [lambda k=k, x=x: g.tensor.matmul(x[0][0], x[1][0], x[2][0], start and k == 0, stop and k == len(terms) - 1) for k, x in part]
            turn = [("turn" + terms[0][0][1][0][0], 0, 1)]
            put("P", calls, [r for k, x in part for r in regs_of(x[1], x[2])] + turn * free,
                [r for k, x in part for r in x[0][1]] + turn * (not free),
                sum(PFIX + max(64, x[2][2]) * PCY * (1 if narrow(x[2]) else 4) for k, x in part))

    def iota(out, pattern, base, ch):
        put("G", [lambda: g.iota(out[0], pattern, base, ch, allow_small_or_imprecise_dtypes=SCRATCH[out[1][0][0]][2] != I)], [], out[1], 130.0 + 2 * out[2] * CY)

    def zeros(out):
        iota(out, [[0, out[2]]], 0, 0)

    def sel(out, in_, pattern, base, ch, op=OP.is_equal, other=0.0):
        put("G", [lambda: g.affine_select(out[0], in_[0], pattern, op, other, base, ch)], regs_of(in_), out[1], 170.0 + 2 * out[2] * CY)

    def load(k, eng, out, src):
        put(eng, [lambda: queue[eng].dma_start(out[0], src).then_inc(T.sem["ld%d" % k], 16)], [], out[1] + [("turn" + eng, 0, 1)], 100.0, ("ld%d" % k, 16),
            LAND[k] if k < 7 else LAND[6] + 1800.0 * (k - 6))

    def send(to, sem, lsem, also=()):
        trs = []
        for k, (r, src, dst) in enumerate(to):
            rid, pid, _ = topo.addr(T.cores[r])
            eng = topo.engines(core, T.cores[r])[:8]
            n = len(eng) // len(to)
            trs.append(RemoteDMATransfer(dst_ids=[DstId(rid=rid, pnc=pid)], dma_engine_mask=sum(1 << x for x in eng[n * k:n * k + n]),
                                         remote_sem=T.sem[sem], src=src[0], dst=dst))
        return put("G", [lambda: g.remote_dma_fused(trs, local_sem=T.sem[lsem])], regs_of(*[x[1] for x in to]) + list(also), [],
                   500.0 + FIRST * (lsem == "la0_1"), (lsem, 8), LATE + ROW * len(to) * to[0][1][2])

    def arrives(kind, t, p, region, like):
        put("R", [], [], region[1], 0.0, ("%s%d_%d" % (kind, t, place[p]), engines(p)), 0.0, {like: WAKE})

    def places(q):
        def key(r):
            c1, c2 = topo.chip(T.cores[q]), topo.chip(T.cores[r])
            return r != max(x for x in range(N) if x != q), 0 if topo.mates(c1, c2) else 1 if topo.same_plane(c1, c2) else 2
        return [q] + sorted([r for r in range(N) if r != q], key=key)
    place = places(me)
    CALLS = ((1,), (2, 3))

    def there(p):
        return places(place[p]).index(me)

    def engines(p):
        return 8 // len([ps for ps in CALLS if there(p) in ps][0])

    load(0, "Y", a("n0_i"), T.n0[:])
    load(1, "S", a("rch_s"), T.rch[:])
    load(2, "S", a("dr_i", rows=96), T.dr[:, :])
    load(3, "Y", a("acts_i", 0, 2048), T.acts[:])
    parts = ((0, 2048), (2048, 3584), (3584, 4096))
    for k, (lo, hi) in enumerate(parts):
        load(4 + k, "Y", a("regs_s", lo, hi), T.regs[:, lo:hi])
        ts(a("P", lo, hi), a("regs_s", lo, hi), 0.0, OP.max)

    kf = a("kf")
    def col(j):
        return a("cols", j, j + 1)
    home_te = [4 * t + e for t in range(RO) for e in (0, 1)]
    far_te = [4 * t + e for t in range(RO) for e in (2, 3)]

    iota(a("li"), [[1, 64]], 0, 0)
    iota(a("pi"), [[0, 2]], 0, 1)
    iota(a("Bm"), [[1, 8], [0, 16]], 0, 0)
    iota(a("rp", 0, 128), [[0, 8], [1, 16]], 0, 0)
    iota(a("lid"), [[1, 256]], 1, 0)
    fill(a("ONE"), 1.0)
    fill(a("SIX"), 0.0625)
    fill(a("C16", 0, 256, rows=1), 0.0)
    fill(a("C16", 256, 512, rows=1), 16.0)
    cp(a("crep"), a("li"))
    ts(a("crep16"), a("li", 0, 32), 16.0, OP.mult)
    ts(a("pk", 0, 1), a("pi", 0, 1), 15, OP.bitwise_and)
    ts(a("pk", 1, 2), a("pi", 1, 2), 4, OP.arith_shift_right)
    cp(a("kf"), a("pk", 0, 1))
    cp(a("pg"), a("pk", 1, 2))
    ts(a("BO"), a("Bm"), a("pg"), OP.is_equal)
    fill(a("Z"), 0.0)
    cp(a("Z", 15, 143, 16), a("BO", 0, 128, 16))
    fill(a("nil"), 0.0)
    ts(a("TRI"), a("Bm"), a("pg"), OP.is_equal, 64.0, OP.mult)
    sel(a("TRI"), a("TRI"), [[1, 128]], 0, -1, OP.is_ge)
    zeros(a("TRI", 15, 128, 16))
    ts(col(0), kf, 8.0, OP.is_lt)
    ts(a("BO8"), a("BO"), col(0), OP.mult)
    for n, k in (("TRa", 0), ("TRb", 8)):
        ts(a(n), a("BO8"), 64.0, OP.mult)
        sel(a(n), a(n), [[1, 128]], -k, -1, OP.is_ge)
        zeros(a(n, 15, 128, 16))
    for j in range(6):
        sel(a("SEL", 128 * j, 128 * j + 128, rows=96), a("ONE", 0, 128, rows=96), [[-12, 8], [0, 16]], -home_te[j], 1)
    sel(a("ID"), a("ONE", 0, 128), [[-1, 128]], 0, 1)

    def entry(n, c, row, value, src=None):
        sel(a(n, c, c + 113, 16), src or a("nil", 0, 8), [[-16, 8]], -row, 1, OP.not_equal, value)
    for n, side in (("OHM", -1), ("DIF", 1)):
        sel(a(n), a("nil", 0, 128), [[1, 128]], side, -1, OP.not_equal, 1.0)
        sel(a(n), a(n), [[1, 128]], 0, -1, OP.not_equal, -1.0)
    entry("OHM", 0, 0, -1.0)
    entry("OHM", 0, 15, 1.0, a("OHM", 0, 113, 16))
    entry("OHM", 15, 14, 1.0)
    entry("DIF", 15, 0, 1.0)
    for out, src, c in (("I5", "ID", 5.0), ("IDn", "ID", -1.0), ("In", "ID", -2048.0), ("Zm", "Z", -1.0), ("Z2", "Z", 2.0)):
        ts(a(out), a(src), c, OP.mult)
    fill(a("T13", rows=1), 13.0)
    iota(a("NR", rows=1), [[1, 512]], 0, 0)
    for lo, hi, c in ((0, 8, 1.0), (16, 40, 0.0), (24, 32, -2048.0), (40, 48, 3.0)):
        fill(a("LC", lo, hi), c)
    ts(col(1), kf, 16.0, OP.mult, -1.0, OP.add)
    for c in (8, 48):
        ts(a("LC", c, c + 8), a("li", 0, 8), 256.0, OP.mult, col(1), OP.add)
    ts(a("CW", rows=1), a("rp", 0, 128, rows=1), 0.5, OP.add, -EPS, OP.mult)
    fill(a("CW", 15, 128, 16, rows=1), EPS)
    cp(a("n0u"), a("n0_i"))
    l = 0
    for n, way in WAYS[1][0] + WAYS[1][1]:
        if way == "V":
            for j in range(l, l + n, 48):
                m = min(48, l + n - j)
                act(a("xr1", 16 * j, 16 * (j + m)), via(a("rch_s", j, j + m), a("crep", 0, m)))
        else:
            mm((a("b%d" % (l // 128), 0, 128, rows=n), a("rch_s", l, l + n), a("ID")))
            cp(a("xT%d" % (l // 32), rows=n), a("b%d" % (l // 128), 0, 128, rows=n))
        l += n
    cp(a("drb", rows=96), a("dr_i", rows=96))
    ts(a("w_i", rows=96), a("dr_i", rows=96), 15, OP.bitwise_and)
    ts(a("wb", rows=96), a("w_i", rows=96), EPS, OP.mult)
    ts(a("y1"), a("rch_s"), -1.0, OP.add)
    zeros(a("DST", 112, 128))
    tt(a("E1", 0, 124), a("OHM", 0, 124), a("OHM", 4, 128), OP.add)
    tt(a("DST", 0, 116), a("E1", 0, 116), a("E1", 8, 124), OP.add)
    sel(a("DST"), a("DST"), [[0, 8], [-1, 16]], 3, 0, OP.is_ge)
    ts(col(4), kf, float(REG), OP.mult, -1.0, OP.add)
    fill(a("ZT"), 0.0)
    for j in range(6):
        sel(a("ZT", 144 * j + 15, 144 * j + 143, 16, rows=96), a("ONE", 0, 8, rows=96), [[-12, 8]], -far_te[j], 1)
    sel(a("M23"), a("ONE", 0, 128), [[-1, 128]], 0, 1)
    entry("M23", 3, 2, -1.0, a("ID", 3, 116, 16))
    zeros(a("ZN"))
    entry("ZN", 15, 2, 1.0)
    entry("ZN", 15, 3, 1.0, a("ZN", 15, 128, 16))
    for j, (row, w) in enumerate(((0, 1.0), (1, 1.0), (5, 1.0), (6, 1.0), (4, -8192.0))):
        sel(a("SR", 128 * j, 128 * j + 128), a("nil", 0, 128), [[-16, 8], [0, 16]], -row, 1, OP.not_equal, w)
    sel(a("ZM"), a("BO"), [[-1, 128]], 0, 1, OP.not_equal, -15.0)
    for n in "hf":
        zeros(a("D" + n))
        for c in (0, 16):
            iota(a("D" + n, c, 384, 48), [[0, 8]], -4, 0)
    iota(a("K0"), [[0, 64], [16, 16]], 1, 0)
    for j in range(4):
        sel(a("EX", 256 * j, 256 * j + 256, rows=64), a("ONE", rows=64), [[-1, 16], [0, 16]], -16 * j, 1)

    def later(after):
        first = len(ops)
        ts(col(5), kf, float(REG), OP.mult, 64.0, OP.add)
        ts(col(2), kf, 4096.0, OP.add)
        ts(col(3), kf, 4112.0, OP.add)
        ts(a("rd", 0, 16), a("rp", 0, 16), kf, OP.subtract)
        ts(a("ta"), a("rd", 0, 16), 0.0, OP.is_gt, 16384.0, OP.mult)
        ts(a("tb"), a("rd", 0, 16), 0.0, OP.is_equal, -8192.0, OP.mult)
        tt(a("ta"), a("ta"), a("tb"), OP.add)
        for n, c in (("h", 2048.0), ("f", 10240.0)):
            fill(a("CM" + n, 16, 32), c)
            ts(a("CM" + n, 0, 16), a("ta"), c, OP.add)
            ts(a("CM" + n, 32, 48), a("ta"), c, OP.add)
            for c in (48, 96, 192):
                cp(a("CM" + n, c, 2 * c), a("CM" + n, 0, c))
        for j, c in enumerate((15.0, 47.0, 47.0)):
            ts(a("crep48", j, 24, 3), a("li", 0, 8), 48.0, OP.mult, c, OP.add)
        ts(a("ownl"), a("li", 0, 16), 16.0, OP.mult, kf, OP.add)
        ts(a("own"), a("ownl"), 4128.0, OP.add, 2.0 ** -21, OP.mult)
        ts(a("ownl"), a("ownl"), 1.0, OP.add, 2.0 ** -8, OP.mult)
        ts(a("ID32"), a("ID"), 1.0, OP.mult)
        ts(a("BO2"), a("BO"), 2.0, OP.mult)
        ts(a("crep2"), a("li", 0, 32), 2.0, OP.mult, 1.0, OP.add)
        ts(a("Zs"), a("Z"), -2.0 ** -12, OP.mult)
        cp(a("paym", 2048, 2056), a("paym", 0, 8))
        for o in ops[first:]:
            o["after"][after] = 0.0
    for c in (0, 2048):
        act(a("xz", c, c + 1024), a("nil", 0, 1024))
    hop = [[a("send%d" % t, 0, 1024), a("send%d" % t, 1024, 2048), a("zr%d" % t)] for t in range(RO)]
    blank = [a("xz", 3072, 4096)] + hop[0] + [a("who", 1032 * j, 1032 * j + 1032) for j in range(4)] + [a("pay_s")] + hop[1] + hop[2]
    for k, x in enumerate(blank):
        if k == 8:
            load(7 + k, "Y", x, T.pay[:])
        else:
            load(7 + k, "Y", x, a("nil", 0, x[2])[0])
            ops[-1]["r"] = [("nil", 0, 1040)]
    for j in range(4):
        act(a("paym", 512 * j, 512 * j + 512), a("pay_s", 512 * j, 512 * j + 512), ACT.Identity, bias=-1.0)


    def draws(t):
        for j in (0, 1):
            s = 128 * (2 * t + j)
            mm((a("b6", 256 * j, 256 * j + 256), a("SEL", s, s + 128, rows=96), a("drb", rows=96)))
        act(a("vb%d" % t), a("b6"), ACT.Identity, bias=BETA)
        grp = []
        for src, j, row in (("drb", 0, 0), ("drb", 1, 1), ("wb", 0, 5), ("wb", 1, 6)):
            s = 144 * (2 * t + j) + 15 - row
            grp.append((a("b7", 256, 512), a("ZT", s, s + 128, rows=96), a(src, 0, 256, rows=96)))
        mm(*(grp + [(a("b7", 256, 512), a("Z", 11, 139), a("SIX"))]))
        act(a("auxS%d" % t), a("b7", 256, 512))

    def lists(out, src, n, first=(), z="Z", step=1):
        name, lo = src
        mm(*(list(first) + [(out, a(z, 15 - r, 143 - r), a(name, lo + step * r, lo + n, 16 * step)) for r in range(16)]))

    def acts_at(e, lo, hi, nodes):
        cp(a("A%d" % e, lo, hi), via(a("acts_i"), nodes))

    def node_table():
        for j in range(4):
            lo, hi, b = 512 * j, 512 * j + 512, a("b%d" % (4, 5, 2, 3)[j])
            ts(a("AH", lo, hi), a("acts_i", lo, hi), -2048.0, OP.add)
            u = [(b, a("I5"), a("AH", lo, hi)), (b, a("T13", rows=1), a("NR", rows=1))]
            mm(*u)
            act(a("fl", lo, hi), b, ACT.Identity, bias=129.0 + (10240.0 + 6656 * j - 1023.5) / 2048.0, scale=2.0 ** -11)
            mm(*(u + [(b, a("In"), a("fl", lo, hi))]))
            if j > 1:
                ts(a("NN", lo, hi), b, 274432.0 + 6656 * j, OP.add)
            else:
                act(a("NN", lo, hi), b, ACT.Identity, bias=274432.0 + 6656 * j)
        for n in ("NN", "acts_i"):
            cp(a(n, 2048, 2056), a(n, 0, 8))

    def next_nodes(e, u, nodes):
        ta, c = "TA%d" % u, 128 * ((e, u) == (2, 0))
        if e % 2:
            act(a(ta, 0, 128), via(a("NN"), nodes))
            mm((a("b%d" % (2 + u), 128, 256), a("DIF"), a(ta, 0, 128)))
        else:
            act(a(ta, c, c + 128), via(a("NN"), nodes), ACT.Identity, bias=e - 2048.0)
            half = e / 4.0
            act(a(ta, 128 - c, 256 - c), via(a("acts_i"), nodes), ACT.Identity, bias=-2048.0 * half, scale=half)

    def yz(lo, hi):
        return a("xz", 16 * lo, 16 * hi - 15, 16)

    def weights(e, u, l0, n, way, y, last, lead):
        c, x, yT = l0 - 128 * u, "b%d" % u, "%sT%d" % ("xy"[e > 1], l0 // 32)
        y = y or yz(l0, l0 + n)
        out = a(x, c, c + n)
        if e > 1 and way == "V":
            scan(a("xr", 16 * l0, 16 * (l0 + n)), a("K0", 0, 16 * n), a("xz", 16 * l0, 16 * (l0 + n)), 1.0, OP.min, OP.add)
        elif e > 1 and way == "G":
            name, w0, w1 = y[1][0]
            st, w0 = (16, w0) if name == "xz" else (2, w0 - 1)
            for l, m in [x for l in range(0, n, 32) for x in (((l, 16), (l + 16, 16)) if (l0 + l) % 128 == 0 else ((l, 32),))]:
                act(a("xr", 16 * (l0 + l), 16 * (l0 + l + m)), via(a(name, w0 + st * l, w0 + st * (l + m)), a("crep%d" % st, 0, m)), ACT.Identity, bias=1.0)
        elif e > 1:
            z = a("b%d" % (4 + u), 128, 256, rows=n)
            mm((z, y, a("ID")))
            act(a(yT, rows=n), z, ACT.Identity, bias=1.0)
        for j, m in [x for l in range(l0, l0 + n, 32) for x in (((l, 16), (l + 16, 16)) if l % 128 == 0 and way == "G" else ((l, 32),))]:
            w, xr = a("W", 16 * j, 16 * (j + m)), a("xr1" if e == 1 else "xr", 16 * j, 16 * (j + m))
            p = via(a("P", 0, 4096), a("A%d" % e, j, j + m))
            if way in "VG":
                tt(w, p, xr, OP.min)
                ops[-1]["w"] = ops[-1]["w"] + [("turnV", 0, 1)]
            else:
                b = a("b%d" % (6 + (j // 32 + (e > 1 or u)) % 2), 0, 16 * m)
                if e == 1 and now[0] == 0:
                    act(w, via(a("regs_s", 0, 4096), a("A1", j, j + m)), ACT.Relu)
                else:
                    act(w, p)
                ops[-1]["w"] = ops[-1]["w"] + [("turnS", 0, 1)]
                mm((b, a(yT, rows=n), a("EX", 16 * (j - l0), 16 * (j - l0 + m), rows=n)), stop=False)
                mm((b, a("IDn"), w), start=False)
                act(a("xr", 16 * j, 16 * (j + m)), b, ACT.Relu)
        two = c >= TWO[e][u]
        if way == "S":
            for o in (a(x, wide(e, u, c), wide(e, u, c + n), 2), a(x, wide(e, u, c) + 1, wide(e, u, c + n), 2)) if two else (out,):
                mm((o, a("BO"), a("rch_s", l0, l0 + n) if e == 1 else y), start=False, stop=False, free=True)
        z, src = ("Zm", "xr") if way == "S" else ("Z", "W")
        if lead < 0:
            return
        l0, n, c = l0 - lead, n + lead, c - lead
        first = len(ops)
        if two:
            groups = [[(a(x, wide(e, u, c + j), wide(e, u, c + j + 32)), a(z, 15 - k, 143 - k), a(src, 16 * (l0 + j) + k, 16 * (l0 + j + 32), 8)) for k in range(8)]
                      for j in range(0, n, 32)]
        else:
            groups = [[(a(x, c, c + n), a(z, 15 - k, 143 - k), a(src, 16 * l0 + k, 16 * (l0 + n), 16)) for k in range(16)]]
        end = groups[-1].pop() if last else None
        for terms in groups:
            mm(*terms, start=False, stop=False, free=True)
        for o in ops[first:]:
            o["r"] = o["r"] + [("turnP", 0, 1)]
        if last:
            mm(end, start=False)
            ops[-1]["w"] = ops[-1]["w"] + [("turnP", 0, 1)]

    def wide(e, u, c):
        return c + max(0, c - TWO[e][u])

    def unit(e, u, l0=None, ways=None, y=None):
        l0, ways = (128 * u, WAYS[e][u]) if ways is None else (l0, ways)
        c, n, x = l0 - 128 * u, sum(w[0] for w in ways), "b%d" % u
        lo, hi = wide(e, u, c), wide(e, u, c + n)
        v = wide(e, u, c + sum(w[0] for w in ways if w[1] != "S")) - lo if e > 1 else 256
        mm((a(x, lo, hi), a("ONE", 0, 128, rows=1), a("C16", 256 - v, 256 - v + hi - lo, rows=1)), stop=False)
        l, lead = l0, 0
        for m, way in ways:
            weights(e, u, l, m, way[0], y and y(l - l0, m), l + m == l0 + n, -1 if way[1:] else lead)
            l, lead = l + m, lead + m if way[1:] else 0

    def choose(e, t, u, aux=None):
        lo, hi = 128 * u, 128 * u + 128
        x, y, z, q, L = "b%d" % u, "b%d" % (2 + u), "b%d" % (4 + u), "q%d_%d" % (e, u), "L%d_%d" % (e, u)
        if e < 3:
            vb = a("vb%d" % t, 256 * (e - 1) + lo, 256 * (e - 1) + hi)
            mod16 = [(a(y, 384, 512), a("SEL", 256 * t + 128 * e - 128, 256 * t + 128 * e, rows=96), a("wb", lo, hi, rows=96))]
        else:
            vb = a("vbF%d" % u, 128 * (e - 3), 128 * (e - 2))
            mod16 = [(a(y, 384 + l - lo, 384 + l - lo + n), a("SR", 128 * e - 128, 128 * e), aux(l, n)) for l, n in FAR[u]]
        odd = e % 2
        ind = a(q, 128, 256) if odd else a("ind", lo, hi)
        c, m = TWO[e][u], 192 * u
        act(a("ms", m, m + 256 - c), a(x, 0, 256 - c))
        mm((a(y, 384, 512), a("CW", rows=1), a("ONE", 0, 128, rows=1)), *mod16, stop=False)
        halves = [a("ms", m + c + h, m + 256 - c, 2) for h in (0, 1)] * (c < 128)
        mm((a(y, 384, 384 + c), a("BO"), a("ms", m, m + c)), *[(a(y, 384 + c, 512), a("BO8"), h) for h in halves], start=False)
        mm((a(x, 256, 256 + c), a("TRI"), a("ms", m, m + c)))
        if halves:
            mm((a(x, 256 + c, 384), a("TRa"), halves[0]), (a(x, 256 + c, 384), a("TRb"), halves[1]))
        tt(a("t1", lo, hi), a(y, 384, 512), vb, OP.mult)
        tt(ind, a(x, 256, 384), a("t1", lo, hi), OP.is_lt)
        yin = a("y1", lo, hi) if e == 1 else yz(lo, hi)
        yout = yz(lo, hi) if odd else a("y%d" % (e + 1), lo, hi)
        if odd:
            tt(a(q, 0, 128), a(y, 128, 256), ind, OP.mult)
            lists(a(z, 0, 16), (q, 0), 256, [(a(z, 0, 16), a("ID"), a("LC", 20 * e - 20, 20 * e - 4))])
            cp(a(L), a(z, 0, 16))
            acts_at(e + 1, lo, hi, a(L, 0, 8))
            tt(yout, via(a("W", 16 * lo, 16 * hi), a(L, 8, 16)), yin, OP.min)
            next_nodes(e + 1, u, a(L, 0, 8))
            return
        if e == 2:
            mm((a(z, 128, 256), a("DST"), ind))
        mm((a(x, 128, 256), a("OHM"), ind))
        mm((a(x, 256, 384), a("OHM"), ind))
        if e == 4:
            tt(a(q), a(x, 128, 384), a("TA%d" % u), OP.mult)
            lists(a(z, 0, 16), (q, 0), 256)
            ts(a(L), a(z, 0, 16), 2048.0, OP.add)
            c, rec = 8, a(L, 8, 16)
        else:
            nodes = a("q2", 256 + lo, 256 + hi)
            scan(a("cum", lo, hi), a("ONE", lo, hi), a(z, 128, 256), col(4) if u == 0 else a("cum", lo - 1, lo))
            tt(a("q2", 640 * u, 640 * u + 128), a(z, 128, 256), a("cum", lo, hi), OP.mult)
            tt(a("q2", 128 + 256 * u, 384 + 256 * u), a(x, 128, 384), a("TA%d" % u), OP.mult)
            mm((a(y, 0, 128), a("ID"), a("auxS%d" % t, lo, hi)), (a(y, 0, 128), a("Z", 13, 141), nodes))
            act(a("aux1", lo, hi), a(y, 0, 128))
            lists(a(z, 0, 16), ("q2", 512 * u), 256, [(a(z, 0, 16), a("ID"), a("LC", 24 - 8 * u, 40 - 8 * u))], z="Z2")
            ts(a("L2", 16 * u, 16 * u + 16), a(z, 0, 16), 2048.0, OP.add)
            ts(a("Ly", 8 * u, 8 * u + 8), a(z, 8 * u, 8 * u + 8), 2049.0, OP.add)
            c, rec = 8 - 8 * u, a("L2", 8 + 8 * u, 16 + 8 * u)
        for j in (0, 1):
            act(a("D" + "hf"[e // 4], 192 * u + 15 + 32 * j, 192 * u + 192, 48), a(z, c + j, c + 8, 2), ACT.Identity, bias=2.0 ** -10, scale=2.0 ** -21)
        tt(yout, via(a("P", 0, 4096), rec), yin, OP.min)
        if e == 2:
            mm((a(y, 128, 256), a("M23"), a("aux1", lo, hi)), (a(y, 128, 256), a("Z", 12, 140), nodes))
            act(a("auxB", lo, hi), a(y, 128, 256))

    def first_of(n, b, j0, j1, dead, alive, rec):
        lo, hi = 48 * j0, 48 * j1
        at = a(b, 128, 128 + hi - lo)
        terms = [(at, a("ID"), a("CM" + n, lo, hi))]
        for m, x in ((dead, alive), (a("BO2" if n == "h" else "BO"), rec)):
            for j in range(j0, j1):
                c = 128 + 48 * (j - j0)
                terms += [(a(b, c, c + 16), m, x(32 * j, 16)), (a(b, c + 16, c + 48), m, x(32 * j, 32))]
        mm(*terms[:1], stop=False)
        mm(*terms[1:], start=False)
        off = "offf" if n == "f" else "offw"
        act(a("Y" + n, lo, hi), via(a("D" + n, lo, hi), a("crep48", 0, (hi - lo) // 16)), scale=2.0 ** 21)
        tt(a("eq" + n, lo, hi), at, a("Y" + n, lo, hi), OP.is_equal)
        scan(a("lc" + n, lo, hi), a("D" + n, lo, hi), a("eq" + n, lo, hi), 0.0, OP.add, OP.max)
        ts(a(off, 2 * j0, 2 * j1, 2), a("lc" + n, lo + 15, hi, 48), 2.0 ** 21, OP.mult, col(2), OP.min)
        ts(a(off, 2 * j0 + 1, 2 * j1, 2), a("lc" + n, lo + 47, hi, 48), 2.0 ** 21, OP.mult, col(3), OP.min)

    def change(off, blocks, values, table):
        for c in blocks:
            scatter(a(table), a(off, 2 * c, 2 * c + 2), a(values, 32 * c, 32 * c + 32))

    def first_of_all():
        change("offw", range(7, -1, -1), "lid", "who")
        act(a("found"), via(a("who"), a("offw")))
        lists(a("b7", 32, 48), ("found", 0), 256, [(a("b7", 32, 48), a("ID32"), a("ownl")), (a("b7", 32, 48, 2), a("ID32"), a("lch", 15, 384, 48)),
                                                   (a("b7", 33, 48, 2), a("ID32"), a("lch", 47, 384, 48))], z="Zs")
        tt(a("o32"), a("b7", 32, 48), a("own"), OP.min)
        ts(a("offh"), a("o32"), 2.0 ** 21, OP.mult)

    draws(0)
    node_table()
    cp(a("A1"), via(a("acts_i", 0, 2048), a("n0u")))
    act(a("TD1"), via(a("NN", 0, 2048), a("n0u")))
    for t in range(RO):
        more = t + 1 < RO
        land, zr, out = "land%d" % t, "zr%d" % t, "send%d" % t
        for e in (1, 2):
            for u in (0, 1):
                if e == 1:
                    mm((a("b%d" % (2 + u), 128, 256), a("DIF"), a("TD1", 128 * u, 128 * u + 128)))
                unit(e, u)
                choose(e, t, u)
        for u in (0, 1):
            scatter(a(out), a("L2", 24 * u, 24 * u + 8), a("auxB", 128 * u, 128 * u + 128))
            scatter(a(out), a("Ly", 8 * u, 8 * u + 8), a("y3", 128 * u, 128 * u + 128))
        if t == 0:
            later(len(ops) - 1)
        for ps in CALLS:
            o = send([(place[p], a(out, 2 * REG * place[p], 2 * REG * place[p] + 128), T[land][:, 128 * there(p):128 * there(p) + 128]) for p in ps],
                     "a%d_%d" % (t, me), "la%d_%d" % (t, ps[0]), [(zr, 0, 1040)])
            for p in ps:
                arrives("a", t, p, a(land, 128 * p, 128 * p + 128), o)
        ts(a("Lz"), a("Ly"), -1.0, OP.add, 0.5, OP.mult)
        ops[-1]["after"][o] = -ops[o]["late"]
        for u in (0, 1):
            ts(a("ng", 128 * u, 128 * u + 128), a("q2", 640 * u, 640 * u + 128), col(5), OP.is_ge, 8192.0, OP.mult)
        for u in (0, 1):
            first_of("h", "b%d" % u, 4 * u, 4 * u + 4, a("BO"), lambda l, n: a("ng", l, l + n), lambda l, n: a("q2", 128 + l + 256 * (l // 128), 128 + l + 256 * (l // 128) + n))

        def aux(l, n, odd=0):
            name, s = (out, 2 * REG * me + 2 * l + odd) if l < 64 else (land, 2 * l + odd)
            return a(name, s, s + 2 * n - 1, 2)
        for u in (0, 1):
            z, m, nF = "b%d" % (4 + u), "b%d" % (2 + u), "nF%d" % u
            for k, (l, n) in enumerate(FAR[u]):
                c = l % 128 // 16
                lists(a(z, c, c + n // 16), aux(l, n)[1][0][:2], 2 * n, z="ZN", step=2)
                ts(a(nF, c, c + n // 16), a(z, c, c + n // 16), 2048.0, OP.add)
                acts_at(3, l, l + n, a(nF, c, c + n // 16))
                sel(yz(l, l + n), aux(l, n, 1), [[0, n]], 0, 0)
                ops[-1]["after"][o] = -ops[o]["late"]
                unit(3, u, l, WAYS[3][2 * u + k], lambda j, n: aux(l + j, n, 1))
            for l, n in FAR[u]:
                for j in (0, 1):
                    mm((a(m, 128 * j + l % 128, 128 * j + l % 128 + n), a("SR", 128 * j, 128 * j + 128), aux(l, n)))
            act(a("vbF%d" % u), a(m, 0, 256), ACT.Identity, bias=BETA)
            next_nodes(3, u, a(nF, 0, 8))
            choose(3, t, u, aux)
        for u in (0, 1):
            lo, hi, x, y, L = 128 * u, 128 * u + 128, "b%d" % u, "b%d" % (2 + u), "L4_%d" % u
            unit(4, u)
            choose(4, t, u, aux)
            tt(a("lv", lo, hi), via(a("paym"), a(L, 0, 8)), a("y5", lo, hi), OP.min)
            mm((a(x, 0, 128), a("ZM"), a("lv", lo, hi)))
            act(a("zN", lo, hi), a(x, 0, 128), ACT.Sign)
            ps = CALLS[u]
            o = send([(place[p], a("zN", 64 * p, 64 * p + 64), T[zr][:, REG * me:REG * me + 64]) for p in ps], "z%d_%d" % (t, me), "lz%d_%d" % (t, ps[0]))
            for p in ps:
                arrives("z", t, p, a(zr, REG * place[p], REG * place[p] + 64), o)
            if u == 0:
                act(a(zr, REG * me, REG * me + 64), a("zN", 0, 64))
            act(a("NV", lo, hi), via(a("regs_s", 0, 4096), a(L, 8, 16)))
            mm((a(y, 384, 512), a("ID"), a("NV", lo, hi)), (a(y, 384, 512), a("IDn"), a("zN", lo, hi)))
            ts(a("NV", lo, hi), a(y, 384, 512), 15.0, OP.min, -15.0, OP.max)
            if more:
                act(a("NP", lo, hi), a(y, 384, 512), ACT.Relu)
            first_of("f", "b%d" % (4 + u), 4 * u, 4 * u + 4, a("SR", 512, 640), aux,
                     lambda l, n: a("q4_%d" % (l // 128), 128 + l % 128, 128 + l % 128 + n))
        first_of_all()
        if more:
            first = len(ops)
            draws(t + 1)
            for x in ops[first:]:
                x["after"][o] = -ops[o]["late"] - 500.0
        blocks = [2 * place.index(r) + c for r in (3, 2, 1, 0) for c in (1, 0)]
        change("offf", blocks, "NV", "regs_s")
        if more:
            change("offf", blocks, "NP", "P")
        act(a("HR"), via(a("regs_s", 0, 4096), a("L2", 8, 24)))
        tt(a("HV"), via(a(zr), a("Lz")), a("HR"), OP.add)
        if more:
            ts(a("HP"), a("HV"), 15.0, OP.min, 0.0, OP.max)
            scatter(a("P"), a("offh"), a("HP"))
            ends.append(len(ops) - 1)
            now[0] += 1
        ts(a("HV"), a("HV"), 15.0, OP.min, -15.0, OP.max)
        for lo, hi in ((0, 8), (8, 16)) if more else ((0, 16),):
            scatter(a("regs_s"), a("offh", lo, hi), a("HV", 16 * lo, 16 * hi))
    ends.append(put("Y", [lambda: g.sync.dma_start(T.yr[:], T.regs_s[:, 0:4096]).then_inc(T.sem.yo, 16)], [("regs_s", 0, 4384)], [], 100.0, ("yo", 16), 8000.0))

    seen = {}
    for i, o in enumerate(ops):
        pred = dict(o["after"])
        for regs, w in ((o["r"], False), (o["w"], True)):
            for name, lo, hi in regs:
                for j, l2, h2, w2 in seen.get(name, []):
                    if l2 < hi and lo < h2 and (w or w2) and j != i:
                        same = w and ops[j]["e"] == o["e"] == "P"
                        pred[j] = max(pred.get(j, -1e9), -ops[j]["late"] if name[:4] == "turn" else 0.0 if same else WAKE)
        for regs, w in ((o["r"], False), (o["w"], True)):
            for name, lo, hi in regs:
                seen[name] = [x for x in seen.get(name, []) if not (w and lo <= x[1] and x[2] <= hi)] + [(i, lo, hi, w)]
        o["in"], o["out"] = {j: ops[j]["d"] + ops[j]["late"] + w for j, w in pred.items()}, {}
        o["ins"] = [{j: ops[j]["ds"][c] + (ops[j]["late"] * SLOW[c][ops[j]["e"] == "G"] + x[3] if w == WAKE else ops[j]["late"] + w) for j, w in pred.items()}
                    for c, x in enumerate(CASES)]
        o["use"] = [] if o["e"] == "R" else [o["e"]] + sorted(set(r[0] for r in o["r"] + o["w"] if r[0] in BANKS))
        for j, w in pred.items():
            ops[j]["out"][i] = o["d"] + ops[j]["late"] + w
    for o in reversed(ops):
        o["way"] = o["d"] + max([o["late"]] + [ops[j]["way"] + w - ops[j]["d"] for j, w in o["out"].items()])

    def lay(order, at, busy, back=False):
        for i in order:
            o = ops[i]
            t, d, eng = (o["late"] if back else 0.0), o["d"], o["e"]
            for j, w in o["out" if back else "in"].items():
                if j in at and at[j] + w > t:
                    t = at[j] + w
            moved = True
            while moved:
                moved = False
                for r in o["use"]:
                    b = busy[r]
                    k = len(b)
                    while k and b[k - 1][1] + WAKE > t:
                        k -= 1
                    for t0, t1, e in b[k:]:
                        pad = WAKE if e != eng else 0.0
                        if t0 - pad >= t + d:
                            break
                        if t1 + pad > t:
                            t, moved = t1 + pad, True
            for r in o["use"]:
                b = busy[r]
                k = len(b)
                while k and b[k - 1][0] > t:
                    k -= 1
                b.insert(k, (t, t + d, eng))
            at[i] = t
        return at

    def in_order(part, key):
        k = {}
        for i in sorted(part):
            k[i] = max([key[i]] + [k[j] + 0.001 for j in ops[i]["in"] if j in k])
        return sorted(part, key=lambda i: (k[i], i))

    seed = [SEED]
    def chance(lo, hi):
        seed[0] = (seed[0] * 1103515245 + 12345) % 2147483648
        return lo + (hi - lo) * seed[0] / 2147483648.0

    def improve(part, end, tries, hot):
        n, idx, cases = len(part), {i: k for k, i in enumerate(part)}, range(len(CASES))
        base = [[max([0.0] + [past[c][j] + w for j, w in ops[i]["ins"][c].items() if j not in idx]) for i in part] for c in cases]
        pred = [[[(idx[j], w) for j, w in ops[i]["ins"][c].items() if j in idx] for i in part] for c in cases]
        before, after = [set(j for j, w in p) for p in pred[0]], [[idx[j] for j in ops[i]["out"] if j in idx] for i in part]
        use, eng = [[NAMES.index(r) for r in ops[i]["use"]] for i in part], [ops[i]["e"] for i in part]
        dur, end = [[ops[i]["ds"][c] for i in part] for c in cases], idx[end]

        def times(c, seq, old=None, lo=0):
            if old:
                at, why, marks = old[0][:], old[1][:], old[4][:lo // 32 + 1]
            else:
                at, why, marks = [0.0] * n, [-1] * n, [(ready[c], [-1] * len(NAMES))]
            free, last = marks[-1][0][:], marks[-1][1][:]
            b, p, d, wake = base[c], pred[c], dur[c], CASES[c][3]
            for lo in range(32 * len(marks) - 32, n, 32):
                for k in seq[lo:lo + 32]:
                    t, y, e, u = b[k], -1, eng[k], use[k]
                    for j, w in p[k]:
                        w += at[j]
                        if w > t:
                            t, y = w, j
                    for r in u:
                        j = last[r]
                        x = free[r] if j < 0 or eng[j] == e else free[r] + wake
                        if x > t:
                            t, y = x, j
                    at[k], why[k] = t, y
                    t += d[k]
                    for r in u:
                        free[r], last[r] = t, k
                marks.append((free[:], last[:]))
            return at, why, free, max((at[end], end), *[(free[r] + x, last[r]) for r, x in ((1, 600.0), (2, -d[end]), (3, -3000.0)) if last[r] >= 0]), marks

        def worth(x):
            return sum((y[3][0] + PULL * sum(y[0]) / n) / z for y, z in zip(x, scale))
        seq = best = list(range(n))
        cur = [times(c, seq) for c in cases]
        scale = [len(CASES) * (x[3][0] - ready[c][0]) / 45000.0 for c, x in enumerate(cur)]
        now = least = worth(cur)
        for m in range(tries):
            _, why, _, (_, k), _ = cur[m % len(CASES)]
            pairs = []
            while why[k] >= 0:
                if why[k] not in before[k]:
                    pairs.append((why[k], k))
                k = why[k]
            if not pairs:
                break
            x = y = int(chance(0, len(pairs)))
            if chance(0, 1) < RUN:
                while x and pairs[x - 1][0] == pairs[x][1] and chance(0, 1) < 0.8:
                    x -= 1
                while y + 1 < len(pairs) and pairs[y + 1][1] == pairs[y][0] and chance(0, 1) < 0.8:
                    y += 1
            j, i = pairs[y][0], pairs[x][1]
            lo, hi, far = seq.index(j), seq.index(i), int(chance(1, 30)) * (chance(0, 1) < 0.3)
            if chance(0, 1) < 0.5:
                lo, move = max(0, lo - far), {i}
                for k in reversed(seq[lo:hi + 1]):
                    if k in move:
                        move.update(before[k])
                if j in move:
                    continue
                new = [k for k in seq[lo:hi + 1] if k in move] + [k for k in seq[lo:hi + 1] if k not in move]
            else:
                hi, move = min(n - 1, hi + far), {j}
                for k in seq[lo:hi + 1]:
                    if k in move:
                        move.update(after[k])
                if i in move:
                    continue
                new = [k for k in seq[lo:hi + 1] if k not in move] + [k for k in seq[lo:hi + 1] if k in move]
            new = seq[:lo] + new + seq[hi + 1:]
            if m % PACK == 0:
                at = lay([part[k] for k in seq], dict(past[0]), {r: [(-1e7, ready[0][k], "")] for k, r in enumerate(NAMES)})
                new, lo = sorted(seq, key=lambda k: at[part[k]]), 0
            x = [times(c, new, cur[c], lo) for c in cases]
            w = worth(x)
            if w - now <= -hot * (COLD / hot) ** (m / tries) * math.log(chance(1e-9, 1)):
                cur, now, seq = x, w, new
                if m % 16 == 0:
                    seq = sorted(new, key=lambda k: x[0][0][k])
                    cur = [times(c, seq) for c in cases]
                if now < least:
                    least, best = now, seq
        return least, [part[k] for k in best], [times(c, best) for c in cases], part

    def idle():
        return {r: [] for r in list("VPSGY") + BANKS}

    def laid(part, end):
        order, best = sorted(part, key=lambda i: (-ops[i]["way"], i)), None
        for _ in range(PASSES):
            at = lay(order, {}, idle())
            if best is None or at[end] < best[end]:
                best = at
            ta = lay(sorted(part, key=lambda i: (-at[i] - ops[i]["d"], -i)), {}, idle(), True)
            order = sorted(part, key=lambda i: (-ta[i] - ops[i]["d"], i))
        return best

    seen = {}
    for o in ops:
        n, lo, _ = (o["w"] or o["r"])[0]
        for m in ("vb%d", "auxS%d"):
            for t in range(RO):
                if n == AT[m % t][0] and 0 <= lo - AT[m % t][1] < AT[m % t][2]:
                    n, lo = m, 0
        x = o["e"], n[:-1] if n[:-1] in ("send", "land", "zr") else n, lo
        seen[o["round"], x] = seen.get((o["round"], x), 0) + 1
        o["name"] = x, seen[o["round"], x]
    for o in ops:
        if o["round"] == 0:
            x, k = o["name"]
            o["name"] = x, k - seen[0, x] + seen.get((1, x), 0)
    rounds = [[i for i, o in enumerate(ops) if o["round"] == t] for t in range(RO)]
    NAMES = list("VPSGY") + BANKS
    past, ready, calls = [{} for c in CASES], [[0.0] * len(NAMES) for c in CASES], []
    if not PLAN:
        past = [{i: -1e6 for i in rounds[0]} for c in CASES]
        at = laid(rounds[1], ends[1])
        x = min(improve(sorted(rounds[1], key=lambda i: (at[i], i)), ends[1], TRIES[0], HOT) for _ in range(TRIES[1]))
        x = improve(x[1], ends[1], LONG, MILD)
        PLAN["model"] = {ops[i]["name"]: x[2][0][0][k] - x[2][0][3][0] for k, i in enumerate(x[3])}
        PLAN["worth"] = [y[3][0] for y in x[2]]
        past = [{} for c in CASES]
    for t, part in enumerate(rounds):
        if t in PLAN:
            at, tries = PLAN[t], AGAIN
        else:
            at, tries, like = laid(part, ends[t]), TRIES[2 + t], PLAN["model"]
            shift = min(at[i] - like[ops[i]["name"]] for i in part if ops[i]["name"] in like and ops[i]["w"][:1] == [("W", 0, 512)])
            at = {i: like[ops[i]["name"]] + shift if ops[i]["name"] in like else at[i] for i in part}
        x = improve(in_order(part, at), ends[t], tries, WARM)
        for c, y in enumerate(x[2]):
            past[c].update(zip(x[3], y[0]))
            ready[c] = y[2]
        if t == 1 and t not in PLAN:
            PLAN["model"] = {ops[i]["name"]: past[0][i] for i in part}
        PLAN.setdefault(t, {i: past[0][i] for i in part})
        calls += x[1]

    count = {"eV": 0, "eP": 0, "eS": 0, "eG": 0}
    known = {e: {} for e in "VPSGYR"}
    snap, acc = {}, {}

    def needs(eng, reads, writes):
        need = {}
        for regs, w in ((reads, False), (writes, True)):
            for name, lo, hi in regs:
                for (e2, tok, l2, h2, w2) in acc.get(name, []):
                    if name in BANKS and e2 != eng:
                        hit = True
                    elif l2 < hi and lo < h2:
                        hit = (w or w2) and not (w and eng == "P" and e2 == "P")
                    else:
                        hit = False
                    if hit and known[eng].get(tok[0], 0) < tok[1] and need.get(tok[0], 0) < tok[1]:
                        need[tok[0]] = tok[1]
        return need

    for i in calls:
        o = ops[i]
        eng, tok = o["e"], o["tok"]
        writes = [r for r in o["w"] if r[0] in SCRATCH]
        if eng != "R":
            need = needs(eng, o["r"], writes)
            for s in sorted(need):
                v = need[s]
                if not any(s2 != s and need[s2] and snap[(s2, need[s2])].get(s, 0) >= v for s2 in need):
                    queue[eng].wait_ge(T.sem[s], v)
                    for s3, v3 in snap[(s, v)].items():
                        known[eng][s3] = max(known[eng].get(s3, 0), v3)
                else:
                    need[s] = 0
        for call in o["calls"]:
            if tok:
                call()
            else:
                count["e" + eng] += 1
                call().then_inc(T.sem["e" + eng], 1)
        who = eng if not tok else "D" + tok[0]
        tok = tok or ("e" + eng, count["e" + eng])
        snap[tok] = dict(known[eng])
        snap[tok][tok[0]] = tok[1]
        for regs, w in ((o["r"], False), (writes, True)):
            for name, lo, hi in regs:
                keep = [x for x in acc.get(name, []) if not (lo <= x[2] and x[3] <= hi and (w or (x[0] == who and not x[4])))]
                acc[name] = keep + [(who, tok, lo, hi, w)]

    g.sync.wait_ge(T.sem.yo, 16)
    for s in ("eV", "eP", "eS", "eG"):
        g.sync.wait_ge(T.sem[s], count[s])
    for o in ops:
        if o["tok"] and o["tok"][0][:2] == "ld":
            g.sync.wait_ge(T.sem[o["tok"][0]], 16)
    for t in range(RO):
        for ps in CALLS:
            for k in "az":
                g.sync.wait_ge(T.sem["l%s%d_%d" % (k, t, ps[0])], 8)
                for p in ps:
                    g.sync.wait_ge(T.sem["%s%d_%d" % (k, t, place[p])], engines(p))
